import numpy as np
import ml_dtypes


def mxq(x, axis, fmt="e4m3"):
    dtype, down = {"e4m3": (ml_dtypes.float8_e4m3fn, 7), "e5m2": (ml_dtypes.float8_e5m2, 14)}[fmt]
    v = np.moveaxis(np.asarray(x, np.float32).astype(ml_dtypes.bfloat16).astype(np.float64), axis, -1)
    blocks = v.reshape(v.shape[:-1] + (-1, 32))
    amax = np.abs(blocks).max(-1, keepdims=True)
    byte = np.maximum(np.where(amax > 0, np.frexp(amax)[1] - 1 + 127, 0) - down, 1)
    scale = np.exp2(byte - 127.0)
    codes = (blocks / scale).astype(np.float32).astype(dtype).astype(np.float64)
    return np.moveaxis((codes * scale).reshape(v.shape), -1, axis)


WIDE = False


def mx_kscale(k):
    if not WIDE:
        return np.ones(k)
    levels = np.array([10, -10, 5, -5, 0])
    if k % 512:
        return np.exp2(np.random.permutation(np.resize(levels, k // 32))).repeat(32)
    a = np.empty((k // 512, 16))
    for p in range(k // 512):
        a[p, :8] = np.random.permutation(np.resize(levels, 8))
        for g in range(8):
            far = levels[np.abs(levels - a[p, g]) >= 10]
            a[p, g + 8] = far[np.random.randint(len(far))]
    return np.exp2(a.ravel()).repeat(32)


BF16 = ml_dtypes.bfloat16


def bf(x):
    return np.asarray(x, np.float32).astype(BF16)


def f64(x):
    return np.asarray(x).astype(np.float64)


N, L, F, H, P = 4096, 512, 512, 256, 4
PH = P * H


def draw0():
    s, t = mx_kscale(L), mx_kscale(F)
    return {
        "x": bf(np.random.standard_normal((N, L)) * s),
        "fut": bf(np.random.standard_normal((N, P, H))),
        "w1": bf(np.random.standard_normal((L, F)) / np.sqrt(L) / s[:, None] * t),
        "w2": bf(np.random.standard_normal((F, PH)) * 1.4 / np.sqrt(F) / t[:, None]),
        "wsk": bf(np.random.standard_normal((L, PH)) / np.sqrt(L) / s[:, None]),
        "vp": bf(np.random.uniform(0.4, 0.8, P)),
        "wres": bf(np.random.standard_normal((L, H)) / np.sqrt(L) / s[:, None]),
    }


def residual_block(xq, w1, w2, wsk):
    h = np.maximum(xq @ mxq(f64(w1), 0, "e4m3"), 0.0)
    return (mxq(h, 1, "e4m3") @ mxq(f64(w2), 0, "e4m3")) + (xq @ mxq(f64(wsk), 0, "e4m3"))


def temporal_decoder(g, fut, vp):
    u = np.maximum(g + f64(fut), 0.0)
    return np.sum(f64(vp)[None, :, None] * u, axis=1)


def core(x, fut, w1, w2, wsk, vp, wres):
    xq = mxq(f64(x), 1, "e4m3")
    r = residual_block(xq, w1, w2, wsk)
    g = np.reshape(r, fut.shape)
    dec = temporal_decoder(g, fut, vp)
    return dec + (xq @ mxq(f64(wres), 0, "e4m3"))


def e4m3fn_bytes(y):
    return np.clip(np.asarray(y, np.float64), -448.0, 448.0).astype(np.float32).astype(ml_dtypes.float8_e4m3fn).view(np.uint8)


def e4m3fn_values(b):
    return np.asarray(b, np.uint8).view(ml_dtypes.float8_e4m3fn).astype(np.float64)


def setup_inputs():
    d = draw0()
    x0 = np.asarray(d['x']).astype(np.float64)
    s = (np.max(np.abs(x0), axis=(0,), keepdims=True) / 448.0).astype(np.float32)
    out = {}
    for k, v in d.items():
        if k == 'x':
            out['x_bytes'] = e4m3fn_bytes(x0 / s.astype(np.float64))
            out['x_scale'] = s
        else:
            out[k] = v
    return out


def reference(x_bytes, x_scale, fut, w1, w2, wsk, vp, wres):
    return core(e4m3fn_values(x_bytes) * x_scale.astype(np.float64), fut, w1, w2, wsk, vp, wres)

@@ -1,0 +1,385 @@
+from contextlib import ExitStack
+
+import concourse.mybir as mybir
+from concourse.masks import make_identity
+
+N, L, F, H, P_DEC = 4096, 512, 512, 256, 4
+PH = P_DEC * H
+FLOPS = 2 * N * (L * F + F * PH + L * PH + L * H)
+
+F32 = mybir.dt.float32
+BF16 = mybir.dt.bfloat16
+U32 = mybir.dt.uint32
+U8 = mybir.dt.uint8
+FP8 = mybir.dt.float8_e4m3fn
+FP8X4 = mybir.dt.float8_e4m3fn_x4
+ADD = mybir.AluOpType.add
+MULT = mybir.AluOpType.mult
+RELU = mybir.ActivationFunctionType.Relu
+
+P = 128
+SHARE = 256
+LEAD = 4
+STEP = 256
+STEPS = N // STEP
+GROUPS = [2, 2, 4, 4, 4]
+W1E = "VS"
+WE = "SSSSSVSSS"
+
+
+def tile_tideresidualencodertemporaldecoder_t_kernel(
+    tc, x_bytes, x_scale, fut, w1, w2, wsk, vp, wres, out
+):
+    nc = tc.nc
+    with ExitStack() as ctx:
+        keep = ctx.enter_context(tc.tile_pool(name="keep", bufs=1))
+        work = ctx.enter_context(tc.tile_pool(name="work", bufs=2))
+        psum = ctx.enter_context(tc.psum_pool(name="psum", bufs=1))
+        ctx.enter_context(tc.manual_schedule())
+
+        place = []
+        x_view, fut_view, out_view = [], [], []
+        row0 = 0
+        for count in GROUPS:
+            rows = slice(row0, row0 + count * STEP)
+            x_view.append(x_bytes[rows, :].rearrange("(p i) k -> p i k", p=P))
+            fut_view.append(fut[rows, :, :].rearrange("(p i) q j -> p i (q j)", p=P))
+            out_view.append(out[rows, :].rearrange("(p i) j -> p i j", p=P))
+            for j in range(count):
+                place.append((len(x_view) - 1, j))
+            row0 += count * STEP
+
+        x_in, fut_in = {}, {}
+
+        def load_x(g, first=0, count=None):
+            n = GROUPS[g] if count is None else count
+            t = keep.tile([P, 2 * n, L], U8, name=f"xbytes{g}_{first}", align_bytes=64)
+            nc.sync.dma_start(out=t[:], in_=x_view[g][:, 2 * first : 2 * (first + n), :])
+            for j in range(n):
+                x_in[g, first + j] = t[:, 2 * j : 2 * j + 2, :]
+
+        def load_fut(s):
+            g, j = place[s]
+            t = keep.tile([P, 2, PH], BF16, name=f"fut{s}")
+            nc.sync.dma_start(out=t[:], in_=fut_view[g][:, 2 * j : 2 * j + 2, :])
+            fut_in[s] = t
+
+        def load_w(name, w, cols):
+            t = keep.tile([P, 4, cols.stop - cols.start], BF16, name=name)
+            nc.sync.dma_start(out=t[:], in_=w.rearrange("(p j) c -> p j c", j=4)[:, :, cols])
+            return t
+
+        scale = keep.tile([P, 2 * L], F32, name="scale")
+        scale_col = keep.tile([P, 4], F32, name="scale_col")
+        nc.scalar.dma_start(out=scale_col[:], in_=x_scale.rearrange("o (n c) -> (o n) c", c=4))
+        load_x(0, 0, 1)
+        w1_raw = load_w("w1_raw", w1, slice(0, F))
+        load_x(0, 1, 1)
+        wsk_raw = [load_w(f"wsk_raw{b}", wsk, slice(512 * b, 512 * b + 512)) for b in range(2)]
+        w2_raw = [load_w(f"w2_raw{b}", w2, slice(512 * b, 512 * b + 512)) for b in range(2)]
+        wres_raw = load_w("wres_raw", wres, slice(0, H))
+        vp_bf = keep.tile([P, P_DEC], BF16, name="vp_bf")
+        nc.vector.memset(vp_bf[:], 0.0)
+        nc.sync.dma_start(out=vp_bf[0:1, :], in_=vp.rearrange("(o q) -> o q", o=1))
+        load_x(1)
+        load_fut(0)
+        load_fut(1)
+        load_x(2)
+        for s in range(2, 6):
+            load_fut(s)
+        load_x(3)
+        for s in range(6, 10):
+            load_fut(s)
+        load_x(4)
+        for s in range(10, 16):
+            load_fut(s)
+
+        warm = keep.tile([P, 1], F32, name="warm")
+        nc.vector.memset(warm[:], 0.0)
+        nc.scalar.activation(out=warm[:], in_=warm[:], func=RELU)
+        ident = keep.tile([P, P], F32, name="ident")
+        make_identity(nc, ident[:])
+        ident_bf = keep.tile([P, P], BF16, name="ident_bf")
+        make_identity(nc, ident_bf[:])
+        ones_bf = keep.tile([P, P], BF16, name="ones_bf")
+        nc.vector.memset(ones_bf[:], 1.0)
+
+        bank = psum.tile([P, 4, P], F32, name="sbank", tag="rb", bufs=4)
+        for c in range(4):
+            nc.tensor.transpose(bank[:, c, :], scale_col[:, c : c + 1].to_broadcast([P, P]), ident[:])
+        nc.scalar.copy(out=scale[:, 0:L].rearrange("p (n c) -> p n c", c=4), in_=bank[:].rearrange("p c n -> p n c"))
+        nc.scalar.copy(out=scale[:, L : 2 * L], in_=scale[:, 0:L])
+
+        xc, xb, xg, xq, xs, hg, hq, hs, xt, hb, rb, res, zt, acc, both = ({} for i in range(15))
+
+        def x_bytes_of(s):
+            g, j = place[s]
+            return x_in[g, j].rearrange("p i k -> p (i k)").bitcast(FP8)
+
+        def cast(s):
+            xc[s] = work.tile([P, 2 * L], BF16, name="xc")
+            nc.scalar.copy(out=xc[s][:, SHARE:], in_=x_bytes_of(s)[:, SHARE:])
+
+        def widen_gpsimd(s):
+            xb[s] = work.tile([P, 2 * L], BF16, name="xb", bufs=3, align_bytes=64)
+            nc.vector.tensor_tensor(
+                out=xb[s][:, 0 : SHARE + 2], in0=x_bytes_of(s)[:, 0 : SHARE + 2], in1=scale[:, 0 : SHARE + 2], op=MULT
+            )
+            nc.gpsimd.tensor_tensor(out=xb[s][:, SHARE:], in0=xc[s][:, SHARE:], in1=scale[:, SHARE:], op=MULT)
+
+        def transposes(s):
+            xt[s] = psum.tile([P, 512], F32, name="xt", bufs=1)
+            words = xb[s][:].bitcast(F32)
+            for i in range(2):
+                for u in range(2):
+                    nc.tensor.transpose(
+                        xt[s][:, (2 * i + u) * P : (2 * i + u + 1) * P],
+                        words[:, 256 * i + u : 256 * (i + 1) : 2],
+                        ident[:],
+                    )
+
+        def empty_x(s):
+            if s >= 3:
+                xg[s] = both[s - 1][:, 4 * STEP : 8 * STEP]
+            else:
+                xg[s] = work.tile([P, 4 * STEP], BF16, name="xg", align_bytes=64)
+            nc.scalar.copy(
+                out=xg[s][:].bitcast(F32).rearrange("q (i p u) -> q i p u", i=2, u=2),
+                in_=xt[s][:].rearrange("q (i u p) -> q i p u", i=2, u=2),
+            )
+
+        def quantize_x(s):
+            xq[s] = work.tile([P, STEP], U32, name="xq", bufs=5, align_bytes=64)
+            xs[s] = work.tile([P, STEP], U8, name="xs", bufs=5, align_bytes=64)
+            nc.vector.quantize_mx(out=xq[s][:].bitcast(FP8X4), scales=xs[s][:], in_=xg[s][:])
+
+        def hidden(s):
+            for i in range(2):
+                hb[s, i] = psum.tile([P, 512], F32, name="hb", bufs=2)
+                cols = slice(i * P, i * P + P)
+                for t in range(4):
+                    part = slice(t * P, t * P + P)
+                    nc.tensor.matmul_mx(
+                        out=hb[s, i][:, part],
+                        lhsT=w1_q[:, part].bitcast(FP8X4), lhsT_scale=w1_s[:, part],
+                        rhs=xq[s][:, cols].bitcast(FP8X4), rhs_scale=xs[s][:, cols],
+                        start=True, stop=True,
+                    )
+
+        def relu_h(s):
+            if s >= 2 and s + 1 < STEPS:
+                both[s] = work.tile([P, 8 * STEP], BF16, name="both", align_bytes=64)
+                hg[s] = both[s][:, 0 : 4 * STEP]
+            else:
+                hg[s] = work.tile([P, 4 * STEP], BF16, name="hg", align_bytes=64)
+            for i in range(2):
+                nc.scalar.activation(
+                    out=hg[s][:, 512 * i : 512 * i + 512].rearrange("m (n t) -> m n t", t=4),
+                    in_=hb[s, i][:].rearrange("m (t n) -> m n t", t=4),
+                    func=RELU,
+                )
+
+        def quantize_both(s):
+            codes = work.tile([P, 2 * STEP], U32, name="codes", bufs=6, align_bytes=64)
+            scales = work.tile([P, 2 * STEP], U8, name="scales", bufs=6, align_bytes=64)
+            nc.vector.quantize_mx(out=codes[:].bitcast(FP8X4), scales=scales[:], in_=both[s][:])
+            hq[s], hs[s] = codes[:, 0:STEP], scales[:, 0:STEP]
+            xq[s + 1], xs[s + 1] = codes[:, STEP : 2 * STEP], scales[:, STEP : 2 * STEP]
+
+        def quantize_h(s):
+            hq[s] = work.tile([P, STEP], U32, name="hq", bufs=4, align_bytes=64)
+            hs[s] = work.tile([P, STEP], U8, name="hs", bufs=4, align_bytes=64)
+            nc.vector.quantize_mx(out=hq[s][:].bitcast(FP8X4), scales=hs[s][:], in_=hg[s][:])
+
+        def main(s, i):
+            cols = slice(i * P, i * P + P)
+            for b in range(2):
+                rb[s, i, b] = psum.tile([P, 512], F32, name="rb", bufs=4)
+                nc.tensor.matmul_mx(
+                    out=rb[s, i, b][:],
+                    lhsT=xq[s][:, cols].bitcast(FP8X4), lhsT_scale=xs[s][:, cols],
+                    rhs=wsk_q[b][:].bitcast(FP8X4), rhs_scale=wsk_s[b][:],
+                    start=True, stop=False,
+                )
+            for b in range(2):
+                nc.tensor.matmul_mx(
+                    out=rb[s, i, b][:],
+                    lhsT=hq[s][:, cols].bitcast(FP8X4), lhsT_scale=hs[s][:, cols],
+                    rhs=w2_q[b][:].bitcast(FP8X4), rhs_scale=w2_s[b][:],
+                    start=False, stop=True,
+                )
+
+        def skip(s):
+            res[s] = psum.tile([P, 512], F32, name="res", bufs=1)
+            for i in range(2):
+                cols = slice(i * P, i * P + P)
+                nc.tensor.matmul_mx(
+                    out=res[s][:, H * i : H * i + H],
+                    lhsT=xq[s][:, cols].bitcast(FP8X4), lhsT_scale=xs[s][:, cols],
+                    rhs=wres_q[:].bitcast(FP8X4), rhs_scale=wres_s[:],
+                    start=True, stop=True,
+                )
+
+        def add_fut(s, i):
+            q, half = s // 2, 2 * (s % 2)
+            if q not in zt:
+                zt[q] = work.tile([P, 4, PH], F32, name="zt", bufs=2)
+            for b in range(2):
+                cols = slice(512 * b, 512 * b + 512)
+                nc.vector.tensor_tensor(
+                    out=zt[q][:, half + i, cols], in0=rb[s, i, b][:], in1=fut_in[s][:, i, cols], op=ADD
+                )
+
+        def relu_z(s, pieces=1):
+            q, half = s // 2, 2 * (s % 2)
+            z = zt[q][:, half : half + 2, :].rearrange("p i c -> p (i c)")
+            width = 2 * PH // pieces
+            for c in range(pieces):
+                cols = slice(width * c, width * c + width)
+                nc.scalar.activation(out=z[:, cols], in_=z[:, cols], func=RELU)
+
+        def weigh_first(s, rows=slice(0, 2)):
+            q, half = s // 2, 2 * (s % 2)
+            if q not in acc:
+                acc[q] = work.tile([P, 4, H], F32, name="acc", bufs=2)
+            to = slice(half + rows.start, half + rows.stop)
+            nc.vector.scalar_tensor_tensor(
+                out=acc[q][:, to, :], in0=zt[q][:, to, 0:H], scalar=vp_f[:, 0:1],
+                in1=res[s][:].rearrange("p (i j) -> p i j", i=2)[:, rows, :], op0=MULT, op1=ADD,
+            )
+
+        def weigh(q, p, rows=slice(0, 4)):
+            nc.vector.scalar_tensor_tensor(
+                out=acc[q][:, rows, :], in0=zt[q][:, rows, H * p : H * p + H],
+                scalar=vp_f[:, p : p + 1], in1=acc[q][:, rows, :], op0=MULT, op1=ADD,
+            )
+
+        def store(q, rows=slice(0, 4)):
+            g, j = place[2 * q]
+            nc.sync.dma_start(
+                out=out_view[g][:, 2 * j + rows.start : 2 * j + rows.stop, :], in_=acc[q][:, rows, :]
+            )
+
+        def quantize_w(name, group):
+            width = group.shape[1] // 4
+            q = keep.tile([P, width], U32, name=name + "_q", align_bytes=64)
+            sc = keep.tile([P, width], U8, name=name + "_s", align_bytes=64)
+            nc.vector.quantize_mx(out=q[:].bitcast(FP8X4), scales=sc[:], in_=group[:])
+            return q, sc
+
+        def spread(raw, group, c0, engine, view=None):
+            bank = psum.tile([P, 4, 256], BF16, name="wbank", tag="rb", bufs=4)
+            for j in range(4):
+                src = raw[:, j, c0 : c0 + 256] if view is None else view[:, j]
+                nc.tensor.matmul(out=bank[:, j, :], lhsT=ident_bf[:], rhs=src, start=True, stop=True)
+            dst = group[:, 4 * c0 : 4 * c0 + 1024].rearrange("p (c j) -> p c j", j=4)
+            src = bank[:].rearrange("p j c -> p c j")
+            if engine == "V":
+                nc.vector.tensor_copy(out=dst, in_=src)
+            else:
+                nc.scalar.copy(out=dst, in_=src)
+
+        def group_tile(name, width):
+            return keep.tile([P, 4 * width], BF16, name=name + "_g", align_bytes=64)
+
+        wsk_q, wsk_s, w2_q, w2_s = [None] * 2, [None] * 2, [None] * 2, [None] * 2
+        wsk_g = [group_tile(f"wsk{b}", 512) for b in range(2)]
+        w2_g = [group_tile(f"w2{b}", 512) for b in range(2)]
+        wres_g = group_tile("wres", H)
+        w1_g = group_tile("w1", F)
+        w1_t = w1_raw[:].rearrange("p j (m t) -> p j t m", t=4)
+
+        def widen(s):
+            xb[s] = work.tile([P, 2 * L], BF16, name="xb", bufs=3, align_bytes=64)
+            parts = 2 if s == 0 else 1
+            for i in range(parts):
+                cols = slice(2 * L // parts * i, 2 * L // parts * (i + 1))
+                nc.vector.tensor_tensor(out=xb[s][:, cols], in0=x_bytes_of(s)[:, cols], in1=scale[:, 0 : cols.stop - cols.start], op=MULT)
+
+        widen(0)
+        transposes(0)
+        empty_x(0)
+        spread(w1_raw, w1_g, 0, W1E[0], w1_t[:, :, 0:2, :])
+        quantize_x(0)
+        spread(w1_raw, w1_g, 256, W1E[1], w1_t[:, :, 2:4, :])
+        w1_q, w1_s = quantize_w("w1", w1_g)
+        spread(wsk_raw[0], wsk_g[0], 0, WE[0])
+        spread(wsk_raw[0], wsk_g[0], 256, WE[1])
+        hidden(0)
+        relu_h(0)
+        widen(1)
+        wsk_q[0], wsk_s[0] = quantize_w("wsk0", wsk_g[0])
+        transposes(1)
+        empty_x(1)
+        quantize_h(0)
+        quantize_x(1)
+        vp_f = keep.tile([P, P_DEC], F32, name="vp_f")
+        vbank = psum.tile([P, P_DEC], F32, name="vbank", tag="rb", bufs=4)
+        nc.tensor.matmul(out=vbank[:], lhsT=ones_bf[:], rhs=vp_bf[:], start=True, stop=True)
+        nc.vector.tensor_copy(out=vp_f[:], in_=vbank[:])
+        spread(wsk_raw[1], wsk_g[1], 0, WE[2])
+        widen(2)
+        spread(wsk_raw[1], wsk_g[1], 256, WE[3])
+        widen(3)
+        spread(w2_raw[0], w2_g[0], 0, WE[4])
+        spread(w2_raw[0], w2_g[0], 256, WE[5])
+        spread(w2_raw[1], w2_g[1], 0, WE[6])
+        wsk_q[1], wsk_s[1] = quantize_w("wsk1", wsk_g[1])
+        w2_q[0], w2_s[0] = quantize_w("w20", w2_g[0])
+        hidden(1)
+        relu_h(1)
+        spread(w2_raw[1], w2_g[1], 256, WE[7])
+        transposes(2)
+        w2_q[1], w2_s[1] = quantize_w("w21", w2_g[1])
+        empty_x(2)
+        spread(wres_raw, wres_g, 0, WE[8])
+        quantize_x(2)
+        quantize_h(1)
+        wres_q, wres_s = quantize_w("wres", wres_g)
+        cast(LEAD)
+
+        for s in range(STEPS):
+            q, odd = s // 2, s % 2
+            main(s, 0)
+            if s >= 1:
+                skip(s - 1)
+            main(s, 1)
+            if s + 2 < STEPS:
+                hidden(s + 2)
+            if s + 3 < STEPS:
+                transposes(s + 3)
+            if s + LEAD < STEPS:
+                widen_gpsimd(s + LEAD)
+            add_fut(s, 0)
+            add_fut(s, 1)
+            if s + 2 < STEPS:
+                relu_h(s + 2)
+            if s + 3 < STEPS:
+                empty_x(s + 3)
+            if s + LEAD + 1 < STEPS:
+                cast(s + LEAD + 1)
+            relu_z(s, 4 if s == STEPS - 1 else 1)
+            if s >= 1:
+                weigh_first(s - 1)
+            if odd and q >= 1:
+                weigh(q - 1, 2)
+            if s + 3 < STEPS:
+                quantize_both(s + 2)
+            elif s + 2 < STEPS:
+                quantize_h(s + 2)
+            if q >= 1:
+                weigh(q - 1, 3 if odd else 1)
+            if odd and q >= 1:
+                store(q - 1)
+        last = STEPS // 2 - 1
+        skip(STEPS - 1)
+        for p in range(1, P_DEC):
+            weigh(last, p, slice(0, 2))
+        store(last, slice(0, 2))
+        for i in range(2):
+            weigh_first(STEPS - 1, slice(i, i + 1))
+        for p in range(1, P_DEC):
+            for i in range(2):
+                weigh(last, p, slice(2 + i, 3 + i))
+                if p == P_DEC - 1:
+                    store(last, slice(2 + i, 3 + i))

@@ -18,13 +18,11 @@ MULT = mybir.AluOpType.mult
 RELU = mybir.ActivationFunctionType.Relu
 
 P = 128
-SHARE = 256
-LEAD = 4
 STEP = 256
 STEPS = N // STEP
-GROUPS = [2, 2, 4, 4, 4]
-W1E = "VS"
-WE = "SSSSSVSSS"
+LEAD = 4
+FUT_AHEAD = 4
+X_GROUP = 4
 
 
 def tile_tideresidualencodertemporaldecoder_t_kernel(
@@ -37,95 +35,84 @@ def tile_tideresidualencodertemporaldecoder_t_kernel(
         psum = ctx.enter_context(tc.psum_pool(name="psum", bufs=1))
         ctx.enter_context(tc.manual_schedule())
 
-        place = []
-        x_view, fut_view, out_view = [], [], []
-        row0 = 0
-        for count in GROUPS:
-            rows = slice(row0, row0 + count * STEP)
-            x_view.append(x_bytes[rows, :].rearrange("(p i) k -> p i k", p=P))
-            fut_view.append(fut[rows, :, :].rearrange("(p i) q j -> p i (q j)", p=P))
-            out_view.append(out[rows, :].rearrange("(p i) j -> p i j", p=P))
-            for j in range(count):
-                place.append((len(x_view) - 1, j))
-            row0 += count * STEP
+        x_view = x_bytes.rearrange("(s p i) k -> p s (i k)", p=P, i=2)
+        fut_view = fut.rearrange("(s p i) q j -> p s i (q j)", p=P, i=2)
+        out_view = out.rearrange("(s p i) j -> p s i j", p=P, i=2)
 
         x_in, fut_in = {}, {}
 
-        def load_x(g, first=0, count=None):
-            n = GROUPS[g] if count is None else count
-            t = keep.tile([P, 2 * n, L], U8, name=f"xbytes{g}_{first}", align_bytes=64)
-            nc.sync.dma_start(out=t[:], in_=x_view[g][:, 2 * first : 2 * (first + n), :])
-            for j in range(n):
-                x_in[g, first + j] = t[:, 2 * j : 2 * j + 2, :]
+        def load_x(first, count):
+            t = keep.tile([P, count, 2 * L], U8, name=f"xbytes{first}", align_bytes=64)
+            nc.sync.dma_start(out=t[:], in_=x_view[:, first : first + count, :])
+            for j in range(count):
+                x_in[first + j] = t[:, j, :].bitcast(FP8)
 
         def load_fut(s):
-            g, j = place[s]
-            t = keep.tile([P, 2, PH], BF16, name=f"fut{s}")
-            nc.sync.dma_start(out=t[:], in_=fut_view[g][:, 2 * j : 2 * j + 2, :])
-            fut_in[s] = t
+            fut_in[s] = work.tile([P, 2, PH], BF16, name="fut_in", bufs=FUT_AHEAD + 1)
+            nc.sync.dma_start(out=fut_in[s][:], in_=fut_view[:, s, :, :])
 
         def load_w(name, w, cols):
             t = keep.tile([P, 4, cols.stop - cols.start], BF16, name=name)
             nc.sync.dma_start(out=t[:], in_=w.rearrange("(p j) c -> p j c", j=4)[:, :, cols])
             return t
 
-        scale = keep.tile([P, 2 * L], F32, name="scale")
+        scale = keep.tile([P, L], F32, name="scale")
         scale_col = keep.tile([P, 4], F32, name="scale_col")
         nc.scalar.dma_start(out=scale_col[:], in_=x_scale.rearrange("o (n c) -> (o n) c", c=4))
-        load_x(0, 0, 1)
-        w1_raw = load_w("w1_raw", w1, slice(0, F))
-        load_x(0, 1, 1)
-        wsk_raw = [load_w(f"wsk_raw{b}", wsk, slice(512 * b, 512 * b + 512)) for b in range(2)]
-        w2_raw = [load_w(f"w2_raw{b}", w2, slice(512 * b, 512 * b + 512)) for b in range(2)]
-        wres_raw = load_w("wres_raw", wres, slice(0, H))
         vp_bf = keep.tile([P, P_DEC], BF16, name="vp_bf")
         nc.vector.memset(vp_bf[:], 0.0)
-        nc.sync.dma_start(out=vp_bf[0:1, :], in_=vp.rearrange("(o q) -> o q", o=1))
-        load_x(1)
+        halves = [slice(0, 512), slice(512, 1024)]
+        w1_raw = load_w("w1_raw", w1, slice(0, F))
+        load_x(0, 1)
+        load_x(1, 2)
+        wsk_raw, w2_raw = {}, {}
+        wsk_raw[0] = load_w("wsk_raw0", wsk, halves[0])
+        w2_raw[0] = load_w("w2_raw0", w2, halves[0])
+        wsk_raw[1] = load_w("wsk_raw1", wsk, halves[1])
+        load_x(3, 2)
+        w2_raw[1] = load_w("w2_raw1", w2, halves[1])
         load_fut(0)
+        wres_raw = load_w("wres_raw", wres, slice(0, H))
+        nc.sync.dma_start(out=vp_bf[0:1, :], in_=vp.rearrange("(o q) -> o q", o=1))
         load_fut(1)
-        load_x(2)
-        for s in range(2, 6):
-            load_fut(s)
-        load_x(3)
-        for s in range(6, 10):
-            load_fut(s)
-        load_x(4)
-        for s in range(10, 16):
-            load_fut(s)
+        load_x(5, 5)
+        load_fut(2)
+        load_fut(3)
+        load_x(10, 6)
 
-        warm = keep.tile([P, 1], F32, name="warm")
-        nc.vector.memset(warm[:], 0.0)
-        nc.scalar.activation(out=warm[:], in_=warm[:], func=RELU)
         ident = keep.tile([P, P], F32, name="ident")
         make_identity(nc, ident[:])
         ident_bf = keep.tile([P, P], BF16, name="ident_bf")
-        make_identity(nc, ident_bf[:])
+        nc.scalar.activation(out=ident_bf[:], in_=ident[:], func=RELU)
         ones_bf = keep.tile([P, P], BF16, name="ones_bf")
         nc.vector.memset(ones_bf[:], 1.0)
 
         bank = psum.tile([P, 4, P], F32, name="sbank", tag="rb", bufs=4)
         for c in range(4):
             nc.tensor.transpose(bank[:, c, :], scale_col[:, c : c + 1].to_broadcast([P, P]), ident[:])
-        nc.scalar.copy(out=scale[:, 0:L].rearrange("p (n c) -> p n c", c=4), in_=bank[:].rearrange("p c n -> p n c"))
-        nc.scalar.copy(out=scale[:, L : 2 * L], in_=scale[:, 0:L])
+        nc.scalar.copy(out=scale[:].rearrange("p (n c) -> p n c", c=4), in_=bank[:].rearrange("p c n -> p n c"))
 
-        xc, xb, xg, xq, xs, hg, hq, hs, xt, hb, rb, res, zt, acc, both = ({} for i in range(15))
+        xc, xb, xg, xq, xs, hg, hq, hs, xt, hb, rb, res, zt, acc = ({} for i in range(14))
+        ring = [keep.tile([P, 8 * STEP], BF16, name=f"ring{r}", align_bytes=64) for r in range(2)]
 
-        def x_bytes_of(s):
-            g, j = place[s]
-            return x_in[g, j].rearrange("p i k -> p (i k)").bitcast(FP8)
+        def widen(s):
+            xb[s] = work.tile([P, 2 * L], BF16, name="xb", bufs=LEAD, align_bytes=64)
+            for i in range(2):
+                cols = slice(L * i, L * i + L)
+                nc.vector.tensor_tensor(out=xb[s][:, cols], in0=x_in[s][:, cols], in1=scale[:], op=MULT)
 
         def cast(s):
             xc[s] = work.tile([P, 2 * L], BF16, name="xc")
-            nc.scalar.copy(out=xc[s][:, SHARE:], in_=x_bytes_of(s)[:, SHARE:])
+            nc.scalar.copy(out=xc[s][:], in_=x_in[s])
 
-        def widen_gpsimd(s):
-            xb[s] = work.tile([P, 2 * L], BF16, name="xb", bufs=3, align_bytes=64)
-            nc.vector.tensor_tensor(
-                out=xb[s][:, 0 : SHARE + 2], in0=x_bytes_of(s)[:, 0 : SHARE + 2], in1=scale[:, 0 : SHARE + 2], op=MULT
+        def product(s):
+            xb[s] = ring[(s - 3) % 2][:, 0 : 2 * L]
+            nc.gpsimd.tensor_tensor(
+                out=xb[s].rearrange("p (i k) -> p i k", i=2),
+                in0=xc[s][:].rearrange("p (i k) -> p i k", i=2),
+                in1=scale[:].unsqueeze(1).to_broadcast([P, 2, L]),
+                op=MULT,
             )
-            nc.gpsimd.tensor_tensor(out=xb[s][:, SHARE:], in0=xc[s][:, SHARE:], in1=scale[:, SHARE:], op=MULT)
 
         def transposes(s):
             xt[s] = psum.tile([P, 512], F32, name="xt", bufs=1)
@@ -140,7 +127,7 @@ def tile_tideresidualencodertemporaldecoder_t_kernel(
 
         def empty_x(s):
             if s >= 3:
-                xg[s] = both[s - 1][:, 4 * STEP : 8 * STEP]
+                xg[s] = ring[(s - 1) % 2][:, 4 * STEP : 8 * STEP]
             else:
                 xg[s] = work.tile([P, 4 * STEP], BF16, name="xg", align_bytes=64)
             nc.scalar.copy(
@@ -148,10 +135,23 @@ def tile_tideresidualencodertemporaldecoder_t_kernel(
                 in_=xt[s][:].rearrange("q (i u p) -> q i p u", i=2, u=2),
             )
 
+        def quantize(name, source, bufs):
+            width = source.shape[1] // 4
+            codes = work.tile([P, width], U32, name=name + "_q", bufs=bufs, align_bytes=64)
+            scales = work.tile([P, width], U8, name=name + "_s", bufs=bufs, align_bytes=64)
+            nc.vector.quantize_mx(out=codes[:].bitcast(FP8X4), scales=scales[:], in_=source)
+            return codes, scales
+
         def quantize_x(s):
-            xq[s] = work.tile([P, STEP], U32, name="xq", bufs=5, align_bytes=64)
-            xs[s] = work.tile([P, STEP], U8, name="xs", bufs=5, align_bytes=64)
-            nc.vector.quantize_mx(out=xq[s][:].bitcast(FP8X4), scales=xs[s][:], in_=xg[s][:])
+            xq[s], xs[s] = quantize("x", xg[s][:], 3)
+
+        def quantize_h(s):
+            hq[s], hs[s] = quantize("h", hg[s][:], 3)
+
+        def quantize_both(s):
+            codes, scales = quantize("both", ring[s % 2][:], 5)
+            hq[s], hs[s] = codes[:, 0:STEP], scales[:, 0:STEP]
+            xq[s + 1], xs[s + 1] = codes[:, STEP : 2 * STEP], scales[:, STEP : 2 * STEP]
 
         def hidden(s):
             for i in range(2):
@@ -167,9 +167,8 @@ def tile_tideresidualencodertemporaldecoder_t_kernel(
                     )
 
         def relu_h(s):
-            if s >= 2 and s + 1 < STEPS:
-                both[s] = work.tile([P, 8 * STEP], BF16, name="both", align_bytes=64)
-                hg[s] = both[s][:, 0 : 4 * STEP]
+            if s >= 2:
+                hg[s] = ring[s % 2][:, 0 : 4 * STEP]
             else:
                 hg[s] = work.tile([P, 4 * STEP], BF16, name="hg", align_bytes=64)
             for i in range(2):
@@ -179,35 +178,21 @@ def tile_tideresidualencodertemporaldecoder_t_kernel(
                     func=RELU,
                 )
 
-        def quantize_both(s):
-            codes = work.tile([P, 2 * STEP], U32, name="codes", bufs=6, align_bytes=64)
-            scales = work.tile([P, 2 * STEP], U8, name="scales", bufs=6, align_bytes=64)
-            nc.vector.quantize_mx(out=codes[:].bitcast(FP8X4), scales=scales[:], in_=both[s][:])
-            hq[s], hs[s] = codes[:, 0:STEP], scales[:, 0:STEP]
-            xq[s + 1], xs[s + 1] = codes[:, STEP : 2 * STEP], scales[:, STEP : 2 * STEP]
-
-        def quantize_h(s):
-            hq[s] = work.tile([P, STEP], U32, name="hq", bufs=4, align_bytes=64)
-            hs[s] = work.tile([P, STEP], U8, name="hs", bufs=4, align_bytes=64)
-            nc.vector.quantize_mx(out=hq[s][:].bitcast(FP8X4), scales=hs[s][:], in_=hg[s][:])
-
-        def main(s, i):
+        def main(s, i, b):
             cols = slice(i * P, i * P + P)
-            for b in range(2):
-                rb[s, i, b] = psum.tile([P, 512], F32, name="rb", bufs=4)
-                nc.tensor.matmul_mx(
-                    out=rb[s, i, b][:],
-                    lhsT=xq[s][:, cols].bitcast(FP8X4), lhsT_scale=xs[s][:, cols],
-                    rhs=wsk_q[b][:].bitcast(FP8X4), rhs_scale=wsk_s[b][:],
-                    start=True, stop=False,
-                )
-            for b in range(2):
-                nc.tensor.matmul_mx(
-                    out=rb[s, i, b][:],
-                    lhsT=hq[s][:, cols].bitcast(FP8X4), lhsT_scale=hs[s][:, cols],
-                    rhs=w2_q[b][:].bitcast(FP8X4), rhs_scale=w2_s[b][:],
-                    start=False, stop=True,
-                )
+            rb[s, i, b] = psum.tile([P, 512], F32, name="rb", bufs=4)
+            nc.tensor.matmul_mx(
+                out=rb[s, i, b][:],
+                lhsT=xq[s][:, cols].bitcast(FP8X4), lhsT_scale=xs[s][:, cols],
+                rhs=wsk_q[b][:].bitcast(FP8X4), rhs_scale=wsk_s[b][:],
+                start=True, stop=False,
+            )
+            nc.tensor.matmul_mx(
+                out=rb[s, i, b][:],
+                lhsT=hq[s][:, cols].bitcast(FP8X4), lhsT_scale=hs[s][:, cols],
+                rhs=w2_q[b][:].bitcast(FP8X4), rhs_scale=w2_s[b][:],
+                start=False, stop=True,
+            )
 
         def skip(s):
             res[s] = psum.tile([P, 512], F32, name="res", bufs=1)
@@ -220,166 +205,154 @@ def tile_tideresidualencodertemporaldecoder_t_kernel(
                     start=True, stop=True,
                 )
 
-        def add_fut(s, i):
-            q, half = s // 2, 2 * (s % 2)
-            if q not in zt:
-                zt[q] = work.tile([P, 4, PH], F32, name="zt", bufs=2)
-            for b in range(2):
-                cols = slice(512 * b, 512 * b + 512)
-                nc.vector.tensor_tensor(
-                    out=zt[q][:, half + i, cols], in0=rb[s, i, b][:], in1=fut_in[s][:, i, cols], op=ADD
-                )
+        def add_fut(s, i, b):
+            if s not in zt:
+                zt[s] = work.tile([P, 2, PH], F32, name="zt", bufs=4)
+            nc.vector.tensor_tensor(
+                out=zt[s][:, i, halves[b]], in0=rb[s, i, b][:], in1=fut_in[s][:, i, halves[b]], op=ADD
+            )
 
-        def relu_z(s, pieces=1):
-            q, half = s // 2, 2 * (s % 2)
-            z = zt[q][:, half : half + 2, :].rearrange("p i c -> p (i c)")
-            width = 2 * PH // pieces
-            for c in range(pieces):
-                cols = slice(width * c, width * c + width)
-                nc.scalar.activation(out=z[:, cols], in_=z[:, cols], func=RELU)
+        def relu_z(s, b):
+            nc.scalar.activation(out=zt[s][:, :, halves[b]], in_=zt[s][:, :, halves[b]], func=RELU)
 
-        def weigh_first(s, rows=slice(0, 2)):
-            q, half = s // 2, 2 * (s % 2)
-            if q not in acc:
-                acc[q] = work.tile([P, 4, H], F32, name="acc", bufs=2)
-            to = slice(half + rows.start, half + rows.stop)
+        def weigh(s, p, rows=slice(0, 2)):
+            if s not in acc:
+                acc[s] = work.tile([P, 2, H], F32, name="acc", bufs=4)
+            before = res[s][:].rearrange("p (i j) -> p i j", i=2) if p == 0 else acc[s]
             nc.vector.scalar_tensor_tensor(
-                out=acc[q][:, to, :], in0=zt[q][:, to, 0:H], scalar=vp_f[:, 0:1],
-                in1=res[s][:].rearrange("p (i j) -> p i j", i=2)[:, rows, :], op0=MULT, op1=ADD,
+                out=acc[s][:, rows, :], in0=zt[s][:, rows, H * p : H * p + H],
+                scalar=vp_f[:, p : p + 1], in1=before[:, rows, :], op0=MULT, op1=ADD,
             )
 
-        def weigh(q, p, rows=slice(0, 4)):
-            nc.vector.scalar_tensor_tensor(
-                out=acc[q][:, rows, :], in0=zt[q][:, rows, H * p : H * p + H],
-                scalar=vp_f[:, p : p + 1], in1=acc[q][:, rows, :], op0=MULT, op1=ADD,
-            )
+        def store(s, rows=slice(0, 2)):
+            nc.sync.dma_start(out=out_view[:, s, rows, :], in_=acc[s][:, rows, :])
 
-        def store(q, rows=slice(0, 4)):
-            g, j = place[2 * q]
-            nc.sync.dma_start(
-                out=out_view[g][:, 2 * j + rows.start : 2 * j + rows.stop, :], in_=acc[q][:, rows, :]
-            )
+        groups = {}
 
-        def quantize_w(name, group):
-            width = group.shape[1] // 4
-            q = keep.tile([P, width], U32, name=name + "_q", align_bytes=64)
-            sc = keep.tile([P, width], U8, name=name + "_s", align_bytes=64)
-            nc.vector.quantize_mx(out=q[:].bitcast(FP8X4), scales=sc[:], in_=group[:])
-            return q, sc
-
-        def spread(raw, group, c0, engine, view=None):
-            bank = psum.tile([P, 4, 256], BF16, name="wbank", tag="rb", bufs=4)
-            for j in range(4):
-                src = raw[:, j, c0 : c0 + 256] if view is None else view[:, j]
-                nc.tensor.matmul(out=bank[:, j, :], lhsT=ident_bf[:], rhs=src, start=True, stop=True)
-            dst = group[:, 4 * c0 : 4 * c0 + 1024].rearrange("p (c j) -> p c j", j=4)
-            src = bank[:].rearrange("p j c -> p c j")
+        def spread(name, view, c0, engine, tag="rb", bufs=4):
+            if name not in groups:
+                groups[name] = keep.tile([P, 4 * view.shape[1]], BF16, name=name + "_g", align_bytes=64)
+            bank = psum.tile([P, 2, 512], BF16, name="wbank", tag=tag, bufs=bufs)
+            for n in range(2):
+                first = c0 + P * n
+                nc.tensor.matmul(out=bank[:, n, :], lhsT=ident_bf[:], rhs=view[:, first : first + P, :], start=True, stop=True)
+            dst = groups[name][:, 4 * c0 : 4 * c0 + 1024]
+            src = bank[:].rearrange("p n c -> p (n c)")
             if engine == "V":
                 nc.vector.tensor_copy(out=dst, in_=src)
             else:
                 nc.scalar.copy(out=dst, in_=src)
 
-        def group_tile(name, width):
-            return keep.tile([P, 4 * width], BF16, name=name + "_g", align_bytes=64)
+        def spread_w1(half, engine):
+            if "w1" not in groups:
+                groups["w1"] = keep.tile([P, 4 * F], BF16, name="w1_g", align_bytes=64)
+            view = w1_raw[:].rearrange("p j (m t) -> p t m j", t=4)
+            bank = psum.tile([P, 2, 512], BF16, name="wbank", tag="rb", bufs=4)
+            for n in range(2):
+                nc.tensor.matmul(out=bank[:, n, :], lhsT=ident_bf[:], rhs=view[:, 2 * half + n], start=True, stop=True)
+            dst = groups["w1"][:, 1024 * half : 1024 * half + 1024]
+            src = bank[:].rearrange("p n c -> p (n c)")
+            if engine == "V":
+                nc.vector.tensor_copy(out=dst, in_=src)
+            else:
+                nc.scalar.copy(out=dst, in_=src)
 
-        wsk_q, wsk_s, w2_q, w2_s = [None] * 2, [None] * 2, [None] * 2, [None] * 2
-        wsk_g = [group_tile(f"wsk{b}", 512) for b in range(2)]
-        w2_g = [group_tile(f"w2{b}", 512) for b in range(2)]
-        wres_g = group_tile("wres", H)
-        w1_g = group_tile("w1", F)
-        w1_t = w1_raw[:].rearrange("p j (m t) -> p j t m", t=4)
+        def by_column(raw):
+            return raw[:].rearrange("p j c -> p c j")
 
-        def widen(s):
-            xb[s] = work.tile([P, 2 * L], BF16, name="xb", bufs=3, align_bytes=64)
-            parts = 2 if s == 0 else 1
-            for i in range(parts):
-                cols = slice(2 * L // parts * i, 2 * L // parts * (i + 1))
-                nc.vector.tensor_tensor(out=xb[s][:, cols], in0=x_bytes_of(s)[:, cols], in1=scale[:, 0 : cols.stop - cols.start], op=MULT)
+        wsk_q, wsk_s, w2_q, w2_s = {}, {}, {}, {}
 
+        spread_w1(0, "S")
+        spread_w1(1, "S")
         widen(0)
         transposes(0)
         empty_x(0)
-        spread(w1_raw, w1_g, 0, W1E[0], w1_t[:, :, 0:2, :])
-        quantize_x(0)
-        spread(w1_raw, w1_g, 256, W1E[1], w1_t[:, :, 2:4, :])
-        w1_q, w1_s = quantize_w("w1", w1_g)
-        spread(wsk_raw[0], wsk_g[0], 0, WE[0])
-        spread(wsk_raw[0], wsk_g[0], 256, WE[1])
-        hidden(0)
-        relu_h(0)
         widen(1)
-        wsk_q[0], wsk_s[0] = quantize_w("wsk0", wsk_g[0])
+        w1_q, w1_s = quantize("w1", groups["w1"][:], 1)
+        quantize_x(0)
+        for c0 in (0, 256):
+            spread("wsk0", by_column(wsk_raw[0]), c0, "S")
         transposes(1)
-        empty_x(1)
-        quantize_h(0)
-        quantize_x(1)
-        vp_f = keep.tile([P, P_DEC], F32, name="vp_f")
-        vbank = psum.tile([P, P_DEC], F32, name="vbank", tag="rb", bufs=4)
-        nc.tensor.matmul(out=vbank[:], lhsT=ones_bf[:], rhs=vp_bf[:], start=True, stop=True)
-        nc.vector.tensor_copy(out=vp_f[:], in_=vbank[:])
-        spread(wsk_raw[1], wsk_g[1], 0, WE[2])
+        hidden(0)
         widen(2)
-        spread(wsk_raw[1], wsk_g[1], 256, WE[3])
-        widen(3)
-        spread(w2_raw[0], w2_g[0], 0, WE[4])
-        spread(w2_raw[0], w2_g[0], 256, WE[5])
-        spread(w2_raw[1], w2_g[1], 0, WE[6])
-        wsk_q[1], wsk_s[1] = quantize_w("wsk1", wsk_g[1])
-        w2_q[0], w2_s[0] = quantize_w("w20", w2_g[0])
-        hidden(1)
-        relu_h(1)
-        spread(w2_raw[1], w2_g[1], 256, WE[7])
+        for c0 in (0, 256):
+            spread("w20", by_column(w2_raw[0]), c0, "V")
+        empty_x(1)
+        relu_h(0)
+        wsk_q[0], wsk_s[0] = quantize("wsk0", groups["wsk0"][:], 1)
+        quantize_x(1)
+        w2_q[0], w2_s[0] = quantize("w20", groups["w20"][:], 1)
         transposes(2)
-        w2_q[1], w2_s[1] = quantize_w("w21", w2_g[1])
+        for c0 in (0, 256):
+            spread("wsk1", by_column(wsk_raw[1]), c0, "S")
+        quantize_h(0)
+        hidden(1)
         empty_x(2)
-        spread(wres_raw, wres_g, 0, WE[8])
+        for c0 in (0, 256):
+            spread("w21", by_column(w2_raw[1]), c0, "S")
+        widen(3)
+        wsk_q[1], wsk_s[1] = quantize("wsk1", groups["wsk1"][:], 1)
         quantize_x(2)
-        quantize_h(1)
-        wres_q, wres_s = quantize_w("wres", wres_g)
+        w2_q[1], w2_s[1] = quantize("w21", groups["w21"][:], 1)
+        relu_h(1)
         cast(LEAD)
+        for b in range(2):
+            for i in range(2):
+                main(0, i, b)
+        transposes(3)
+        spread("wres", by_column(wres_raw), 0, "S", "res", 1)
+        vp_f = keep.tile([P, P_DEC], F32, name="vp_f")
+        vbank = psum.tile([P, P_DEC], F32, name="vbank", tag="res", bufs=1)
+        nc.tensor.matmul(out=vbank[:], lhsT=ones_bf[:], rhs=vp_bf[:], start=True, stop=True)
+        nc.scalar.copy(out=vp_f[:], in_=vbank[:])
+        quantize_h(1)
 
         for s in range(STEPS):
-            q, odd = s // 2, s % 2
-            main(s, 0)
-            if s >= 1:
-                skip(s - 1)
-            main(s, 1)
-            if s + 2 < STEPS:
-                hidden(s + 2)
-            if s + 3 < STEPS:
-                transposes(s + 3)
+            if s + FUT_AHEAD < STEPS:
+                load_fut(s + FUT_AHEAD)
             if s + LEAD < STEPS:
-                widen_gpsimd(s + LEAD)
-            add_fut(s, 0)
-            add_fut(s, 1)
-            if s + 2 < STEPS:
-                relu_h(s + 2)
+                product(s + LEAD)
             if s + 3 < STEPS:
                 empty_x(s + 3)
+            if s + 2 < STEPS:
+                hidden(s + 2)
             if s + LEAD + 1 < STEPS:
                 cast(s + LEAD + 1)
-            relu_z(s, 4 if s == STEPS - 1 else 1)
+            for b in range(2):
+                for i in range(2):
+                    add_fut(s, i, b)
+                    if s + 1 < STEPS:
+                        main(s + 1, i, b)
+                if b == 0 and s + 2 < STEPS:
+                    relu_h(s + 2)
             if s >= 1:
-                weigh_first(s - 1)
-            if odd and q >= 1:
-                weigh(q - 1, 2)
+                weigh(s - 1, 0)
+            else:
+                wres_q, wres_s = quantize("wres", groups["wres"][:], 1)
+            skip(s)
+            if s + LEAD < STEPS:
+                transposes(s + LEAD)
+            for b in range(2):
+                relu_z(s, b)
+            if s >= 2:
+                weigh(s - 2, 2)
+            if s >= 1:
+                weigh(s - 1, 1)
+            if s >= 2:
+                weigh(s - 2, 3)
+                store(s - 2)
             if s + 3 < STEPS:
                 quantize_both(s + 2)
             elif s + 2 < STEPS:
                 quantize_h(s + 2)
-            if q >= 1:
-                weigh(q - 1, 3 if odd else 1)
-            if odd and q >= 1:
-                store(q - 1)
-        last = STEPS // 2 - 1
-        skip(STEPS - 1)
-        for p in range(1, P_DEC):
-            weigh(last, p, slice(0, 2))
-        store(last, slice(0, 2))
-        for i in range(2):
-            weigh_first(STEPS - 1, slice(i, i + 1))
+        last = STEPS - 1
+        weigh(last - 1, 2)
+        weigh(last, 0, slice(0, 1))
+        weigh(last - 1, 3)
+        store(last - 1)
+        weigh(last, 0, slice(1, 2))
         for p in range(1, P_DEC):
             for i in range(2):
-                weigh(last, p, slice(2 + i, 3 + i))
+                weigh(last, p, slice(i, i + 1))
                 if p == P_DEC - 1:
-                    store(last, slice(2 + i, 3 + i))
+                    store(last, slice(i, i + 1))

@@ -22,7 +22,6 @@ STEP = 256
 STEPS = N // STEP
 LEAD = 4
 FUT_AHEAD = 4
-X_GROUP = 4
 
 
 def tile_tideresidualencodertemporaldecoder_t_kernel(
@@ -62,15 +61,15 @@ def tile_tideresidualencodertemporaldecoder_t_kernel(
         vp_bf = keep.tile([P, P_DEC], BF16, name="vp_bf")
         nc.vector.memset(vp_bf[:], 0.0)
         halves = [slice(0, 512), slice(512, 1024)]
-        w1_raw = load_w("w1_raw", w1, slice(0, F))
-        load_x(0, 1)
-        load_x(1, 2)
         wsk_raw, w2_raw = {}, {}
         wsk_raw[0] = load_w("wsk_raw0", wsk, halves[0])
+        load_x(0, 1)
         w2_raw[0] = load_w("w2_raw0", w2, halves[0])
+        w1_raw = load_w("w1_raw", w1, slice(0, F))
+        load_x(1, 2)
         wsk_raw[1] = load_w("wsk_raw1", wsk, halves[1])
-        load_x(3, 2)
         w2_raw[1] = load_w("w2_raw1", w2, halves[1])
+        load_x(3, 2)
         load_fut(0)
         wres_raw = load_w("wres_raw", wres, slice(0, H))
         nc.sync.dma_start(out=vp_bf[0:1, :], in_=vp.rearrange("(o q) -> o q", o=1))
@@ -125,12 +124,12 @@ def tile_tideresidualencodertemporaldecoder_t_kernel(
                         ident[:],
                     )
 
-        def empty_x(s):
+        def empty_x(s, copy=nc.scalar.copy):
             if s >= 3:
                 xg[s] = ring[(s - 1) % 2][:, 4 * STEP : 8 * STEP]
             else:
                 xg[s] = work.tile([P, 4 * STEP], BF16, name="xg", align_bytes=64)
-            nc.scalar.copy(
+            copy(
                 out=xg[s][:].bitcast(F32).rearrange("q (i p u) -> q i p u", i=2, u=2),
                 in_=xt[s][:].rearrange("q (i u p) -> q i p u", i=2, u=2),
             )
@@ -229,19 +228,10 @@ def tile_tideresidualencodertemporaldecoder_t_kernel(
 
         groups = {}
 
-        def spread(name, view, c0, engine, tag="rb", bufs=4):
+        def group_of(name, width):
             if name not in groups:
-                groups[name] = keep.tile([P, 4 * view.shape[1]], BF16, name=name + "_g", align_bytes=64)
-            bank = psum.tile([P, 2, 512], BF16, name="wbank", tag=tag, bufs=bufs)
-            for n in range(2):
-                first = c0 + P * n
-                nc.tensor.matmul(out=bank[:, n, :], lhsT=ident_bf[:], rhs=view[:, first : first + P, :], start=True, stop=True)
-            dst = groups[name][:, 4 * c0 : 4 * c0 + 1024]
-            src = bank[:].rearrange("p n c -> p (n c)")
-            if engine == "V":
-                nc.vector.tensor_copy(out=dst, in_=src)
-            else:
-                nc.scalar.copy(out=dst, in_=src)
+                groups[name] = keep.tile([P, 4 * width], BF16, name=name + "_g", align_bytes=64)
+            return groups[name]
 
         def spread_w1(half, engine):
             if "w1" not in groups:
@@ -257,54 +247,57 @@ def tile_tideresidualencodertemporaldecoder_t_kernel(
             else:
                 nc.scalar.copy(out=dst, in_=src)
 
-        def by_column(raw):
-            return raw[:].rearrange("p j c -> p c j")
+        def weave(name, raw, c0, copy, width=256):
+            dst = group_of(name, raw.shape[2])[:, 4 * c0 : 4 * (c0 + width)]
+            copy(
+                out=dst.rearrange("p (c i j) -> p c j i", i=4, j=4),
+                in_=raw[:, :, c0 : c0 + width].rearrange("p j (c i) -> p c j i", i=4),
+            )
 
         wsk_q, wsk_s, w2_q, w2_s = {}, {}, {}, {}
 
+        weave("wsk0", wsk_raw[0], 0, nc.vector.tensor_copy, 512)
+        widen(0)
+        wsk_q[0], wsk_s[0] = quantize("wsk0", groups["wsk0"][:], 1)
+        transposes(0)
+        weave("w20", w2_raw[0], 0, nc.scalar.copy)
+        empty_x(0)
         spread_w1(0, "S")
         spread_w1(1, "S")
-        widen(0)
-        transposes(0)
-        empty_x(0)
         widen(1)
-        w1_q, w1_s = quantize("w1", groups["w1"][:], 1)
         quantize_x(0)
-        for c0 in (0, 256):
-            spread("wsk0", by_column(wsk_raw[0]), c0, "S")
         transposes(1)
-        hidden(0)
         widen(2)
-        for c0 in (0, 256):
-            spread("w20", by_column(w2_raw[0]), c0, "V")
+        w1_q, w1_s = quantize("w1", groups["w1"][:], 1)
         empty_x(1)
-        relu_h(0)
-        wsk_q[0], wsk_s[0] = quantize("wsk0", groups["wsk0"][:], 1)
-        quantize_x(1)
-        w2_q[0], w2_s[0] = quantize("w20", groups["w20"][:], 1)
+        weave("w20", w2_raw[0], 256, nc.scalar.copy)
+        hidden(0)
         transposes(2)
-        for c0 in (0, 256):
-            spread("wsk1", by_column(wsk_raw[1]), c0, "S")
-        quantize_h(0)
+        weave("wsk1", wsk_raw[1], 0, nc.vector.tensor_copy, 512)
+        quantize_x(1)
+        relu_h(0)
         hidden(1)
         empty_x(2)
-        for c0 in (0, 256):
-            spread("w21", by_column(w2_raw[1]), c0, "S")
-        widen(3)
-        wsk_q[1], wsk_s[1] = quantize("wsk1", groups["wsk1"][:], 1)
-        quantize_x(2)
-        w2_q[1], w2_s[1] = quantize("w21", groups["w21"][:], 1)
+        w2_q[0], w2_s[0] = quantize("w20", groups["w20"][:], 1)
+        weave("w21", w2_raw[1], 0, nc.vector.tensor_copy)
+        quantize_h(0)
+        weave("w21", w2_raw[1], 256, nc.scalar.copy)
         relu_h(1)
         cast(LEAD)
-        for b in range(2):
-            for i in range(2):
-                main(0, i, b)
+        weave("wres", wres_raw, 0, nc.scalar.copy)
+        wsk_q[1], wsk_s[1] = quantize("wsk1", groups["wsk1"][:], 1)
+        widen(3)
+        for i in range(2):
+            main(0, i, 0)
         transposes(3)
-        spread("wres", by_column(wres_raw), 0, "S", "res", 1)
+        w2_q[1], w2_s[1] = quantize("w21", groups["w21"][:], 1)
+        quantize_x(2)
         vp_f = keep.tile([P, P_DEC], F32, name="vp_f")
         vbank = psum.tile([P, P_DEC], F32, name="vbank", tag="res", bufs=1)
         nc.tensor.matmul(out=vbank[:], lhsT=ones_bf[:], rhs=vp_bf[:], start=True, stop=True)
         nc.scalar.copy(out=vp_f[:], in_=vbank[:])
+        for i in range(2):
+            main(0, i, 1)
         quantize_h(1)
 
         for s in range(STEPS):
@@ -312,7 +305,7 @@ def tile_tideresidualencodertemporaldecoder_t_kernel(
                 load_fut(s + FUT_AHEAD)
             if s + LEAD < STEPS:
                 product(s + LEAD)
-            if s + 3 < STEPS:
+            if 0 < s < STEPS - 3:
                 empty_x(s + 3)
             if s + 2 < STEPS:
                 hidden(s + 2)
@@ -328,6 +321,7 @@ def tile_tideresidualencodertemporaldecoder_t_kernel(
             if s >= 1:
                 weigh(s - 1, 0)
             else:
+                empty_x(3, nc.vector.tensor_copy)
                 wres_q, wres_s = quantize("wres", groups["wres"][:], 1)
             skip(s)
             if s + LEAD < STEPS:

@@ -15,6 +15,7 @@ FP8 = mybir.dt.float8_e4m3fn
 FP8X4 = mybir.dt.float8_e4m3fn_x4
 ADD = mybir.AluOpType.add
 MULT = mybir.AluOpType.mult
+COPY = mybir.ActivationFunctionType.Copy
 RELU = mybir.ActivationFunctionType.Relu
 
 P = 128
@@ -91,7 +92,7 @@ def tile_tideresidualencodertemporaldecoder_t_kernel(
             nc.tensor.transpose(bank[:, c, :], scale_col[:, c : c + 1].to_broadcast([P, P]), ident[:])
         nc.scalar.copy(out=scale[:].rearrange("p (n c) -> p n c", c=4), in_=bank[:].rearrange("p c n -> p n c"))
 
-        xc, xb, xg, xq, xs, hg, hq, hs, xt, hb, rb, res, zt, acc = ({} for i in range(14))
+        xc, xb, xg, xq, xs, hg, hq, hs, xt, hb, rb, res, zt, acc, part = ({} for i in range(15))
         ring = [keep.tile([P, 8 * STEP], BF16, name=f"ring{r}", align_bytes=64) for r in range(2)]
 
         def widen(s):
@@ -223,6 +224,23 @@ def tile_tideresidualencodertemporaldecoder_t_kernel(
                 scalar=vp_f[:, p : p + 1], in1=before[:, rows, :], op0=MULT, op1=ADD,
             )
 
+        def on_tensor(s):
+            return s > 3 and (s % 2 == 0 or s > 12)
+
+        def weigh_on_tensor(s):
+            part[s] = psum.tile([P, H], F32, name="part", tag="xt", bufs=1)
+            for p in range(1, P_DEC):
+                nc.tensor.matmul(
+                    out=part[s][:], lhsT=vp_diag[:, p - 1, :], rhs=zt[s][:, 1, H * p : H * p + H],
+                    start=(p == 1), stop=(p == P_DEC - 1),
+                )
+
+        def add_part(s):
+            nc.vector.tensor_tensor(out=acc[s][:, 1, :], in0=part[s][:], in1=acc[s][:, 1, :], op=ADD)
+
+        def rows_left(s):
+            return slice(0, 1) if on_tensor(s) else slice(0, 2)
+
         def store(s, rows=slice(0, 2)):
             nc.sync.dma_start(out=out_view[:, s, rows, :], in_=acc[s][:, rows, :])
 
@@ -296,6 +314,7 @@ def tile_tideresidualencodertemporaldecoder_t_kernel(
         vbank = psum.tile([P, P_DEC], F32, name="vbank", tag="res", bufs=1)
         nc.tensor.matmul(out=vbank[:], lhsT=ones_bf[:], rhs=vp_bf[:], start=True, stop=True)
         nc.scalar.copy(out=vp_f[:], in_=vbank[:])
+        vp_diag = keep.tile([P, P_DEC - 1, P], F32, name="vp_diag")
         for i in range(2):
             main(0, i, 1)
         quantize_h(1)
@@ -305,48 +324,58 @@ def tile_tideresidualencodertemporaldecoder_t_kernel(
                 load_fut(s + FUT_AHEAD)
             if s + LEAD < STEPS:
                 product(s + LEAD)
-            if 0 < s < STEPS - 3:
-                empty_x(s + 3)
             if s + 2 < STEPS:
                 hidden(s + 2)
+            if s >= 1 and on_tensor(s - 1):
+                weigh_on_tensor(s - 1)
             if s + LEAD + 1 < STEPS:
                 cast(s + LEAD + 1)
+            n = 0
             for b in range(2):
                 for i in range(2):
                     add_fut(s, i, b)
+                    n = n + 1
+                    if n == 4 and s == 0:
+                        empty_x(3, nc.vector.tensor_copy)
+                        wres_q, wres_s = quantize("wres", groups["wres"][:], 1)
+                    if n == 4 and s >= 1 and on_tensor(s - 1):
+                        add_part(s - 1)
+                    if n == 4 and s + LEAD < STEPS:
+                        transposes(s + LEAD)
                     if s + 1 < STEPS:
                         main(s + 1, i, b)
                 if b == 0 and s + 2 < STEPS:
                     relu_h(s + 2)
-            if s >= 1:
-                weigh(s - 1, 0)
-            else:
-                empty_x(3, nc.vector.tensor_copy)
-                wres_q, wres_s = quantize("wres", groups["wres"][:], 1)
+                if b == 0 and s >= 1:
+                    weigh(s - 1, 0)
             skip(s)
-            if s + LEAD < STEPS:
-                transposes(s + LEAD)
             for b in range(2):
                 relu_z(s, b)
+            if s == 3:
+                for p in range(1, P_DEC):
+                    nc.scalar.activation(out=vp_diag[:, p - 1, :], in_=ident[:], func=COPY, scale=vp_f[:, p : p + 1])
             if s >= 2:
-                weigh(s - 2, 2)
+                weigh(s - 2, 2, rows_left(s - 2))
             if s >= 1:
-                weigh(s - 1, 1)
+                weigh(s - 1, 1, rows_left(s - 1))
             if s >= 2:
-                weigh(s - 2, 3)
+                weigh(s - 2, 3, rows_left(s - 2))
                 store(s - 2)
             if s + 3 < STEPS:
                 quantize_both(s + 2)
             elif s + 2 < STEPS:
                 quantize_h(s + 2)
+            if s + LEAD < STEPS:
+                empty_x(s + LEAD)
         last = STEPS - 1
-        weigh(last - 1, 2)
-        weigh(last, 0, slice(0, 1))
-        weigh(last - 1, 3)
+        weigh_on_tensor(last)
+        weigh(last, 0)
+        weigh(last - 1, 2, rows_left(last - 1))
+        weigh(last, 1, rows_left(last))
+        weigh(last - 1, 3, rows_left(last - 1))
         store(last - 1)
-        weigh(last, 0, slice(1, 2))
-        for p in range(1, P_DEC):
-            for i in range(2):
-                weigh(last, p, slice(i, i + 1))
-                if p == P_DEC - 1:
-                    store(last, slice(i, i + 1))
+        weigh(last, 2, rows_left(last))
+        add_part(last)
+        store(last, slice(1, 2))
+        weigh(last, 3, rows_left(last))
+        store(last, slice(0, 1))

@@ -63,11 +63,11 @@ def tile_tideresidualencodertemporaldecoder_t_kernel(
         nc.vector.memset(vp_bf[:], 0.0)
         halves = [slice(0, 512), slice(512, 1024)]
         wsk_raw, w2_raw = {}, {}
-        wsk_raw[0] = load_w("wsk_raw0", wsk, halves[0])
         load_x(0, 1)
-        w2_raw[0] = load_w("w2_raw0", w2, halves[0])
-        w1_raw = load_w("w1_raw", w1, slice(0, F))
+        wsk_raw[0] = load_w("wsk_raw0", wsk, halves[0])
         load_x(1, 2)
+        w1_raw = load_w("w1_raw", w1, slice(0, F))
+        w2_raw[0] = load_w("w2_raw0", w2, halves[0])
         wsk_raw[1] = load_w("wsk_raw1", wsk, halves[1])
         w2_raw[1] = load_w("w2_raw1", w2, halves[1])
         load_x(3, 2)
@@ -87,7 +87,7 @@ def tile_tideresidualencodertemporaldecoder_t_kernel(
         ones_bf = keep.tile([P, P], BF16, name="ones_bf")
         nc.vector.memset(ones_bf[:], 1.0)
 
-        bank = psum.tile([P, 4, P], F32, name="sbank", tag="rb", bufs=4)
+        bank = psum.tile([P, 4, P], F32, name="sbank", tag="rb", bufs=3)
         for c in range(4):
             nc.tensor.transpose(bank[:, c, :], scale_col[:, c : c + 1].to_broadcast([P, P]), ident[:])
         nc.scalar.copy(out=scale[:].rearrange("p (n c) -> p n c", c=4), in_=bank[:].rearrange("p c n -> p n c"))
@@ -167,7 +167,7 @@ def tile_tideresidualencodertemporaldecoder_t_kernel(
                     )
 
         def relu_h(s):
-            if s >= 2:
+            if s >= 1:
                 hg[s] = ring[s % 2][:, 0 : 4 * STEP]
             else:
                 hg[s] = work.tile([P, 4 * STEP], BF16, name="hg", align_bytes=64)
@@ -180,7 +180,7 @@ def tile_tideresidualencodertemporaldecoder_t_kernel(
 
         def main(s, i, b):
             cols = slice(i * P, i * P + P)
-            rb[s, i, b] = psum.tile([P, 512], F32, name="rb", bufs=4)
+            rb[s, i, b] = psum.tile([P, 512], F32, name="rb", bufs=3)
             nc.tensor.matmul_mx(
                 out=rb[s, i, b][:],
                 lhsT=xq[s][:, cols].bitcast(FP8X4), lhsT_scale=xs[s][:, cols],
@@ -227,9 +227,13 @@ def tile_tideresidualencodertemporaldecoder_t_kernel(
         def on_tensor(s):
             return s > 3 and (s % 2 == 0 or s > 12)
 
-        def weigh_on_tensor(s):
-            part[s] = psum.tile([P, H], F32, name="part", tag="xt", bufs=1)
-            for p in range(1, P_DEC):
+        def weigh_on_tensor(s, planes):
+            if s not in part:
+                if s < STEPS - 3 or s % 2 == 0:
+                    part[s] = psum.tile([P, H], F32, name="part", bufs=1)
+                else:
+                    part[s] = psum.tile([P, H], F32, name="part", tag="hb", bufs=2)
+            for p in planes:
                 nc.tensor.matmul(
                     out=part[s][:], lhsT=vp_diag[:, p - 1, :], rhs=zt[s][:, 1, H * p : H * p + H],
                     start=(p == 1), stop=(p == P_DEC - 1),
@@ -251,19 +255,24 @@ def tile_tideresidualencodertemporaldecoder_t_kernel(
                 groups[name] = keep.tile([P, 4 * width], BF16, name=name + "_g", align_bytes=64)
             return groups[name]
 
-        def spread_w1(half, engine):
-            if "w1" not in groups:
-                groups["w1"] = keep.tile([P, 4 * F], BF16, name="w1_g", align_bytes=64)
-            view = w1_raw[:].rearrange("p j (m t) -> p t m j", t=4)
-            bank = psum.tile([P, 2, 512], BF16, name="wbank", tag="rb", bufs=4)
+        banks = []
+
+        def fill_w(views, half):
+            bank = psum.tile([P, 2, 512], BF16, name="wbank", tag="rb", bufs=3)
             for n in range(2):
-                nc.tensor.matmul(out=bank[:, n, :], lhsT=ident_bf[:], rhs=view[:, 2 * half + n], start=True, stop=True)
-            dst = groups["w1"][:, 1024 * half : 1024 * half + 1024]
-            src = bank[:].rearrange("p n c -> p (n c)")
-            if engine == "V":
-                nc.vector.tensor_copy(out=dst, in_=src)
-            else:
-                nc.scalar.copy(out=dst, in_=src)
+                nc.tensor.matmul(out=bank[:, n, :], lhsT=ident_bf[:], rhs=views[:, 2 * half + n], start=True, stop=True)
+            banks.append(bank)
+
+        def empty_w(name, half):
+            dst = group_of(name, 512)[:, 1024 * half : 1024 * half + 1024]
+            nc.scalar.copy(out=dst, in_=banks[-1][:].rearrange("p n c -> p (n c)"))
+
+        def spread(name, views, half):
+            fill_w(views, half)
+            empty_w(name, half)
+
+        def in_order(raw):
+            return raw[:].rearrange("p j (t m) -> p t m j", t=4)
 
         def weave(name, raw, c0, copy, width=256):
             dst = group_of(name, raw.shape[2])[:, 4 * c0 : 4 * (c0 + width)]
@@ -274,37 +283,40 @@ def tile_tideresidualencodertemporaldecoder_t_kernel(
 
         wsk_q, wsk_s, w2_q, w2_s = {}, {}, {}, {}
 
-        weave("wsk0", wsk_raw[0], 0, nc.vector.tensor_copy, 512)
+        w1_view = w1_raw[:].rearrange("p j (m t) -> p t m j", t=4)
         widen(0)
-        wsk_q[0], wsk_s[0] = quantize("wsk0", groups["wsk0"][:], 1)
+        spread("wsk0", in_order(wsk_raw[0]), 0)
         transposes(0)
-        weave("w20", w2_raw[0], 0, nc.scalar.copy)
         empty_x(0)
-        spread_w1(0, "S")
-        spread_w1(1, "S")
+        spread("wsk0", in_order(wsk_raw[0]), 1)
         widen(1)
         quantize_x(0)
-        transposes(1)
+        spread("w1", w1_view, 0)
+        spread("w1", w1_view, 1)
         widen(2)
+        transposes(1)
+        wsk_q[0], wsk_s[0] = quantize("wsk0", groups["wsk0"][:], 1)
+        weave("w20", w2_raw[0], 0, nc.vector.tensor_copy, 512)
         w1_q, w1_s = quantize("w1", groups["w1"][:], 1)
         empty_x(1)
-        weave("w20", w2_raw[0], 256, nc.scalar.copy)
+        weave("wsk1", wsk_raw[1], 0, nc.scalar.copy)
+        fill_w(in_order(w2_raw[1]), 0)
         hidden(0)
         transposes(2)
-        weave("wsk1", wsk_raw[1], 0, nc.vector.tensor_copy, 512)
         quantize_x(1)
+        w2_q[0], w2_s[0] = quantize("w20", groups["w20"][:], 1)
         relu_h(0)
+        empty_w("w21", 0)
         hidden(1)
         empty_x(2)
-        w2_q[0], w2_s[0] = quantize("w20", groups["w20"][:], 1)
-        weave("w21", w2_raw[1], 0, nc.vector.tensor_copy)
+        weave("wsk1", wsk_raw[1], 256, nc.vector.tensor_copy)
+        widen(3)
         quantize_h(0)
-        weave("w21", w2_raw[1], 256, nc.scalar.copy)
         relu_h(1)
+        weave("w21", w2_raw[1], 256, nc.vector.tensor_copy)
+        wsk_q[1], wsk_s[1] = quantize("wsk1", groups["wsk1"][:], 1)
         cast(LEAD)
         weave("wres", wres_raw, 0, nc.scalar.copy)
-        wsk_q[1], wsk_s[1] = quantize("wsk1", groups["wsk1"][:], 1)
-        widen(3)
         for i in range(2):
             main(0, i, 0)
         transposes(3)
@@ -315,61 +327,71 @@ def tile_tideresidualencodertemporaldecoder_t_kernel(
         nc.tensor.matmul(out=vbank[:], lhsT=ones_bf[:], rhs=vp_bf[:], start=True, stop=True)
         nc.scalar.copy(out=vp_f[:], in_=vbank[:])
         vp_diag = keep.tile([P, P_DEC - 1, P], F32, name="vp_diag")
-        for i in range(2):
-            main(0, i, 1)
+        main(0, 0, 1)
         quantize_h(1)
 
         for s in range(STEPS):
+            more = s + 1 < STEPS
             if s + FUT_AHEAD < STEPS:
                 load_fut(s + FUT_AHEAD)
             if s + LEAD < STEPS:
                 product(s + LEAD)
             if s + 2 < STEPS:
                 hidden(s + 2)
-            if s >= 1 and on_tensor(s - 1):
-                weigh_on_tensor(s - 1)
+            if s + 2 < STEPS:
+                relu_h(s + 2)
             if s + LEAD + 1 < STEPS:
                 cast(s + LEAD + 1)
-            n = 0
-            for b in range(2):
-                for i in range(2):
-                    add_fut(s, i, b)
-                    n = n + 1
-                    if n == 4 and s == 0:
-                        empty_x(3, nc.vector.tensor_copy)
-                        wres_q, wres_s = quantize("wres", groups["wres"][:], 1)
-                    if n == 4 and s >= 1 and on_tensor(s - 1):
-                        add_part(s - 1)
-                    if n == 4 and s + LEAD < STEPS:
-                        transposes(s + LEAD)
-                    if s + 1 < STEPS:
-                        main(s + 1, i, b)
-                if b == 0 and s + 2 < STEPS:
-                    relu_h(s + 2)
-                if b == 0 and s >= 1:
-                    weigh(s - 1, 0)
+            add_fut(s, 0, 0)
+            main(s, 1, 1)
+            add_fut(s, 1, 0)
+            if more:
+                main(s + 1, 0, 0)
+            if s >= 1:
+                weigh(s - 1, 0)
+            if s >= 2 and on_tensor(s - 2):
+                weigh_on_tensor(s - 2, [3])
+            if s >= 1 and on_tensor(s - 1):
+                weigh_on_tensor(s - 1, [1])
+            add_fut(s, 0, 1)
+            if more:
+                main(s + 1, 1, 0)
+            add_fut(s, 1, 1)
+            if s == 0:
+                empty_x(3, nc.vector.tensor_copy)
+                wres_q, wres_s = quantize("wres", groups["wres"][:], 1)
             skip(s)
-            for b in range(2):
-                relu_z(s, b)
+            if s + LEAD < STEPS:
+                transposes(s + LEAD)
+            if more:
+                main(s + 1, 0, 1)
+            relu_z(s, 0)
+            relu_z(s, 1)
+            if s + LEAD < STEPS:
+                empty_x(s + LEAD)
             if s == 3:
                 for p in range(1, P_DEC):
                     nc.scalar.activation(out=vp_diag[:, p - 1, :], in_=ident[:], func=COPY, scale=vp_f[:, p : p + 1])
+            if s >= 1 and on_tensor(s - 1):
+                weigh_on_tensor(s - 1, [2])
             if s >= 2:
                 weigh(s - 2, 2, rows_left(s - 2))
+            if s >= 2 and on_tensor(s - 2):
+                add_part(s - 2)
             if s >= 1:
                 weigh(s - 1, 1, rows_left(s - 1))
-            if s >= 2:
-                weigh(s - 2, 3, rows_left(s - 2))
-                store(s - 2)
             if s + 3 < STEPS:
                 quantize_both(s + 2)
             elif s + 2 < STEPS:
                 quantize_h(s + 2)
-            if s + LEAD < STEPS:
-                empty_x(s + LEAD)
+            if s >= 2:
+                weigh(s - 2, 3, rows_left(s - 2))
+                store(s - 2)
         last = STEPS - 1
-        weigh_on_tensor(last)
+        weigh_on_tensor(last - 1, [3])
         weigh(last, 0)
+        add_part(last - 1)
+        weigh_on_tensor(last, [1, 2, 3])
         weigh(last - 1, 2, rows_left(last - 1))
         weigh(last, 1, rows_left(last))
         weigh(last - 1, 3, rows_left(last - 1))

@@ -22,6 +22,7 @@ P = 128
 STEP = 256
 STEPS = N // STEP
 LEAD = 4
+GFIRST = STEPS - LEAD - 1
 FUT_AHEAD = 4
 
 
@@ -180,7 +181,10 @@ def tile_tideresidualencodertemporaldecoder_t_kernel(
 
         def main(s, i, b):
             cols = slice(i * P, i * P + P)
-            rb[s, i, b] = psum.tile([P, 512], F32, name="rb", bufs=3)
+            if s > STEPS - LEAD and (i, b) == (1, 1):
+                rb[s, i, b] = psum.tile([P, 512], F32, name="rb4", tag="xt", bufs=1)
+            else:
+                rb[s, i, b] = psum.tile([P, 512], F32, name="rb", bufs=3)
             nc.tensor.matmul_mx(
                 out=rb[s, i, b][:],
                 lhsT=xq[s][:, cols].bitcast(FP8X4), lhsT_scale=xs[s][:, cols],
@@ -212,8 +216,8 @@ def tile_tideresidualencodertemporaldecoder_t_kernel(
                 out=zt[s][:, i, halves[b]], in0=rb[s, i, b][:], in1=fut_in[s][:, i, halves[b]], op=ADD
             )
 
-        def relu_z(s, b):
-            nc.scalar.activation(out=zt[s][:, :, halves[b]], in_=zt[s][:, :, halves[b]], func=RELU)
+        def relu_z(s, rows, b):
+            nc.scalar.activation(out=zt[s][:, rows, halves[b]], in_=zt[s][:, rows, halves[b]], func=RELU)
 
         def weigh(s, p, rows=slice(0, 2)):
             if s not in acc:
@@ -225,7 +229,7 @@ def tile_tideresidualencodertemporaldecoder_t_kernel(
             )
 
         def on_tensor(s):
-            return s > 3 and (s % 2 == 0 or s > 12)
+            return 1 < s < STEPS - 1 and (s % 2 == 0 or s > 12)
 
         def weigh_on_tensor(s, planes):
             if s not in part:
@@ -242,8 +246,31 @@ def tile_tideresidualencodertemporaldecoder_t_kernel(
         def add_part(s):
             nc.vector.tensor_tensor(out=acc[s][:, 1, :], in0=part[s][:], in1=acc[s][:, 1, :], op=ADD)
 
+        def on_gpsimd(s):
+            return GFIRST <= s < STEPS - 2
+
         def rows_left(s):
-            return slice(0, 1) if on_tensor(s) else slice(0, 2)
+            return slice(1 if on_gpsimd(s) else 0, 1 if on_tensor(s) else 2)
+
+        def weigh_left(s, p):
+            rows = rows_left(s)
+            if rows.start < rows.stop:
+                weigh(s, p, rows)
+
+        def scale_planes(s):
+            for p in (1, 2, 3):
+                plane = zt[s][:, 0, H * p : H * p + H]
+                nc.scalar.activation(out=plane, in_=plane, func=COPY, scale=vp_f[:, p : p + 1])
+
+        def sum_on_gpsimd(s):
+            total = zt[s][:, 0, H : 2 * H]
+            for p in (2, 3):
+                nc.gpsimd.tensor_tensor(out=total, in0=total, in1=zt[s][:, 0, H * p : H * p + H], op=ADD)
+                if p == 2 and on_gpsimd(s - 1):
+                    add_sum(s - 1)
+
+        def add_sum(s):
+            nc.gpsimd.tensor_tensor(out=acc[s][:, 0, :], in0=acc[s][:, 0, :], in1=zt[s][:, 0, H : 2 * H], op=ADD)
 
         def store(s, rows=slice(0, 2)):
             nc.sync.dma_start(out=out_view[:, s, rows, :], in_=acc[s][:, rows, :])
@@ -343,14 +370,21 @@ def tile_tideresidualencodertemporaldecoder_t_kernel(
             if s + LEAD + 1 < STEPS:
                 cast(s + LEAD + 1)
             add_fut(s, 0, 0)
-            main(s, 1, 1)
+            if s <= STEPS - LEAD:
+                main(s, 1, 1)
             add_fut(s, 1, 0)
             if more:
                 main(s + 1, 0, 0)
             if s >= 1:
                 weigh(s - 1, 0)
+                if on_gpsimd(s - 1):
+                    sum_on_gpsimd(s - 1)
+                elif on_gpsimd(s - 2):
+                    add_sum(s - 2)
             if s >= 2 and on_tensor(s - 2):
                 weigh_on_tensor(s - 2, [3])
+            if not more:
+                skip(s)
             if s >= 1 and on_tensor(s - 1):
                 weigh_on_tensor(s - 1, [1])
             add_fut(s, 0, 1)
@@ -360,44 +394,54 @@ def tile_tideresidualencodertemporaldecoder_t_kernel(
             if s == 0:
                 empty_x(3, nc.vector.tensor_copy)
                 wres_q, wres_s = quantize("wres", groups["wres"][:], 1)
-            skip(s)
+            if more:
+                skip(s)
             if s + LEAD < STEPS:
                 transposes(s + LEAD)
             if more:
                 main(s + 1, 0, 1)
-            relu_z(s, 0)
-            relu_z(s, 1)
+                if s + 1 > STEPS - LEAD:
+                    main(s + 1, 1, 1)
+            if more:
+                relu_z(s, slice(0, 2), 0)
+                relu_z(s, slice(0, 2), 1)
+            else:
+                for b in range(2):
+                    for i in range(2):
+                        relu_z(s, slice(i, i + 1), b)
+            if on_gpsimd(s):
+                scale_planes(s)
             if s + LEAD < STEPS:
                 empty_x(s + LEAD)
-            if s == 3:
+            if s == 1:
                 for p in range(1, P_DEC):
                     nc.scalar.activation(out=vp_diag[:, p - 1, :], in_=ident[:], func=COPY, scale=vp_f[:, p : p + 1])
             if s >= 1 and on_tensor(s - 1):
                 weigh_on_tensor(s - 1, [2])
             if s >= 2:
-                weigh(s - 2, 2, rows_left(s - 2))
+                weigh_left(s - 2, 2)
+            if s >= 1:
+                weigh_left(s - 1, 1)
             if s >= 2 and on_tensor(s - 2):
                 add_part(s - 2)
-            if s >= 1:
-                weigh(s - 1, 1, rows_left(s - 1))
             if s + 3 < STEPS:
                 quantize_both(s + 2)
             elif s + 2 < STEPS:
                 quantize_h(s + 2)
             if s >= 2:
-                weigh(s - 2, 3, rows_left(s - 2))
+                weigh_left(s - 2, 3)
                 store(s - 2)
         last = STEPS - 1
         weigh_on_tensor(last - 1, [3])
         weigh(last, 0)
+        weigh_left(last - 1, 2)
+        weigh(last, 1, slice(0, 1))
+        weigh_left(last - 1, 3)
+        weigh(last, 1, slice(1, 2))
         add_part(last - 1)
-        weigh_on_tensor(last, [1, 2, 3])
-        weigh(last - 1, 2, rows_left(last - 1))
-        weigh(last, 1, rows_left(last))
-        weigh(last - 1, 3, rows_left(last - 1))
         store(last - 1)
-        weigh(last, 2, rows_left(last))
-        add_part(last)
-        store(last, slice(1, 2))
-        weigh(last, 3, rows_left(last))
-        store(last, slice(0, 1))
+        for p in range(2, P_DEC):
+            for i in range(2):
+                weigh(last, p, slice(i, i + 1))
+                if p == P_DEC - 1:
+                    store(last, slice(i, i + 1))

@@ -65,13 +65,13 @@ def tile_tideresidualencodertemporaldecoder_t_kernel(
         halves = [slice(0, 512), slice(512, 1024)]
         wsk_raw, w2_raw = {}, {}
         load_x(0, 1)
-        wsk_raw[0] = load_w("wsk_raw0", wsk, halves[0])
-        load_x(1, 2)
         w1_raw = load_w("w1_raw", w1, slice(0, F))
-        w2_raw[0] = load_w("w2_raw0", w2, halves[0])
+        load_x(1, 2)
         wsk_raw[1] = load_w("wsk_raw1", wsk, halves[1])
-        w2_raw[1] = load_w("w2_raw1", w2, halves[1])
+        wsk_raw[0] = load_w("wsk_raw0", wsk, halves[0])
+        w2_raw[0] = load_w("w2_raw0", w2, halves[0])
         load_x(3, 2)
+        w2_raw[1] = load_w("w2_raw1", w2, halves[1])
         load_fut(0)
         wres_raw = load_w("wres_raw", wres, slice(0, H))
         nc.sync.dma_start(out=vp_bf[0:1, :], in_=vp.rearrange("(o q) -> o q", o=1))
@@ -92,6 +92,9 @@ def tile_tideresidualencodertemporaldecoder_t_kernel(
         for c in range(4):
             nc.tensor.transpose(bank[:, c, :], scale_col[:, c : c + 1].to_broadcast([P, P]), ident[:])
         nc.scalar.copy(out=scale[:].rearrange("p (n c) -> p n c", c=4), in_=bank[:].rearrange("p c n -> p n c"))
+        scale_sorted = keep.tile([P, 2, 2, P, 2], F32, name="scale_sorted")
+        for i in range(2):
+            nc.scalar.copy(out=scale_sorted[:, :, i], in_=bank[:].rearrange("p (u e) m -> p u m e", u=2))
 
         xc, xb, xg, xq, xs, hg, hq, hs, xt, hb, rb, res, zt, acc, part = ({} for i in range(15))
         ring = [keep.tile([P, 8 * STEP], BF16, name=f"ring{r}", align_bytes=64) for r in range(2)]
@@ -109,9 +112,9 @@ def tile_tideresidualencodertemporaldecoder_t_kernel(
         def product(s):
             xb[s] = ring[(s - 3) % 2][:, 0 : 2 * L]
             nc.gpsimd.tensor_tensor(
-                out=xb[s].rearrange("p (i k) -> p i k", i=2),
-                in0=xc[s][:].rearrange("p (i k) -> p i k", i=2),
-                in1=scale[:].unsqueeze(1).to_broadcast([P, 2, L]),
+                out=xb[s].rearrange("p (u m e) -> p u m e", u=2, e=2),
+                in0=xc[s][:].rearrange("p (m u e) -> p u m e", u=2, e=2),
+                in1=scale_sorted[:].rearrange("p u i m e -> p u (i m) e"),
                 op=MULT,
             )
 
@@ -122,7 +125,7 @@ def tile_tideresidualencodertemporaldecoder_t_kernel(
                 for u in range(2):
                     nc.tensor.transpose(
                         xt[s][:, (2 * i + u) * P : (2 * i + u + 1) * P],
-                        words[:, 256 * i + u : 256 * (i + 1) : 2],
+                        words[:, 256 * i + u : 256 * (i + 1) : 2] if s < LEAD else words[:, 256 * u + P * i : 256 * u + P * i + P],
                         ident[:],
                     )
 
@@ -312,49 +315,50 @@ def tile_tideresidualencodertemporaldecoder_t_kernel(
 
         w1_view = w1_raw[:].rearrange("p j (m t) -> p t m j", t=4)
         widen(0)
-        spread("wsk0", in_order(wsk_raw[0]), 0)
+        spread("w1", w1_view, 0)
         transposes(0)
         empty_x(0)
-        spread("wsk0", in_order(wsk_raw[0]), 1)
-        widen(1)
-        quantize_x(0)
-        spread("w1", w1_view, 0)
+        weave("wsk1", wsk_raw[1], 0, nc.scalar.copy, 128)
         spread("w1", w1_view, 1)
-        widen(2)
+        widen(1)
         transposes(1)
-        wsk_q[0], wsk_s[0] = quantize("wsk0", groups["wsk0"][:], 1)
-        weave("w20", w2_raw[0], 0, nc.vector.tensor_copy, 512)
+        widen(2)
+        quantize_x(0)
         w1_q, w1_s = quantize("w1", groups["w1"][:], 1)
         empty_x(1)
-        weave("wsk1", wsk_raw[1], 0, nc.scalar.copy)
-        fill_w(in_order(w2_raw[1]), 0)
+        weave("wsk1", wsk_raw[1], 128, nc.scalar.copy, 256)
+        fill_w(in_order(wsk_raw[0]), 0)
         hidden(0)
-        transposes(2)
-        quantize_x(1)
-        w2_q[0], w2_s[0] = quantize("w20", groups["w20"][:], 1)
         relu_h(0)
-        empty_w("w21", 0)
+        empty_w("wsk0", 0)
+        spread("wsk0", in_order(wsk_raw[0]), 1)
+        quantize_x(1)
+        transposes(2)
+        weave("w20", w2_raw[0], 0, nc.vector.tensor_copy, 512)
         hidden(1)
         empty_x(2)
-        weave("wsk1", wsk_raw[1], 256, nc.vector.tensor_copy)
         widen(3)
         quantize_h(0)
+        w2_q[0], w2_s[0] = quantize("w20", groups["w20"][:], 1)
+        wsk_q[0], wsk_s[0] = quantize("wsk0", groups["wsk0"][:], 1)
+        weave("wsk1", wsk_raw[1], 384, nc.scalar.copy, 128)
+        spread("w21", in_order(w2_raw[1]), 0)
         relu_h(1)
         weave("w21", w2_raw[1], 256, nc.vector.tensor_copy)
+        quantize_x(2)
         wsk_q[1], wsk_s[1] = quantize("wsk1", groups["wsk1"][:], 1)
+        w2_q[1], w2_s[1] = quantize("w21", groups["w21"][:], 1)
         cast(LEAD)
         weave("wres", wres_raw, 0, nc.scalar.copy)
+        transposes(3)
         for i in range(2):
             main(0, i, 0)
-        transposes(3)
-        w2_q[1], w2_s[1] = quantize("w21", groups["w21"][:], 1)
-        quantize_x(2)
+        main(0, 0, 1)
         vp_f = keep.tile([P, P_DEC], F32, name="vp_f")
         vbank = psum.tile([P, P_DEC], F32, name="vbank", tag="res", bufs=1)
         nc.tensor.matmul(out=vbank[:], lhsT=ones_bf[:], rhs=vp_bf[:], start=True, stop=True)
         nc.scalar.copy(out=vp_f[:], in_=vbank[:])
         vp_diag = keep.tile([P, P_DEC - 1, P], F32, name="vp_diag")
-        main(0, 0, 1)
         quantize_h(1)
 
         for s in range(STEPS):
@@ -394,12 +398,14 @@ def tile_tideresidualencodertemporaldecoder_t_kernel(
             if s == 0:
                 empty_x(3, nc.vector.tensor_copy)
                 wres_q, wres_s = quantize("wres", groups["wres"][:], 1)
-            if more:
+            if more and s > 0:
                 skip(s)
             if s + LEAD < STEPS:
                 transposes(s + LEAD)
             if more:
                 main(s + 1, 0, 1)
+                if s == 0:
+                    skip(s)
                 if s + 1 > STEPS - LEAD:
                     main(s + 1, 1, 1)
             if more:

@@ -55,28 +55,26 @@ def tile_tideresidualencodertemporaldecoder_t_kernel(
         def load_w(name, w, cols):
             t = keep.tile([P, 4, cols.stop - cols.start], BF16, name=name)
             nc.sync.dma_start(out=t[:], in_=w.rearrange("(p j) c -> p j c", j=4)[:, :, cols])
-            return t
+            return t[:]
 
-        scale = keep.tile([P, L], F32, name="scale")
         scale_col = keep.tile([P, 4], F32, name="scale_col")
         nc.scalar.dma_start(out=scale_col[:], in_=x_scale.rearrange("o (n c) -> (o n) c", c=4))
         vp_bf = keep.tile([P, P_DEC], BF16, name="vp_bf")
-        nc.vector.memset(vp_bf[:], 0.0)
+        nc.scalar.dma_start(out=vp_bf[:], in_=vp.partition_broadcast(P))
         halves = [slice(0, 512), slice(512, 1024)]
         wsk_raw, w2_raw = {}, {}
         load_x(0, 1)
         w1_raw = load_w("w1_raw", w1, slice(0, F))
-        load_x(1, 2)
-        wsk_raw[1] = load_w("wsk_raw1", wsk, halves[1])
-        wsk_raw[0] = load_w("wsk_raw0", wsk, halves[0])
+        load_x(1, 3)
+        wsk_all = load_w("wsk_raw", wsk, slice(0, PH))
+        wsk_raw = [wsk_all[:, :, b] for b in halves]
         w2_raw[0] = load_w("w2_raw0", w2, halves[0])
-        load_x(3, 2)
         w2_raw[1] = load_w("w2_raw1", w2, halves[1])
         load_fut(0)
+        load_x(4, 2)
         wres_raw = load_w("wres_raw", wres, slice(0, H))
-        nc.sync.dma_start(out=vp_bf[0:1, :], in_=vp.rearrange("(o q) -> o q", o=1))
         load_fut(1)
-        load_x(5, 5)
+        load_x(6, 4)
         load_fut(2)
         load_fut(3)
         load_x(10, 6)
@@ -85,58 +83,62 @@ def tile_tideresidualencodertemporaldecoder_t_kernel(
         make_identity(nc, ident[:])
         ident_bf = keep.tile([P, P], BF16, name="ident_bf")
         nc.scalar.activation(out=ident_bf[:], in_=ident[:], func=RELU)
-        ones_bf = keep.tile([P, P], BF16, name="ones_bf")
-        nc.vector.memset(ones_bf[:], 1.0)
 
-        bank = psum.tile([P, 4, P], F32, name="sbank", tag="rb", bufs=3)
+        bank = psum.tile([P, 4, P], F32, name="sbank", tag="res", bufs=1)
         for c in range(4):
             nc.tensor.transpose(bank[:, c, :], scale_col[:, c : c + 1].to_broadcast([P, P]), ident[:])
-        nc.scalar.copy(out=scale[:].rearrange("p (n c) -> p n c", c=4), in_=bank[:].rearrange("p c n -> p n c"))
-        scale_sorted = keep.tile([P, 2, 2, P, 2], F32, name="scale_sorted")
-        for i in range(2):
-            nc.scalar.copy(out=scale_sorted[:, :, i], in_=bank[:].rearrange("p (u e) m -> p u m e", u=2))
+        scale_sorted = keep.tile([P, L], F32, name="scale_sorted")
 
         xc, xb, xg, xq, xs, hg, hq, hs, xt, hb, rb, res, zt, acc, part = ({} for i in range(15))
         ring = [keep.tile([P, 8 * STEP], BF16, name=f"ring{r}", align_bytes=64) for r in range(2)]
 
-        def widen(s):
-            xb[s] = work.tile([P, 2 * L], BF16, name="xb", bufs=LEAD, align_bytes=64)
-            for i in range(2):
-                cols = slice(L * i, L * i + L)
-                nc.vector.tensor_tensor(out=xb[s][:, cols], in0=x_in[s][:, cols], in1=scale[:], op=MULT)
-
         def cast(s):
-            xc[s] = work.tile([P, 2 * L], BF16, name="xc")
+            xc[s] = work.tile([P, 2 * L], BF16, name="xc", bufs=4)
             nc.scalar.copy(out=xc[s][:], in_=x_in[s])
 
-        def product(s):
-            xb[s] = ring[(s - 3) % 2][:, 0 : 2 * L]
+        def product(s, home=None):
+            xb[s] = ring[(s - 3) % 2][:, 0 : 2 * L] if home is None else home
             nc.gpsimd.tensor_tensor(
-                out=xb[s].rearrange("p (u m e) -> p u m e", u=2, e=2),
-                in0=xc[s][:].rearrange("p (m u e) -> p u m e", u=2, e=2),
-                in1=scale_sorted[:].rearrange("p u i m e -> p u (i m) e"),
+                out=xb[s].rearrange("p (u i m e) -> p u i m e", u=2, i=2, e=2),
+                in0=xc[s][:].rearrange("p (i m u e) -> p u i m e", i=2, u=2, e=2),
+                in1=scale_sorted[:].rearrange("p (u o m e) -> p u o m e", u=2, o=1, e=2).to_broadcast([P, 2, 2, P, 2]),
                 op=MULT,
             )
 
-        def transposes(s):
-            xt[s] = psum.tile([P, 512], F32, name="xt", bufs=1)
-            words = xb[s][:].bitcast(F32)
-            for i in range(2):
-                for u in range(2):
+        def transposes(s, tag="xt", bufs=1):
+            xt[s] = psum.tile([P, 512], F32, name="xt", tag=tag, bufs=bufs)
+            words = (xb[s] if s in xb else xc[s][:]).bitcast(F32)
+            for u in range(2):
+                for i in range(2):
+                    at = (2 * u + i) * P
                     nc.tensor.transpose(
-                        xt[s][:, (2 * i + u) * P : (2 * i + u + 1) * P],
-                        words[:, 256 * i + u : 256 * (i + 1) : 2] if s < LEAD else words[:, 256 * u + P * i : 256 * u + P * i + P],
+                        xt[s][:, at : at + P],
+                        words[:, at : at + P] if s in xb else words[:, 256 * i + u : 256 * (i + 1) : 2],
                         ident[:],
                     )
 
-        def empty_x(s, copy=nc.scalar.copy):
+        def x_home(s):
             if s >= 3:
                 xg[s] = ring[(s - 1) % 2][:, 4 * STEP : 8 * STEP]
+            elif s == 0:
+                xg[s] = group_of("wsk1")[:, 0 : 4 * STEP]
             else:
-                xg[s] = work.tile([P, 4 * STEP], BF16, name="xg", align_bytes=64)
-            copy(
-                out=xg[s][:].bitcast(F32).rearrange("q (i p u) -> q i p u", i=2, u=2),
-                in_=xt[s][:].rearrange("q (i u p) -> q i p u", i=2, u=2),
+                xg[s] = work.tile([P, 4 * STEP], BF16, name="xg", bufs=3, align_bytes=64)[:]
+
+        def empty_x(s):
+            x_home(s)
+            nc.scalar.copy(
+                out=xg[s].bitcast(F32).rearrange("q (n u) -> q n u", u=2),
+                in_=xt[s][:].rearrange("q (u n) -> q n u", u=2),
+            )
+
+        def scale_x(s):
+            x_home(s)
+            nc.vector.tensor_tensor(
+                out=xg[s].rearrange("q (n u e) -> q n u e", u=2, e=2),
+                in0=xt[s][:].bitcast(BF16).rearrange("q (u n e) -> q n u e", u=2, e=2),
+                in1=scale_col[:].rearrange("q (o u e) -> q o u e", o=1, u=2).to_broadcast([P, STEP, 2, 2]),
+                op=MULT,
             )
 
         def quantize(name, source, bufs):
@@ -147,7 +149,7 @@ def tile_tideresidualencodertemporaldecoder_t_kernel(
             return codes, scales
 
         def quantize_x(s):
-            xq[s], xs[s] = quantize("x", xg[s][:], 3)
+            xq[s], xs[s] = quantize("x", xg[s], 3)
 
         def quantize_h(s):
             hq[s], hs[s] = quantize("h", hg[s][:], 3)
@@ -280,32 +282,31 @@ def tile_tideresidualencodertemporaldecoder_t_kernel(
 
         groups = {}
 
-        def group_of(name, width):
+        def group_of(name, width=512):
             if name not in groups:
                 groups[name] = keep.tile([P, 4 * width], BF16, name=name + "_g", align_bytes=64)
             return groups[name]
 
-        banks = []
+        banks = {}
 
-        def fill_w(views, half):
-            bank = psum.tile([P, 2, 512], BF16, name="wbank", tag="rb", bufs=3)
+        def fill_w(name, raw, half, order="p j (t m) -> p t m j"):
+            views = raw.rearrange(order, t=4)
+            banks[name, half] = psum.tile([P, 2, 512], BF16, name="wbank", tag="rb", bufs=3)
             for n in range(2):
-                nc.tensor.matmul(out=bank[:, n, :], lhsT=ident_bf[:], rhs=views[:, 2 * half + n], start=True, stop=True)
-            banks.append(bank)
+                nc.tensor.matmul(out=banks[name, half][:, n, :], lhsT=ident_bf[:], rhs=views[:, 2 * half + n], start=True, stop=True)
 
-        def empty_w(name, half):
-            dst = group_of(name, 512)[:, 1024 * half : 1024 * half + 1024]
-            nc.scalar.copy(out=dst, in_=banks[-1][:].rearrange("p n c -> p (n c)"))
+        def empty_w(name, half, copy=nc.scalar.copy):
+            dst = group_of(name)[:, 1024 * half : 1024 * half + 1024]
+            copy(out=dst, in_=banks[name, half][:].rearrange("p n c -> p (n c)"))
 
-        def spread(name, views, half):
-            fill_w(views, half)
-            empty_w(name, half)
+        def copy_on_gpsimd(out, in_):
+            nc.gpsimd.tensor_scalar(out=out, in0=in_, scalar1=1.0, scalar2=0.0, op0=MULT, op1=ADD)
 
-        def in_order(raw):
-            return raw[:].rearrange("p j (t m) -> p t m j", t=4)
-
-        def weave(name, raw, c0, copy, width=256):
+        def weave(name, raw, c0, width, copy):
             dst = group_of(name, raw.shape[2])[:, 4 * c0 : 4 * (c0 + width)]
+            if copy is copy_on_gpsimd:
+                copy(out=dst.rearrange("p (c j) -> p c j", j=4), in_=raw[:, :, c0 : c0 + width].rearrange("p j c -> p c j"))
+                return
             copy(
                 out=dst.rearrange("p (c i j) -> p c j i", i=4, j=4),
                 in_=raw[:, :, c0 : c0 + width].rearrange("p j (c i) -> p c j i", i=4),
@@ -313,53 +314,59 @@ def tile_tideresidualencodertemporaldecoder_t_kernel(
 
         wsk_q, wsk_s, w2_q, w2_s = {}, {}, {}, {}
 
-        w1_view = w1_raw[:].rearrange("p j (m t) -> p t m j", t=4)
-        widen(0)
-        spread("w1", w1_view, 0)
+        cast(0)
         transposes(0)
-        empty_x(0)
-        weave("wsk1", wsk_raw[1], 0, nc.scalar.copy, 128)
-        spread("w1", w1_view, 1)
-        widen(1)
-        transposes(1)
-        widen(2)
-        quantize_x(0)
-        w1_q, w1_s = quantize("w1", groups["w1"][:], 1)
-        empty_x(1)
-        weave("wsk1", wsk_raw[1], 128, nc.scalar.copy, 256)
-        fill_w(in_order(wsk_raw[0]), 0)
-        hidden(0)
-        relu_h(0)
-        empty_w("wsk0", 0)
-        spread("wsk0", in_order(wsk_raw[0]), 1)
-        quantize_x(1)
-        transposes(2)
-        weave("w20", w2_raw[0], 0, nc.vector.tensor_copy, 512)
-        hidden(1)
-        empty_x(2)
-        widen(3)
-        quantize_h(0)
-        w2_q[0], w2_s[0] = quantize("w20", groups["w20"][:], 1)
-        wsk_q[0], wsk_s[0] = quantize("wsk0", groups["wsk0"][:], 1)
-        weave("wsk1", wsk_raw[1], 384, nc.scalar.copy, 128)
-        spread("w21", in_order(w2_raw[1]), 0)
-        relu_h(1)
-        weave("w21", w2_raw[1], 256, nc.vector.tensor_copy)
-        quantize_x(2)
-        wsk_q[1], wsk_s[1] = quantize("wsk1", groups["wsk1"][:], 1)
-        w2_q[1], w2_s[1] = quantize("w21", groups["w21"][:], 1)
-        cast(LEAD)
-        weave("wres", wres_raw, 0, nc.scalar.copy)
-        transposes(3)
-        for i in range(2):
-            main(0, i, 0)
-        main(0, 0, 1)
+        nc.scalar.copy(
+            out=scale_sorted[:].rearrange("p (u m e) -> p u m e", u=2, e=2), in_=bank[:].rearrange("p (u e) m -> p u m e", u=2)
+        )
         vp_f = keep.tile([P, P_DEC], F32, name="vp_f")
-        vbank = psum.tile([P, P_DEC], F32, name="vbank", tag="res", bufs=1)
-        nc.tensor.matmul(out=vbank[:], lhsT=ones_bf[:], rhs=vp_bf[:], start=True, stop=True)
-        nc.scalar.copy(out=vp_f[:], in_=vbank[:])
+        nc.scalar.copy(out=vp_f[:], in_=vp_bf[:])
         vp_diag = keep.tile([P, P_DEC - 1, P], F32, name="vp_diag")
+        for p in range(1, P_DEC):
+            nc.scalar.activation(out=vp_diag[:, p - 1, :], in_=ident[:], func=COPY, scale=vp_f[:, p : p + 1])
+        nc.vector.tensor_copy(
+            out=group_of("w1")[:].rearrange("p (t m j) -> p t m j", t=4, j=4),
+            in_=w1_raw.rearrange("p j (m t) -> p t m j", t=4),
+        )
+        cast(1)
+        transposes(1, "part")
+        cast(2)
+        transposes(2, "res")
+        cast(3)
+        scale_x(0)
+        transposes(3)
+        w1_q, w1_s = quantize("w1", groups["w1"][:], 1)
+        quantize_x(0)
+        hidden(0)
+        weave("wsk1", wsk_raw[1], 0, 512, copy_on_gpsimd)
+        weave("wsk0", wsk_raw[0], 0, 512, nc.scalar.copy)
+        scale_x(1)
+        scale_x(2)
+        scale_x(3)
+        relu_h(0)
+        fill_w("w20", w2_raw[0], 0)
+        fill_w("w20", w2_raw[0], 1)
+        quantize_x(1)
+        quantize_x(2)
+        hidden(1)
+        quantize_h(0)
+        empty_w("w20", 0)
+        empty_w("w20", 1)
+        fill_w("w21", w2_raw[1], 0)
+        wsk_q[0], wsk_s[0] = quantize("wsk0", groups["wsk0"][:], 1)
+        wsk_q[1], wsk_s[1] = quantize("wsk1", groups["wsk1"][:], 1)
+        w2_q[0], w2_s[0] = quantize("w20", groups["w20"][:], 1)
+        weave("w21", w2_raw[1], 256, 256, nc.vector.tensor_copy)
+        relu_h(1)
+        empty_w("w21", 0)
+        cast(4)
         quantize_h(1)
+        w2_q[1], w2_s[1] = quantize("w21", groups["w21"][:], 1)
+        weave("wres", wres_raw, 0, 256, nc.scalar.copy)
+        main(0, 0, 0)
+        main(0, 1, 0)
+        hidden(2)
+        main(0, 0, 1)
 
         for s in range(STEPS):
             more = s + 1 < STEPS
@@ -367,7 +374,7 @@ def tile_tideresidualencodertemporaldecoder_t_kernel(
                 load_fut(s + FUT_AHEAD)
             if s + LEAD < STEPS:
                 product(s + LEAD)
-            if s + 2 < STEPS:
+            if 2 < s + 2 < STEPS:
                 hidden(s + 2)
             if s + 2 < STEPS:
                 relu_h(s + 2)
@@ -396,7 +403,6 @@ def tile_tideresidualencodertemporaldecoder_t_kernel(
                 main(s + 1, 1, 0)
             add_fut(s, 1, 1)
             if s == 0:
-                empty_x(3, nc.vector.tensor_copy)
                 wres_q, wres_s = quantize("wres", groups["wres"][:], 1)
             if more and s > 0:
                 skip(s)
@@ -419,9 +425,6 @@ def tile_tideresidualencodertemporaldecoder_t_kernel(
                 scale_planes(s)
             if s + LEAD < STEPS:
                 empty_x(s + LEAD)
-            if s == 1:
-                for p in range(1, P_DEC):
-                    nc.scalar.activation(out=vp_diag[:, p - 1, :], in_=ident[:], func=COPY, scale=vp_f[:, p : p + 1])
             if s >= 1 and on_tensor(s - 1):
                 weigh_on_tensor(s - 1, [2])
             if s >= 2:

@@ -60,7 +60,8 @@ def tile_tideresidualencodertemporaldecoder_t_kernel(
         scale_col = keep.tile([P, 4], F32, name="scale_col")
         nc.scalar.dma_start(out=scale_col[:], in_=x_scale.rearrange("o (n c) -> (o n) c", c=4))
         vp_bf = keep.tile([P, P_DEC], BF16, name="vp_bf")
-        nc.scalar.dma_start(out=vp_bf[:], in_=vp.partition_broadcast(P))
+        nc.vector.memset(vp_bf[:], 0.0)
+        nc.scalar.dma_start(out=vp_bf[0:1, :], in_=vp.rearrange("(o q) -> o q", o=1))
         halves = [slice(0, 512), slice(512, 1024)]
         wsk_raw, w2_raw = {}, {}
         load_x(0, 1)
@@ -83,6 +84,8 @@ def tile_tideresidualencodertemporaldecoder_t_kernel(
         make_identity(nc, ident[:])
         ident_bf = keep.tile([P, P], BF16, name="ident_bf")
         nc.scalar.activation(out=ident_bf[:], in_=ident[:], func=RELU)
+        ones_bf = keep.tile([P, P], BF16, name="ones_bf")
+        nc.vector.memset(ones_bf[:], 1.0)
 
         bank = psum.tile([P, 4, P], F32, name="sbank", tag="res", bufs=1)
         for c in range(4):
@@ -111,11 +114,11 @@ def tile_tideresidualencodertemporaldecoder_t_kernel(
             for u in range(2):
                 for i in range(2):
                     at = (2 * u + i) * P
-                    nc.tensor.transpose(
-                        xt[s][:, at : at + P],
-                        words[:, at : at + P] if s in xb else words[:, 256 * i + u : 256 * (i + 1) : 2],
-                        ident[:],
-                    )
+                    if s in xb:
+                        nc.tensor.transpose(xt[s][:, at : at + P], words[:, at : at + P], ident[:])
+                    else:
+                        second = slice(256 * i + u, 256 * (i + 1), 2)
+                        nc.tensor.transpose(xt[s][:, second], words[:, second], ident[:])
 
         def x_home(s):
             if s >= 3:
@@ -135,9 +138,9 @@ def tile_tideresidualencodertemporaldecoder_t_kernel(
         def scale_x(s):
             x_home(s)
             nc.vector.tensor_tensor(
-                out=xg[s].rearrange("q (n u e) -> q n u e", u=2, e=2),
-                in0=xt[s][:].bitcast(BF16).rearrange("q (u n e) -> q n u e", u=2, e=2),
-                in1=scale_col[:].rearrange("q (o u e) -> q o u e", o=1, u=2).to_broadcast([P, STEP, 2, 2]),
+                out=xg[s].rearrange("q (n t) -> q n t", t=4),
+                in0=xt[s][:].bitcast(BF16).rearrange("q (n t) -> q n t", t=4),
+                in1=scale_col[:].rearrange("q (o t) -> q o t", o=1).to_broadcast([P, STEP, 4]),
                 op=MULT,
             )
 
@@ -314,13 +317,15 @@ def tile_tideresidualencodertemporaldecoder_t_kernel(
 
         wsk_q, wsk_s, w2_q, w2_s = {}, {}, {}, {}
 
+        vp_f = keep.tile([P, P_DEC], F32, name="vp_f")
+        vbank = psum.tile([P, P_DEC], F32, name="vbank", tag="hb", bufs=2)
+        nc.tensor.matmul(out=vbank[:], lhsT=ones_bf[:], rhs=vp_bf[:], start=True, stop=True)
         cast(0)
         transposes(0)
         nc.scalar.copy(
             out=scale_sorted[:].rearrange("p (u m e) -> p u m e", u=2, e=2), in_=bank[:].rearrange("p (u e) m -> p u m e", u=2)
         )
-        vp_f = keep.tile([P, P_DEC], F32, name="vp_f")
-        nc.scalar.copy(out=vp_f[:], in_=vp_bf[:])
+        nc.scalar.copy(out=vp_f[:], in_=vbank[:])
         vp_diag = keep.tile([P, P_DEC - 1, P], F32, name="vp_diag")
         for p in range(1, P_DEC):
             nc.scalar.activation(out=vp_diag[:, p - 1, :], in_=ident[:], func=COPY, scale=vp_f[:, p : p + 1])

@@ -66,16 +66,15 @@ def tile_tideresidualencodertemporaldecoder_t_kernel(
         wsk_raw, w2_raw = {}, {}
         load_x(0, 1)
         w1_raw = load_w("w1_raw", w1, slice(0, F))
-        load_x(1, 3)
+        load_x(1, 4)
         wsk_all = load_w("wsk_raw", wsk, slice(0, PH))
         wsk_raw = [wsk_all[:, :, b] for b in halves]
         w2_raw[0] = load_w("w2_raw0", w2, halves[0])
         w2_raw[1] = load_w("w2_raw1", w2, halves[1])
         load_fut(0)
-        load_x(4, 2)
         wres_raw = load_w("wres_raw", wres, slice(0, H))
+        load_x(5, 5)
         load_fut(1)
-        load_x(6, 4)
         load_fut(2)
         load_fut(3)
         load_x(10, 6)
@@ -92,11 +91,11 @@ def tile_tideresidualencodertemporaldecoder_t_kernel(
             nc.tensor.transpose(bank[:, c, :], scale_col[:, c : c + 1].to_broadcast([P, P]), ident[:])
         scale_sorted = keep.tile([P, L], F32, name="scale_sorted")
 
-        xc, xb, xg, xq, xs, hg, hq, hs, xt, hb, rb, res, zt, acc, part = ({} for i in range(15))
+        xc, xb, xg, xq, xs, hg, hq, hs, xt, hb, rb, res, zt, acc, part, total = ({} for i in range(16))
         ring = [keep.tile([P, 8 * STEP], BF16, name=f"ring{r}", align_bytes=64) for r in range(2)]
 
         def cast(s):
-            xc[s] = work.tile([P, 2 * L], BF16, name="xc", bufs=4)
+            xc[s] = work.tile([P, 2 * L], BF16, name="xc", bufs=5)
             nc.scalar.copy(out=xc[s][:], in_=x_in[s])
 
         def product(s, home=None):
@@ -255,7 +254,7 @@ def tile_tideresidualencodertemporaldecoder_t_kernel(
             nc.vector.tensor_tensor(out=acc[s][:, 1, :], in0=part[s][:], in1=acc[s][:, 1, :], op=ADD)
 
         def on_gpsimd(s):
-            return GFIRST <= s < STEPS - 2
+            return GFIRST <= s < STEPS - 1
 
         def rows_left(s):
             return slice(1 if on_gpsimd(s) else 0, 1 if on_tensor(s) else 2)
@@ -271,14 +270,15 @@ def tile_tideresidualencodertemporaldecoder_t_kernel(
                 nc.scalar.activation(out=plane, in_=plane, func=COPY, scale=vp_f[:, p : p + 1])
 
         def sum_on_gpsimd(s):
-            total = zt[s][:, 0, H : 2 * H]
-            for p in (2, 3):
-                nc.gpsimd.tensor_tensor(out=total, in0=total, in1=zt[s][:, 0, H * p : H * p + H], op=ADD)
-                if p == 2 and on_gpsimd(s - 1):
-                    add_sum(s - 1)
+            at = 4 * STEP if s + 3 != STEPS else 0
+            total[s] = ring[s % 2][:, at : at + 2 * H].bitcast(F32)
+            nc.gpsimd.tensor_tensor(out=total[s], in0=zt[s][:, 0, H : 2 * H], in1=zt[s][:, 0, 2 * H : 3 * H], op=ADD)
+            if on_gpsimd(s - 1):
+                add_sum(s - 1)
+            nc.gpsimd.tensor_tensor(out=total[s], in0=total[s], in1=zt[s][:, 0, 3 * H : 4 * H], op=ADD)
 
-        def add_sum(s):
-            nc.gpsimd.tensor_tensor(out=acc[s][:, 0, :], in0=acc[s][:, 0, :], in1=zt[s][:, 0, H : 2 * H], op=ADD)
+        def add_sum(s, engine=nc.gpsimd):
+            engine.tensor_tensor(out=acc[s][:, 0, :], in0=acc[s][:, 0, :], in1=total[s], op=ADD)
 
         def store(s, rows=slice(0, 2)):
             nc.sync.dma_start(out=out_view[:, s, rows, :], in_=acc[s][:, rows, :])
@@ -330,8 +330,8 @@ def tile_tideresidualencodertemporaldecoder_t_kernel(
         for p in range(1, P_DEC):
             nc.scalar.activation(out=vp_diag[:, p - 1, :], in_=ident[:], func=COPY, scale=vp_f[:, p : p + 1])
         nc.vector.tensor_copy(
-            out=group_of("w1")[:].rearrange("p (t m j) -> p t m j", t=4, j=4),
-            in_=w1_raw.rearrange("p j (m t) -> p t m j", t=4),
+            out=group_of("w1")[:].rearrange("p (t m j) -> p m j t", t=4, j=4),
+            in_=w1_raw.rearrange("p j (m t) -> p m j t", t=4),
         )
         cast(1)
         transposes(1, "part")
@@ -343,6 +343,7 @@ def tile_tideresidualencodertemporaldecoder_t_kernel(
         w1_q, w1_s = quantize("w1", groups["w1"][:], 1)
         quantize_x(0)
         hidden(0)
+        cast(4)
         weave("wsk1", wsk_raw[1], 0, 512, copy_on_gpsimd)
         weave("wsk0", wsk_raw[0], 0, 512, nc.scalar.copy)
         scale_x(1)
@@ -354,17 +355,16 @@ def tile_tideresidualencodertemporaldecoder_t_kernel(
         quantize_x(1)
         quantize_x(2)
         hidden(1)
-        quantize_h(0)
         empty_w("w20", 0)
         empty_w("w20", 1)
         fill_w("w21", w2_raw[1], 0)
-        wsk_q[0], wsk_s[0] = quantize("wsk0", groups["wsk0"][:], 1)
         wsk_q[1], wsk_s[1] = quantize("wsk1", groups["wsk1"][:], 1)
+        wsk_q[0], wsk_s[0] = quantize("wsk0", groups["wsk0"][:], 1)
+        quantize_h(0)
         w2_q[0], w2_s[0] = quantize("w20", groups["w20"][:], 1)
         weave("w21", w2_raw[1], 256, 256, nc.vector.tensor_copy)
         relu_h(1)
         empty_w("w21", 0)
-        cast(4)
         quantize_h(1)
         w2_q[1], w2_s[1] = quantize("w21", groups["w21"][:], 1)
         weave("wres", wres_raw, 0, 256, nc.scalar.copy)
@@ -419,15 +419,18 @@ def tile_tideresidualencodertemporaldecoder_t_kernel(
                     skip(s)
                 if s + 1 > STEPS - LEAD:
                     main(s + 1, 1, 1)
-            if more:
+            if on_gpsimd(s):
+                relu_z(s, slice(0, 2), 0)
+                relu_z(s, slice(0, 1), 1)
+                scale_planes(s)
+                relu_z(s, slice(1, 2), 1)
+            elif more:
                 relu_z(s, slice(0, 2), 0)
                 relu_z(s, slice(0, 2), 1)
             else:
                 for b in range(2):
                     for i in range(2):
                         relu_z(s, slice(i, i + 1), b)
-            if on_gpsimd(s):
-                scale_planes(s)
             if s + LEAD < STEPS:
                 empty_x(s + LEAD)
             if s >= 1 and on_tensor(s - 1):
@@ -448,9 +451,8 @@ def tile_tideresidualencodertemporaldecoder_t_kernel(
         last = STEPS - 1
         weigh_on_tensor(last - 1, [3])
         weigh(last, 0)
-        weigh_left(last - 1, 2)
+        add_sum(last - 1, nc.vector)
         weigh(last, 1, slice(0, 1))
-        weigh_left(last - 1, 3)
         weigh(last, 1, slice(1, 2))
         add_part(last - 1)
         store(last - 1)

@@ -407,16 +407,12 @@ def tile_tideresidualencodertemporaldecoder_t_kernel(
             if more:
                 main(s + 1, 1, 0)
             add_fut(s, 1, 1)
-            if s == 0:
-                wres_q, wres_s = quantize("wres", groups["wres"][:], 1)
             if more and s > 0:
                 skip(s)
             if s + LEAD < STEPS:
                 transposes(s + LEAD)
             if more:
                 main(s + 1, 0, 1)
-                if s == 0:
-                    skip(s)
                 if s + 1 > STEPS - LEAD:
                     main(s + 1, 1, 1)
             if on_gpsimd(s):
@@ -437,16 +433,23 @@ def tile_tideresidualencodertemporaldecoder_t_kernel(
                 weigh_on_tensor(s - 1, [2])
             if s >= 2:
                 weigh_left(s - 2, 2)
-            if s >= 1:
+            if s >= 2:
                 weigh_left(s - 1, 1)
-            if s >= 2 and on_tensor(s - 2):
+            if s >= 2 and on_tensor(s - 2) and s > 12:
                 add_part(s - 2)
             if s + 3 < STEPS:
                 quantize_both(s + 2)
             elif s + 2 < STEPS:
                 quantize_h(s + 2)
+            if s == 0:
+                wres_q, wres_s = quantize("wres", groups["wres"][:], 1)
+                skip(s)
+            if s == 1:
+                weigh_left(0, 1)
             if s >= 2:
                 weigh_left(s - 2, 3)
+                if on_tensor(s - 2) and s <= 12:
+                    add_part(s - 2)
                 store(s - 2)
         last = STEPS - 1
         weigh_on_tensor(last - 1, [3])

@@ -15,6 +15,7 @@ FP8 = mybir.dt.float8_e4m3fn
 FP8X4 = mybir.dt.float8_e4m3fn_x4
 ADD = mybir.AluOpType.add
 MULT = mybir.AluOpType.mult
+MAX = mybir.AluOpType.max
 COPY = mybir.ActivationFunctionType.Copy
 RELU = mybir.ActivationFunctionType.Relu
 
@@ -22,8 +23,10 @@ P = 128
 STEP = 256
 STEPS = N // STEP
 LEAD = 4
-GFIRST = STEPS - LEAD - 1
-FUT_AHEAD = 4
+FUT_AHEAD = 3
+UNIT = 2 * H
+SLOTS = 8
+PLACE = (2, 3, 0, 1)
 
 
 def tile_tideresidualencodertemporaldecoder_t_kernel(
@@ -63,20 +66,16 @@ def tile_tideresidualencodertemporaldecoder_t_kernel(
         nc.vector.memset(vp_bf[:], 0.0)
         nc.scalar.dma_start(out=vp_bf[0:1, :], in_=vp.rearrange("(o q) -> o q", o=1))
         halves = [slice(0, 512), slice(512, 1024)]
-        wsk_raw, w2_raw = {}, {}
         load_x(0, 1)
         w1_raw = load_w("w1_raw", w1, slice(0, F))
         load_x(1, 4)
-        wsk_all = load_w("wsk_raw", wsk, slice(0, PH))
-        wsk_raw = [wsk_all[:, :, b] for b in halves]
-        w2_raw[0] = load_w("w2_raw0", w2, halves[0])
-        w2_raw[1] = load_w("w2_raw1", w2, halves[1])
+        wsk_raw = [load_w(f"wsk_raw{b}", wsk, halves[b]) for b in range(2)]
+        w2_raw = [load_w(f"w2_raw{b}", w2, halves[b]) for b in range(2)]
         load_fut(0)
         wres_raw = load_w("wres_raw", wres, slice(0, H))
         load_x(5, 5)
         load_fut(1)
         load_fut(2)
-        load_fut(3)
         load_x(10, 6)
 
         ident = keep.tile([P, P], F32, name="ident")
@@ -86,60 +85,43 @@ def tile_tideresidualencodertemporaldecoder_t_kernel(
         ones_bf = keep.tile([P, P], BF16, name="ones_bf")
         nc.vector.memset(ones_bf[:], 1.0)
 
-        bank = psum.tile([P, 4, P], F32, name="sbank", tag="res", bufs=1)
-        for c in range(4):
-            nc.tensor.transpose(bank[:, c, :], scale_col[:, c : c + 1].to_broadcast([P, P]), ident[:])
-        scale_sorted = keep.tile([P, L], F32, name="scale_sorted")
-
-        xc, xb, xg, xq, xs, hg, hq, hs, xt, hb, rb, res, zt, acc, part, total = ({} for i in range(16))
+        xc, xg, xq, xs, hg, hq, hs, xt, hb, rb, res, part = ({} for i in range(12))
         ring = [keep.tile([P, 8 * STEP], BF16, name=f"ring{r}", align_bytes=64) for r in range(2)]
+        zring = keep.tile([P, SLOTS * 4 * UNIT], F32, name="zring")
+
+        def base(s):
+            return (SLOTS - 1 - s % SLOTS) * 4 * UNIT
+
+        def unit(s, place, rows=slice(0, 2)):
+            at = base(s) + place * UNIT
+            return zring[:, at + rows.start * H : at + rows.stop * H]
+
+        def plane(s, p, rows=slice(0, 2)):
+            return unit(s, PLACE[p], rows)
 
         def cast(s):
             xc[s] = work.tile([P, 2 * L], BF16, name="xc", bufs=5)
             nc.scalar.copy(out=xc[s][:], in_=x_in[s])
 
-        def product(s, home=None):
-            xb[s] = ring[(s - 3) % 2][:, 0 : 2 * L] if home is None else home
-            nc.gpsimd.tensor_tensor(
-                out=xb[s].rearrange("p (u i m e) -> p u i m e", u=2, i=2, e=2),
-                in0=xc[s][:].rearrange("p (i m u e) -> p u i m e", i=2, u=2, e=2),
-                in1=scale_sorted[:].rearrange("p (u o m e) -> p u o m e", u=2, o=1, e=2).to_broadcast([P, 2, 2, P, 2]),
-                op=MULT,
-            )
-
         def transposes(s, tag="xt", bufs=1):
             xt[s] = psum.tile([P, 512], F32, name="xt", tag=tag, bufs=bufs)
-            words = (xb[s] if s in xb else xc[s][:]).bitcast(F32)
+            words = xc[s][:].bitcast(F32)
             for u in range(2):
                 for i in range(2):
                     at = (2 * u + i) * P
-                    if s in xb:
-                        nc.tensor.transpose(xt[s][:, at : at + P], words[:, at : at + P], ident[:])
-                    else:
-                        second = slice(256 * i + u, 256 * (i + 1), 2)
-                        nc.tensor.transpose(xt[s][:, second], words[:, second], ident[:])
+                    nc.tensor.transpose(xt[s][:, at : at + P], words[:, 256 * i + u : 256 * (i + 1) : 2], ident[:])
 
-        def x_home(s):
-            if s >= 3:
-                xg[s] = ring[(s - 1) % 2][:, 4 * STEP : 8 * STEP]
+        def product(s):
+            if s >= LEAD:
+                xg[s] = ring[s % 2][:, 4 * STEP : 8 * STEP]
             elif s == 0:
-                xg[s] = group_of("wsk1")[:, 0 : 4 * STEP]
+                xg[s] = group_of("wsk0")[:, 0 : 4 * STEP]
             else:
                 xg[s] = work.tile([P, 4 * STEP], BF16, name="xg", bufs=3, align_bytes=64)[:]
-
-        def empty_x(s):
-            x_home(s)
-            nc.scalar.copy(
-                out=xg[s].bitcast(F32).rearrange("q (n u) -> q n u", u=2),
-                in_=xt[s][:].rearrange("q (u n) -> q n u", u=2),
-            )
-
-        def scale_x(s):
-            x_home(s)
             nc.vector.tensor_tensor(
-                out=xg[s].rearrange("q (n t) -> q n t", t=4),
-                in0=xt[s][:].bitcast(BF16).rearrange("q (n t) -> q n t", t=4),
-                in1=scale_col[:].rearrange("q (o t) -> q o t", o=1).to_broadcast([P, STEP, 4]),
+                out=xg[s].rearrange("q (n u e) -> q n u e", u=2, e=2),
+                in0=xt[s][:].bitcast(BF16).rearrange("q (u n e) -> q n u e", u=2, e=2),
+                in1=scale_col[:].rearrange("q (o u e) -> q o u e", o=1, u=2).to_broadcast([P, STEP, 2, 2]),
                 op=MULT,
             )
 
@@ -151,34 +133,34 @@ def tile_tideresidualencodertemporaldecoder_t_kernel(
             return codes, scales
 
         def quantize_x(s):
-            xq[s], xs[s] = quantize("x", xg[s], 3)
+            xq[s], xs[s] = quantize("x", xg[s], 4)
 
         def quantize_h(s):
-            hq[s], hs[s] = quantize("h", hg[s][:], 3)
+            hq[s], hs[s] = quantize("h", hg[s], 3)
 
         def quantize_both(s):
-            codes, scales = quantize("both", ring[s % 2][:], 5)
-            hq[s], hs[s] = codes[:, 0:STEP], scales[:, 0:STEP]
-            xq[s + 1], xs[s + 1] = codes[:, STEP : 2 * STEP], scales[:, STEP : 2 * STEP]
+            codes, scales = quantize("both", ring[s % 2][:], 6)
+            hq[s + 2], hs[s + 2] = codes[:, 0:STEP], scales[:, 0:STEP]
+            xq[s + LEAD], xs[s + LEAD] = codes[:, STEP : 2 * STEP], scales[:, STEP : 2 * STEP]
 
         def hidden(s):
             for i in range(2):
                 hb[s, i] = psum.tile([P, 512], F32, name="hb", bufs=2)
                 cols = slice(i * P, i * P + P)
                 for t in range(4):
-                    part = slice(t * P, t * P + P)
+                    chans = slice(t * P, t * P + P)
                     nc.tensor.matmul_mx(
-                        out=hb[s, i][:, part],
-                        lhsT=w1_q[:, part].bitcast(FP8X4), lhsT_scale=w1_s[:, part],
+                        out=hb[s, i][:, chans],
+                        lhsT=w1_q[:, chans].bitcast(FP8X4), lhsT_scale=w1_s[:, chans],
                         rhs=xq[s][:, cols].bitcast(FP8X4), rhs_scale=xs[s][:, cols],
                         start=True, stop=True,
                     )
 
         def relu_h(s):
-            if s >= 1:
+            if s >= 2:
                 hg[s] = ring[s % 2][:, 0 : 4 * STEP]
             else:
-                hg[s] = work.tile([P, 4 * STEP], BF16, name="hg", align_bytes=64)
+                hg[s] = work.tile([P, 4 * STEP], BF16, name="hg", align_bytes=64)[:]
             for i in range(2):
                 nc.scalar.activation(
                     out=hg[s][:, 512 * i : 512 * i + 512].rearrange("m (n t) -> m n t", t=4),
@@ -188,10 +170,7 @@ def tile_tideresidualencodertemporaldecoder_t_kernel(
 
         def main(s, i, b):
             cols = slice(i * P, i * P + P)
-            if s > STEPS - LEAD and (i, b) == (1, 1):
-                rb[s, i, b] = psum.tile([P, 512], F32, name="rb4", tag="xt", bufs=1)
-            else:
-                rb[s, i, b] = psum.tile([P, 512], F32, name="rb", bufs=3)
+            rb[s, i, b] = psum.tile([P, 512], F32, name="rb", bufs=4)
             nc.tensor.matmul_mx(
                 out=rb[s, i, b][:],
                 lhsT=xq[s][:, cols].bitcast(FP8X4), lhsT_scale=xs[s][:, cols],
@@ -205,8 +184,8 @@ def tile_tideresidualencodertemporaldecoder_t_kernel(
                 start=False, stop=True,
             )
 
-        def skip(s):
-            res[s] = psum.tile([P, 512], F32, name="res", bufs=1)
+        def skip(s, tag="res"):
+            res[s] = psum.tile([P, 512], F32, name="res", tag=tag, bufs=1)
             for i in range(2):
                 cols = slice(i * P, i * P + P)
                 nc.tensor.matmul_mx(
@@ -217,71 +196,67 @@ def tile_tideresidualencodertemporaldecoder_t_kernel(
                 )
 
         def add_fut(s, i, b):
-            if s not in zt:
-                zt[s] = work.tile([P, 2, PH], F32, name="zt", bufs=4)
+            at = base(s) + PLACE[2 * b] * UNIT
+            pair = zring[:, at : at + 2 * UNIT].rearrange("p (q i j) -> p q i j", q=2, i=2)
             nc.vector.tensor_tensor(
-                out=zt[s][:, i, halves[b]], in0=rb[s, i, b][:], in1=fut_in[s][:, i, halves[b]], op=ADD
+                out=pair[:, :, i, :],
+                in0=rb[s, i, b][:].rearrange("p (q j) -> p q j", q=2),
+                in1=fut_in[s][:, i, halves[b]].rearrange("p (q j) -> p q j", q=2),
+                op=ADD,
             )
 
-        def relu_z(s, rows, b):
-            nc.scalar.activation(out=zt[s][:, rows, halves[b]], in_=zt[s][:, rows, halves[b]], func=RELU)
+        def relu_pair(s, b):
+            at = base(s) + PLACE[2 * b] * UNIT
+            nc.scalar.activation(out=zring[:, at : at + 2 * UNIT], in_=zring[:, at : at + 2 * UNIT], func=RELU)
 
-        def weigh(s, p, rows=slice(0, 2)):
-            if s not in acc:
-                acc[s] = work.tile([P, 2, H], F32, name="acc", bufs=4)
-            before = res[s][:].rearrange("p (i j) -> p i j", i=2) if p == 0 else acc[s]
+        def relu_plane(s, p, rows=slice(0, 2)):
+            nc.scalar.activation(out=plane(s, p, rows), in_=plane(s, p, rows), func=RELU)
+
+        def scale_plane(s, p, rows=slice(0, 2)):
+            nc.scalar.activation(out=plane(s, p, rows), in_=plane(s, p, rows), func=COPY, scale=vp_f[:, p : p + 1])
+
+        def relu_scale(s, p):
+            nc.vector.tensor_scalar(
+                out=plane(s, p), in0=plane(s, p), scalar1=0.0, scalar2=vp_f[:, p : p + 1], op0=MAX, op1=MULT
+            )
+
+        def weigh_skip(s):
+            p = 2
             nc.vector.scalar_tensor_tensor(
-                out=acc[s][:, rows, :], in0=zt[s][:, rows, H * p : H * p + H],
-                scalar=vp_f[:, p : p + 1], in1=before[:, rows, :], op0=MULT, op1=ADD,
+                out=plane(s, p), in0=plane(s, p), scalar=vp_f[:, p : p + 1], in1=res[s][:], op0=MULT, op1=ADD
             )
 
-        def on_tensor(s):
-            return 1 < s < STEPS - 1 and (s % 2 == 0 or s > 12)
+        def weigh(s, p, rows, into):
+            before = res[s][:, rows.start * H : rows.stop * H] if into is None else plane(s, into, rows)
+            nc.vector.scalar_tensor_tensor(
+                out=plane(s, p if into is None else into, rows), in0=plane(s, p, rows), scalar=vp_f[:, p : p + 1],
+                in1=before, op0=MULT, op1=ADD,
+            )
 
-        def weigh_on_tensor(s, planes):
+        def sums(s, first, count, rows=slice(0, 2)):
+            at = base(s)
+            pairs = zring[:, at + 2 * first * UNIT : at + 2 * (first + count) * UNIT].rearrange("p (c o i j) -> p c o i j", o=2, i=2, j=H)
+            dest = zring[:, at + first * UNIT : at + (first + count) * UNIT].rearrange("p (c i j) -> p c i j", i=2, j=H)
+            nc.gpsimd.tensor_tensor(out=dest[:, :, rows, :], in0=pairs[:, :, 0, rows, :], in1=pairs[:, :, 1, rows, :], op=ADD)
+
+        def join(s, dest, rows=slice(0, 2)):
+            nc.gpsimd.tensor_tensor(out=dest, in0=unit(s, 0, rows), in1=unit(s, 1, rows), op=ADD)
+
+        def weigh_on_tensor(s, i, planes):
             if s not in part:
-                if s < STEPS - 3 or s % 2 == 0:
-                    part[s] = psum.tile([P, H], F32, name="part", bufs=1)
-                else:
-                    part[s] = psum.tile([P, H], F32, name="part", tag="hb", bufs=2)
+                part[s] = psum.tile([P, H], F32, name="part", tag="hb", bufs=2)
             for p in planes:
                 nc.tensor.matmul(
-                    out=part[s][:], lhsT=vp_diag[:, p - 1, :], rhs=zt[s][:, 1, H * p : H * p + H],
-                    start=(p == 1), stop=(p == P_DEC - 1),
+                    out=part[s][:], lhsT=vp_diag[:, p, :], rhs=plane(s, p, slice(i, i + 1)),
+                    start=(p == 0), stop=(p == 3),
                 )
 
-        def add_part(s):
-            nc.vector.tensor_tensor(out=acc[s][:, 1, :], in0=part[s][:], in1=acc[s][:, 1, :], op=ADD)
+        def add_part(s, i):
+            rows = slice(i, i + 1)
+            nc.vector.tensor_tensor(out=plane(s, 2, rows), in0=part[s][:], in1=plane(s, 2, rows), op=ADD)
 
-        def on_gpsimd(s):
-            return GFIRST <= s < STEPS - 1
-
-        def rows_left(s):
-            return slice(1 if on_gpsimd(s) else 0, 1 if on_tensor(s) else 2)
-
-        def weigh_left(s, p):
-            rows = rows_left(s)
-            if rows.start < rows.stop:
-                weigh(s, p, rows)
-
-        def scale_planes(s):
-            for p in (1, 2, 3):
-                plane = zt[s][:, 0, H * p : H * p + H]
-                nc.scalar.activation(out=plane, in_=plane, func=COPY, scale=vp_f[:, p : p + 1])
-
-        def sum_on_gpsimd(s):
-            at = 4 * STEP if s + 3 != STEPS else 0
-            total[s] = ring[s % 2][:, at : at + 2 * H].bitcast(F32)
-            nc.gpsimd.tensor_tensor(out=total[s], in0=zt[s][:, 0, H : 2 * H], in1=zt[s][:, 0, 2 * H : 3 * H], op=ADD)
-            if on_gpsimd(s - 1):
-                add_sum(s - 1)
-            nc.gpsimd.tensor_tensor(out=total[s], in0=total[s], in1=zt[s][:, 0, 3 * H : 4 * H], op=ADD)
-
-        def add_sum(s, engine=nc.gpsimd):
-            engine.tensor_tensor(out=acc[s][:, 0, :], in0=acc[s][:, 0, :], in1=total[s], op=ADD)
-
-        def store(s, rows=slice(0, 2)):
-            nc.sync.dma_start(out=out_view[:, s, rows, :], in_=acc[s][:, rows, :])
+        def store(s, source, rows=slice(0, 2)):
+            nc.sync.dma_start(out=out_view[:, s, rows, :], in_=source.rearrange("p (i j) -> p i j", j=H))
 
         groups = {}
 
@@ -292,175 +267,214 @@ def tile_tideresidualencodertemporaldecoder_t_kernel(
 
         banks = {}
 
-        def fill_w(name, raw, half, order="p j (t m) -> p t m j"):
-            views = raw.rearrange(order, t=4)
-            banks[name, half] = psum.tile([P, 2, 512], BF16, name="wbank", tag="rb", bufs=3)
+        def fill_w(name, raw, half):
+            views = raw.rearrange("p j (t m) -> p t m j", t=4)
+            banks[name, half] = psum.tile([P, 2, 512], BF16, name="wbank", tag="rb", bufs=4)
             for n in range(2):
                 nc.tensor.matmul(out=banks[name, half][:, n, :], lhsT=ident_bf[:], rhs=views[:, 2 * half + n], start=True, stop=True)
 
-        def empty_w(name, half, copy=nc.scalar.copy):
+        def empty_w(name, half):
             dst = group_of(name)[:, 1024 * half : 1024 * half + 1024]
-            copy(out=dst, in_=banks[name, half][:].rearrange("p n c -> p (n c)"))
+            nc.scalar.copy(out=dst, in_=banks[name, half][:].rearrange("p n c -> p (n c)"))
 
-        def copy_on_gpsimd(out, in_):
-            nc.gpsimd.tensor_scalar(out=out, in0=in_, scalar1=1.0, scalar2=0.0, op0=MULT, op1=ADD)
+        def weave_on_gpsimd(dst, raw):
+            nc.gpsimd.tensor_scalar(
+                out=dst.rearrange("p (c j) -> p c j", j=4), in0=raw.rearrange("p j c -> p c j"),
+                scalar1=1.0, scalar2=0.0, op0=MULT, op1=ADD,
+            )
 
-        def weave(name, raw, c0, width, copy):
-            dst = group_of(name, raw.shape[2])[:, 4 * c0 : 4 * (c0 + width)]
-            if copy is copy_on_gpsimd:
-                copy(out=dst.rearrange("p (c j) -> p c j", j=4), in_=raw[:, :, c0 : c0 + width].rearrange("p j c -> p c j"))
-                return
-            copy(
-                out=dst.rearrange("p (c i j) -> p c j i", i=4, j=4),
-                in_=raw[:, :, c0 : c0 + width].rearrange("p j (c i) -> p c j i", i=4),
+        def weave_on_vector(dst, raw):
+            nc.vector.tensor_copy(
+                out=dst.rearrange("p (c i j) -> p c j i", i=4, j=4), in_=raw.rearrange("p j (c i) -> p c j i", i=4)
+            )
+
+        def weave_on_scalar(dst, raw):
+            nc.scalar.copy(
+                out=dst.rearrange("p (c i j) -> p c j i", i=4, j=4), in_=raw.rearrange("p j (c i) -> p c j i", i=4)
             )
 
         wsk_q, wsk_s, w2_q, w2_s = {}, {}, {}, {}
 
         vp_f = keep.tile([P, P_DEC], F32, name="vp_f")
+        vp_diag = keep.tile([P, P_DEC, P], F32, name="vp_diag")
         vbank = psum.tile([P, P_DEC], F32, name="vbank", tag="hb", bufs=2)
-        nc.tensor.matmul(out=vbank[:], lhsT=ones_bf[:], rhs=vp_bf[:], start=True, stop=True)
         cast(0)
         transposes(0)
-        nc.scalar.copy(
-            out=scale_sorted[:].rearrange("p (u m e) -> p u m e", u=2, e=2), in_=bank[:].rearrange("p (u e) m -> p u m e", u=2)
-        )
+        nc.tensor.matmul(out=vbank[:], lhsT=ones_bf[:], rhs=vp_bf[:], start=True, stop=True)
         nc.scalar.copy(out=vp_f[:], in_=vbank[:])
-        vp_diag = keep.tile([P, P_DEC - 1, P], F32, name="vp_diag")
-        for p in range(1, P_DEC):
-            nc.scalar.activation(out=vp_diag[:, p - 1, :], in_=ident[:], func=COPY, scale=vp_f[:, p : p + 1])
         nc.vector.tensor_copy(
             out=group_of("w1")[:].rearrange("p (t m j) -> p m j t", t=4, j=4),
             in_=w1_raw.rearrange("p j (m t) -> p m j t", t=4),
         )
         cast(1)
-        transposes(1, "part")
+        transposes(1, "rb", 4)
         cast(2)
         transposes(2, "res")
         cast(3)
-        scale_x(0)
+        product(0)
         transposes(3)
         w1_q, w1_s = quantize("w1", groups["w1"][:], 1)
         quantize_x(0)
         hidden(0)
         cast(4)
-        weave("wsk1", wsk_raw[1], 0, 512, copy_on_gpsimd)
-        weave("wsk0", wsk_raw[0], 0, 512, nc.scalar.copy)
-        scale_x(1)
-        scale_x(2)
-        scale_x(3)
+        weave_on_gpsimd(group_of("wsk0")[:], wsk_raw[0])
+        weave_on_scalar(group_of("wsk1")[:], wsk_raw[1])
+        product(1)
+        product(2)
+        product(3)
         relu_h(0)
         fill_w("w20", w2_raw[0], 0)
         fill_w("w20", w2_raw[0], 1)
         quantize_x(1)
         quantize_x(2)
+        quantize_x(3)
         hidden(1)
+        fill_w("w21", w2_raw[1], 0)
         empty_w("w20", 0)
         empty_w("w20", 1)
-        fill_w("w21", w2_raw[1], 0)
-        wsk_q[1], wsk_s[1] = quantize("wsk1", groups["wsk1"][:], 1)
         wsk_q[0], wsk_s[0] = quantize("wsk0", groups["wsk0"][:], 1)
+        wsk_q[1], wsk_s[1] = quantize("wsk1", groups["wsk1"][:], 1)
         quantize_h(0)
         w2_q[0], w2_s[0] = quantize("w20", groups["w20"][:], 1)
-        weave("w21", w2_raw[1], 256, 256, nc.vector.tensor_copy)
+        weave_on_vector(group_of("w21")[:, 1024:2048], w2_raw[1][:, :, 256:512])
+        main(0, 0, 0)
+        main(0, 1, 0)
         relu_h(1)
         empty_w("w21", 0)
         quantize_h(1)
         w2_q[1], w2_s[1] = quantize("w21", groups["w21"][:], 1)
-        weave("wres", wres_raw, 0, 256, nc.scalar.copy)
-        main(0, 0, 0)
-        main(0, 1, 0)
+        wres_g = hg[1]
+        weave_on_gpsimd(wres_g, wres_raw)
         hidden(2)
         main(0, 0, 1)
+        main(0, 1, 1)
+        relu_h(2)
+        transposes(4)
 
-        for s in range(STEPS):
-            more = s + 1 < STEPS
-            if s + FUT_AHEAD < STEPS:
-                load_fut(s + FUT_AHEAD)
-            if s + LEAD < STEPS:
-                product(s + LEAD)
-            if 2 < s + 2 < STEPS:
-                hidden(s + 2)
-            if s + 2 < STEPS:
-                relu_h(s + 2)
+        def adds(s, b):
+            for i in range(2):
+                add_fut(s, i, b)
+                if s + 1 < STEPS - 2:
+                    main(s + 1, i, b)
+
+        def mains(s):
+            for b in range(2):
+                for i in range(2):
+                    main(s, i, b)
+
+        def sums_and_store(s):
+            if s % SLOTS:
+                sums(s, 0, 3)
+            else:
+                sums(s, 0, 2)
+                if s:
+                    join(s - 1, unit(s, 2))
+            if s:
+                store(s - 1, unit(s, 2))
+
+        tile0, tile1 = slice(0, 1), slice(1, 2)
+        for s in range(STEPS - LEAD):
+            load_fut(s + FUT_AHEAD)
             if s + LEAD + 1 < STEPS:
                 cast(s + LEAD + 1)
-            add_fut(s, 0, 0)
-            if s <= STEPS - LEAD:
-                main(s, 1, 1)
-            add_fut(s, 1, 0)
-            if more:
-                main(s + 1, 0, 0)
-            if s >= 1:
-                weigh(s - 1, 0)
-                if on_gpsimd(s - 1):
-                    sum_on_gpsimd(s - 1)
-                elif on_gpsimd(s - 2):
-                    add_sum(s - 2)
-            if s >= 2 and on_tensor(s - 2):
-                weigh_on_tensor(s - 2, [3])
-            if not more:
-                skip(s)
-            if s >= 1 and on_tensor(s - 1):
-                weigh_on_tensor(s - 1, [1])
-            add_fut(s, 0, 1)
-            if more:
-                main(s + 1, 1, 0)
-            add_fut(s, 1, 1)
-            if more and s > 0:
-                skip(s)
-            if s + LEAD < STEPS:
-                transposes(s + LEAD)
-            if more:
-                main(s + 1, 0, 1)
-                if s + 1 > STEPS - LEAD:
-                    main(s + 1, 1, 1)
-            if on_gpsimd(s):
-                relu_z(s, slice(0, 2), 0)
-                relu_z(s, slice(0, 1), 1)
-                scale_planes(s)
-                relu_z(s, slice(1, 2), 1)
-            elif more:
-                relu_z(s, slice(0, 2), 0)
-                relu_z(s, slice(0, 2), 1)
             else:
-                for b in range(2):
-                    for i in range(2):
-                        relu_z(s, slice(i, i + 1), b)
-            if s + LEAD < STEPS:
-                empty_x(s + LEAD)
-            if s >= 1 and on_tensor(s - 1):
-                weigh_on_tensor(s - 1, [2])
-            if s >= 2:
-                weigh_left(s - 2, 2)
-            if s >= 2:
-                weigh_left(s - 1, 1)
-            if s >= 2 and on_tensor(s - 2) and s > 12:
-                add_part(s - 2)
-            if s + 3 < STEPS:
-                quantize_both(s + 2)
-            elif s + 2 < STEPS:
-                quantize_h(s + 2)
-            if s == 0:
-                wres_q, wres_s = quantize("wres", groups["wres"][:], 1)
+                for p in (0, 1, 3):
+                    nc.scalar.activation(out=vp_diag[:, p, :], in_=ident[:], func=COPY, scale=vp_f[:, p : p + 1])
+            if s > 0:
                 skip(s)
-            if s == 1:
-                weigh_left(0, 1)
-            if s >= 2:
-                weigh_left(s - 2, 3)
-                if on_tensor(s - 2) and s <= 12:
-                    add_part(s - 2)
-                store(s - 2)
-        last = STEPS - 1
-        weigh_on_tensor(last - 1, [3])
-        weigh(last, 0)
-        add_sum(last - 1, nc.vector)
-        weigh(last, 1, slice(0, 1))
-        weigh(last, 1, slice(1, 2))
-        add_part(last - 1)
-        store(last - 1)
-        for p in range(2, P_DEC):
-            for i in range(2):
-                weigh(last, p, slice(i, i + 1))
-                if p == P_DEC - 1:
-                    store(last, slice(i, i + 1))
+                hidden(s + 3)
+                adds(s, 0)
+                relu_pair(s, 0)
+                adds(s, 1)
+            else:
+                add_fut(s, 0, 0)
+                main(s + 1, 0, 0)
+                add_fut(s, 1, 0)
+                relu_pair(s, 0)
+                add_fut(s, 0, 1)
+                add_fut(s, 1, 1)
+                wres_q, wres_s = quantize("wres", wres_g, 1)
+                skip(s)
+                main(s + 1, 1, 0)
+                hidden(s + 3)
+                main(s + 1, 0, 1)
+                main(s + 1, 1, 1)
+            product(s + LEAD)
+            if s + LEAD + 1 < STEPS:
+                transposes(s + LEAD + 1)
+            relu_plane(s, 2)
+            scale_plane(s, 0)
+            scale_plane(s, 1)
+            weigh_skip(s)
+            relu_scale(s, 3)
+            relu_h(s + 3)
+            quantize_both(s)
+            sums_and_store(s)
+
+        load_fut(15)
+        skip(12)
+        hidden(15)
+        adds(12, 0)
+        relu_pair(12, 0)
+        adds(12, 1)
+        relu_plane(12, 2)
+        scale_plane(12, 0)
+        scale_plane(12, 1)
+        relu_h(15)
+        adds(13, 0)
+        weigh_skip(12)
+        skip(13)
+        relu_scale(12, 3)
+        quantize_h(14)
+        sums_and_store(12)
+        main(14, 0, 0)
+        main(14, 1, 0)
+        relu_pair(13, 0)
+        adds(13, 1)
+        main(14, 0, 1)
+        main(14, 1, 1)
+        relu_pair(13, 1)
+        skip(14, "xt")
+        weigh_on_tensor(13, 1, [0, 1, 3])
+        adds(14, 0)
+        adds(14, 1)
+        relu_plane(14, 2)
+        for p in (0, 1, 3):
+            scale_plane(13, p, tile0)
+        weigh_skip(13)
+        quantize_h(15)
+        skip(15)
+        mains(15)
+        joined = hg[15].bitcast(F32)
+        join(12, joined)
+        store(12, joined)
+        sums(13, 0, 2, tile0)
+        join(13, unit(13, 0, tile0), tile0)
+        store(13, unit(13, 0, tile0), tile0)
+        relu_pair(14, 0)
+        relu_plane(14, 3)
+        weigh_skip(14)
+        add_part(13, 1)
+        store(13, plane(13, 2, tile1), tile1)
+        weigh_on_tensor(14, 1, [0, 1, 3])
+        adds(15, 0)
+        relu_pair(15, 0)
+        adds(15, 1)
+        relu_plane(15, 3, tile0)
+        relu_plane(15, 2)
+        relu_plane(15, 3, tile1)
+        weigh_on_tensor(15, 0, [0, 1, 3])
+        weigh(14, 0, tile0, 2)
+        weigh(15, 0, tile1, None)
+        weigh(14, 1, tile0, 2)
+        add_part(14, 1)
+        store(14, plane(14, 2, tile1), tile1)
+        weigh(14, 3, tile0, 2)
+        store(14, plane(14, 2, tile0), tile0)
+        weigh(15, 1, tile1, 0)
+        weigh(15, 2, tile0, None)
+        weigh(15, 2, tile1, 0)
+        add_part(15, 0)
+        store(15, plane(15, 2, tile0), tile0)
+        weigh(15, 3, tile1, 0)
+        store(15, plane(15, 0, tile1), tile1)

@@ -109,7 +109,9 @@ def tile_tideresidualencodertemporaldecoder_t_kernel(
             for u in range(2):
                 for i in range(2):
                     at = (2 * u + i) * P
-                    nc.tensor.transpose(xt[s][:, at : at + P], words[:, 256 * i + u : 256 * (i + 1) : 2], ident[:])
+                    second = slice(256 * i + u, 256 * (i + 1), 2)
+                    dest = xt[s][:, second] if s < LEAD else xt[s][:, at : at + P]
+                    nc.tensor.transpose(dest, words[:, second], ident[:])
 
         def product(s):
             if s >= LEAD:
@@ -120,7 +122,7 @@ def tile_tideresidualencodertemporaldecoder_t_kernel(
                 xg[s] = work.tile([P, 4 * STEP], BF16, name="xg", bufs=3, align_bytes=64)[:]
             nc.vector.tensor_tensor(
                 out=xg[s].rearrange("q (n u e) -> q n u e", u=2, e=2),
-                in0=xt[s][:].bitcast(BF16).rearrange("q (u n e) -> q n u e", u=2, e=2),
+                in0=xt[s][:].bitcast(BF16).rearrange("q (n u e) -> q n u e" if s < LEAD else "q (u n e) -> q n u e", u=2, e=2),
                 in1=scale_col[:].rearrange("q (o u e) -> q o u e", o=1, u=2).to_broadcast([P, STEP, 2, 2]),
                 op=MULT,
             )

@@ -26,7 +26,7 @@ LEAD = 4
 FUT_AHEAD = 3
 UNIT = 2 * H
 SLOTS = 8
-PLACE = (2, 3, 0, 1)
+PLACE = (0, 2, 1, 3)
 
 
 def tile_tideresidualencodertemporaldecoder_t_kernel(
@@ -99,6 +99,9 @@ def tile_tideresidualencodertemporaldecoder_t_kernel(
         def plane(s, p, rows=slice(0, 2)):
             return unit(s, PLACE[p], rows)
 
+        def pair(s, b):
+            return zring[:, base(s) : base(s) + 4 * UNIT].rearrange("p (q b c) -> p q b c", q=2, b=2)[:, :, b, :]
+
         def cast(s):
             xc[s] = work.tile([P, 2 * L], BF16, name="xc", bufs=5)
             nc.scalar.copy(out=xc[s][:], in_=x_in[s])
@@ -143,7 +146,10 @@ def tile_tideresidualencodertemporaldecoder_t_kernel(
         def quantize_both(s):
             codes, scales = quantize("both", ring[s % 2][:], 6)
             hq[s + 2], hs[s + 2] = codes[:, 0:STEP], scales[:, 0:STEP]
-            xq[s + LEAD], xs[s + LEAD] = codes[:, STEP : 2 * STEP], scales[:, STEP : 2 * STEP]
+            if s + LEAD < STEPS:
+                xq[s + LEAD], xs[s + LEAD] = codes[:, STEP : 2 * STEP], scales[:, STEP : 2 * STEP]
+            else:
+                hq[s + 3], hs[s + 3] = codes[:, STEP : 2 * STEP], scales[:, STEP : 2 * STEP]
 
         def hidden(s):
             for i in range(2):
@@ -159,7 +165,9 @@ def tile_tideresidualencodertemporaldecoder_t_kernel(
                     )
 
         def relu_h(s):
-            if s >= 2:
+            if s == STEPS - 1:
+                hg[s] = ring[(s - 1) % 2][:, 4 * STEP : 8 * STEP]
+            elif s >= 2:
                 hg[s] = ring[s % 2][:, 0 : 4 * STEP]
             else:
                 hg[s] = work.tile([P, 4 * STEP], BF16, name="hg", align_bytes=64)[:]
@@ -198,18 +206,15 @@ def tile_tideresidualencodertemporaldecoder_t_kernel(
                 )
 
         def add_fut(s, i, b):
-            at = base(s) + PLACE[2 * b] * UNIT
-            pair = zring[:, at : at + 2 * UNIT].rearrange("p (q i j) -> p q i j", q=2, i=2)
             nc.vector.tensor_tensor(
-                out=pair[:, :, i, :],
+                out=pair(s, b)[:, :, i * H : i * H + H],
                 in0=rb[s, i, b][:].rearrange("p (q j) -> p q j", q=2),
                 in1=fut_in[s][:, i, halves[b]].rearrange("p (q j) -> p q j", q=2),
                 op=ADD,
             )
 
         def relu_pair(s, b):
-            at = base(s) + PLACE[2 * b] * UNIT
-            nc.scalar.activation(out=zring[:, at : at + 2 * UNIT], in_=zring[:, at : at + 2 * UNIT], func=RELU)
+            nc.scalar.activation(out=pair(s, b), in_=pair(s, b), func=RELU)
 
         def relu_plane(s, p, rows=slice(0, 2)):
             nc.scalar.activation(out=plane(s, p, rows), in_=plane(s, p, rows), func=RELU)
@@ -223,16 +228,15 @@ def tile_tideresidualencodertemporaldecoder_t_kernel(
             )
 
         def weigh_skip(s):
-            p = 2
+            p = 1
             nc.vector.scalar_tensor_tensor(
                 out=plane(s, p), in0=plane(s, p), scalar=vp_f[:, p : p + 1], in1=res[s][:], op0=MULT, op1=ADD
             )
 
         def weigh(s, p, rows, into):
-            before = res[s][:, rows.start * H : rows.stop * H] if into is None else plane(s, into, rows)
             nc.vector.scalar_tensor_tensor(
-                out=plane(s, p if into is None else into, rows), in0=plane(s, p, rows), scalar=vp_f[:, p : p + 1],
-                in1=before, op0=MULT, op1=ADD,
+                out=plane(s, into, rows), in0=plane(s, p, rows), scalar=vp_f[:, p : p + 1],
+                in1=plane(s, into, rows), op0=MULT, op1=ADD,
             )
 
         def sums(s, first, count, rows=slice(0, 2)):
@@ -255,7 +259,7 @@ def tile_tideresidualencodertemporaldecoder_t_kernel(
 
         def add_part(s, i):
             rows = slice(i, i + 1)
-            nc.vector.tensor_tensor(out=plane(s, 2, rows), in0=part[s][:], in1=plane(s, 2, rows), op=ADD)
+            nc.vector.tensor_tensor(out=plane(s, 1, rows), in0=part[s][:], in1=plane(s, 1, rows), op=ADD)
 
         def store(s, source, rows=slice(0, 2)):
             nc.sync.dma_start(out=out_view[:, s, rows, :], in_=source.rearrange("p (i j) -> p i j", j=H))
@@ -300,10 +304,9 @@ def tile_tideresidualencodertemporaldecoder_t_kernel(
         vp_f = keep.tile([P, P_DEC], F32, name="vp_f")
         vp_diag = keep.tile([P, P_DEC, P], F32, name="vp_diag")
         vbank = psum.tile([P, P_DEC], F32, name="vbank", tag="hb", bufs=2)
+        nc.tensor.matmul(out=vbank[:], lhsT=ones_bf[:], rhs=vp_bf[:], start=True, stop=True)
         cast(0)
         transposes(0)
-        nc.tensor.matmul(out=vbank[:], lhsT=ones_bf[:], rhs=vp_bf[:], start=True, stop=True)
-        nc.scalar.copy(out=vp_f[:], in_=vbank[:])
         nc.vector.tensor_copy(
             out=group_of("w1")[:].rearrange("p (t m j) -> p m j t", t=4, j=4),
             in_=w1_raw.rearrange("p j (m t) -> p m j t", t=4),
@@ -313,6 +316,7 @@ def tile_tideresidualencodertemporaldecoder_t_kernel(
         cast(2)
         transposes(2, "res")
         cast(3)
+        nc.scalar.copy(out=vp_f[:], in_=vbank[:])
         product(0)
         transposes(3)
         w1_q, w1_s = quantize("w1", groups["w1"][:], 1)
@@ -374,13 +378,13 @@ def tile_tideresidualencodertemporaldecoder_t_kernel(
             if s:
                 store(s - 1, unit(s, 2))
 
-        tile0, tile1 = slice(0, 1), slice(1, 2)
+        both, tile0, tile1 = slice(0, 2), slice(0, 1), slice(1, 2)
         for s in range(STEPS - LEAD):
             load_fut(s + FUT_AHEAD)
             if s + LEAD + 1 < STEPS:
                 cast(s + LEAD + 1)
             else:
-                for p in (0, 1, 3):
+                for p in (0, 2, 3):
                     nc.scalar.activation(out=vp_diag[:, p, :], in_=ident[:], func=COPY, scale=vp_f[:, p : p + 1])
             if s > 0:
                 skip(s)
@@ -406,7 +410,7 @@ def tile_tideresidualencodertemporaldecoder_t_kernel(
                 transposes(s + LEAD + 1)
             relu_plane(s, 2)
             scale_plane(s, 0)
-            scale_plane(s, 1)
+            scale_plane(s, 2)
             weigh_skip(s)
             relu_scale(s, 3)
             relu_h(s + 3)
@@ -416,18 +420,18 @@ def tile_tideresidualencodertemporaldecoder_t_kernel(
         load_fut(15)
         skip(12)
         hidden(15)
+        relu_h(15)
         adds(12, 0)
         relu_pair(12, 0)
         adds(12, 1)
         relu_plane(12, 2)
         scale_plane(12, 0)
-        scale_plane(12, 1)
-        relu_h(15)
+        scale_plane(12, 2)
         adds(13, 0)
         weigh_skip(12)
         skip(13)
         relu_scale(12, 3)
-        quantize_h(14)
+        quantize_both(12)
         sums_and_store(12)
         main(14, 0, 0)
         main(14, 1, 0)
@@ -437,46 +441,40 @@ def tile_tideresidualencodertemporaldecoder_t_kernel(
         main(14, 1, 1)
         relu_pair(13, 1)
         skip(14, "xt")
-        weigh_on_tensor(13, 1, [0, 1, 3])
-        adds(14, 0)
-        adds(14, 1)
-        relu_plane(14, 2)
-        for p in (0, 1, 3):
+        for p in (0, 2, 3):
             scale_plane(13, p, tile0)
+        for b in range(2):
+            for i in range(2):
+                add_fut(14, i, b)
+                main(15, i, b)
+            relu_pair(14, b)
         weigh_skip(13)
-        quantize_h(15)
+        weigh_on_tensor(13, 1, [0, 2, 3])
         skip(15)
-        mains(15)
-        joined = hg[15].bitcast(F32)
-        join(12, joined)
-        store(12, joined)
+        join(12, unit(12, 0))
+        store(12, unit(12, 0))
         sums(13, 0, 2, tile0)
         join(13, unit(13, 0, tile0), tile0)
         store(13, unit(13, 0, tile0), tile0)
-        relu_pair(14, 0)
-        relu_plane(14, 3)
-        weigh_skip(14)
-        add_part(13, 1)
-        store(13, plane(13, 2, tile1), tile1)
-        weigh_on_tensor(14, 1, [0, 1, 3])
+        weigh_on_tensor(14, 1, [0, 2, 3])
         adds(15, 0)
         relu_pair(15, 0)
         adds(15, 1)
-        relu_plane(15, 3, tile0)
         relu_plane(15, 2)
-        relu_plane(15, 3, tile1)
-        weigh_on_tensor(15, 0, [0, 1, 3])
-        weigh(14, 0, tile0, 2)
-        weigh(15, 0, tile1, None)
-        weigh(14, 1, tile0, 2)
+        relu_plane(15, 3)
+        weigh_skip(14)
+        add_part(13, 1)
+        store(13, plane(13, 1, tile1), tile1)
+        weigh_skip(15)
+        weigh(14, 0, tile0, 1)
+        weigh(15, 0, both, 1)
+        weigh(14, 2, tile0, 1)
         add_part(14, 1)
-        store(14, plane(14, 2, tile1), tile1)
-        weigh(14, 3, tile0, 2)
-        store(14, plane(14, 2, tile0), tile0)
-        weigh(15, 1, tile1, 0)
-        weigh(15, 2, tile0, None)
-        weigh(15, 2, tile1, 0)
-        add_part(15, 0)
-        store(15, plane(15, 2, tile0), tile0)
-        weigh(15, 3, tile1, 0)
-        store(15, plane(15, 0, tile1), tile1)
+        store(14, plane(14, 1, tile1), tile1)
+        weigh(15, 2, both, 1)
+        weigh(14, 3, tile0, 1)
+        store(14, plane(14, 1, tile0), tile0)
+        weigh(15, 3, tile0, 1)
+        store(15, plane(15, 1, tile0), tile0)
+        weigh(15, 3, tile1, 1)
+        store(15, plane(15, 1, tile1), tile1)

@@ -39,21 +39,21 @@ def tile_tideresidualencodertemporaldecoder_t_kernel(
         psum = ctx.enter_context(tc.psum_pool(name="psum", bufs=1))
         ctx.enter_context(tc.manual_schedule())
 
-        x_view = x_bytes.rearrange("(s p i) k -> p s (i k)", p=P, i=2)
-        fut_view = fut.rearrange("(s p i) q j -> p s i (q j)", p=P, i=2)
-        out_view = out.rearrange("(s p i) j -> p s i j", p=P, i=2)
+        x_view = x_bytes.rearrange("(g p s i) k -> p g s (i k)", p=P, s=4, i=2)
+        fut_view = fut.rearrange("(g p s i) q j -> p g s i (q j)", p=P, s=4, i=2)
+        out_view = out.rearrange("(g p s i) j -> p g s i j", p=P, s=4, i=2)
 
         x_in, fut_in = {}, {}
 
         def load_x(first, count):
             t = keep.tile([P, count, 2 * L], U8, name=f"xbytes{first}", align_bytes=64)
-            nc.sync.dma_start(out=t[:], in_=x_view[:, first : first + count, :])
+            nc.sync.dma_start(out=t[:], in_=x_view[:, first // 4, first % 4 : first % 4 + count, :])
             for j in range(count):
                 x_in[first + j] = t[:, j, :].bitcast(FP8)
 
         def load_fut(s):
             fut_in[s] = work.tile([P, 2, PH], BF16, name="fut_in", bufs=FUT_AHEAD + 1)
-            nc.sync.dma_start(out=fut_in[s][:], in_=fut_view[:, s, :, :])
+            nc.sync.dma_start(out=fut_in[s][:], in_=fut_view[:, s // 4, s % 4, :, :])
 
         def load_w(name, w, cols):
             t = keep.tile([P, 4, cols.stop - cols.start], BF16, name=name)
@@ -68,15 +68,17 @@ def tile_tideresidualencodertemporaldecoder_t_kernel(
         halves = [slice(0, 512), slice(512, 1024)]
         load_x(0, 1)
         w1_raw = load_w("w1_raw", w1, slice(0, F))
-        load_x(1, 4)
-        wsk_raw = [load_w(f"wsk_raw{b}", wsk, halves[b]) for b in range(2)]
+        load_x(1, 3)
+        wsk_all = load_w("wsk_raw", wsk, slice(0, PH))
+        wsk_raw = [wsk_all[:, :, b] for b in halves]
         w2_raw = [load_w(f"w2_raw{b}", w2, halves[b]) for b in range(2)]
         load_fut(0)
+        load_x(4, 4)
         wres_raw = load_w("wres_raw", wres, slice(0, H))
-        load_x(5, 5)
         load_fut(1)
         load_fut(2)
-        load_x(10, 6)
+        load_x(8, 4)
+        load_x(12, 4)
 
         ident = keep.tile([P, P], F32, name="ident")
         make_identity(nc, ident[:])
@@ -87,7 +89,7 @@ def tile_tideresidualencodertemporaldecoder_t_kernel(
 
         xc, xg, xq, xs, hg, hq, hs, xt, hb, rb, res, part = ({} for i in range(12))
         ring = [keep.tile([P, 8 * STEP], BF16, name=f"ring{r}", align_bytes=64) for r in range(2)]
-        zring = keep.tile([P, SLOTS * 4 * UNIT], F32, name="zring")
+        zring = keep.tile([P, (SLOTS * 4 + 3) * UNIT], F32, name="zring")
 
         def base(s):
             return (SLOTS - 1 - s % SLOTS) * 4 * UNIT
@@ -111,22 +113,18 @@ def tile_tideresidualencodertemporaldecoder_t_kernel(
             words = xc[s][:].bitcast(F32)
             for u in range(2):
                 for i in range(2):
-                    at = (2 * u + i) * P
                     second = slice(256 * i + u, 256 * (i + 1), 2)
-                    dest = xt[s][:, second] if s < LEAD else xt[s][:, at : at + P]
-                    nc.tensor.transpose(dest, words[:, second], ident[:])
+                    nc.tensor.transpose(xt[s][:, second], words[:, second], ident[:])
 
         def product(s):
             if s >= LEAD:
                 xg[s] = ring[s % 2][:, 4 * STEP : 8 * STEP]
-            elif s == 0:
-                xg[s] = group_of("wsk0")[:, 0 : 4 * STEP]
             else:
-                xg[s] = work.tile([P, 4 * STEP], BF16, name="xg", bufs=3, align_bytes=64)[:]
+                xg[s] = work.tile([P, 4 * STEP], BF16, name="xg", bufs=LEAD, align_bytes=64)[:]
             nc.vector.tensor_tensor(
-                out=xg[s].rearrange("q (n u e) -> q n u e", u=2, e=2),
-                in0=xt[s][:].bitcast(BF16).rearrange("q (n u e) -> q n u e" if s < LEAD else "q (u n e) -> q n u e", u=2, e=2),
-                in1=scale_col[:].rearrange("q (o u e) -> q o u e", o=1, u=2).to_broadcast([P, STEP, 2, 2]),
+                out=xg[s].rearrange("q (n t) -> q n t", t=4),
+                in0=xt[s][:].bitcast(BF16).rearrange("q (n t) -> q n t", t=4),
+                in1=scale_col[:].rearrange("q (o t) -> q o t", o=1).to_broadcast([P, STEP, 4]),
                 op=MULT,
             )
 
@@ -239,14 +237,20 @@ def tile_tideresidualencodertemporaldecoder_t_kernel(
                 in1=plane(s, into, rows), op0=MULT, op1=ADD,
             )
 
+        def sums_at(s):
+            return base(s + 1) + 4 * UNIT
+
         def sums(s, first, count, rows=slice(0, 2)):
             at = base(s)
             pairs = zring[:, at + 2 * first * UNIT : at + 2 * (first + count) * UNIT].rearrange("p (c o i j) -> p c o i j", o=2, i=2, j=H)
-            dest = zring[:, at + first * UNIT : at + (first + count) * UNIT].rearrange("p (c i j) -> p c i j", i=2, j=H)
+            dest = zring[:, sums_at(s) + first * UNIT : sums_at(s) + (first + count) * UNIT].rearrange("p (c i j) -> p c i j", i=2, j=H)
             nc.gpsimd.tensor_tensor(out=dest[:, :, rows, :], in0=pairs[:, :, 0, rows, :], in1=pairs[:, :, 1, rows, :], op=ADD)
 
-        def join(s, dest, rows=slice(0, 2)):
-            nc.gpsimd.tensor_tensor(out=dest, in0=unit(s, 0, rows), in1=unit(s, 1, rows), op=ADD)
+        def join_last(s):
+            gap = 4 * UNIT + H
+            first = zring[:, base(s) : base(s) + 2 * gap].rearrange("p (c x) -> p c x", c=2)[:, :, 0:H]
+            second = zring[:, base(s) + UNIT : base(s) + UNIT + 2 * gap].rearrange("p (c x) -> p c x", c=2)[:, :, 0:H]
+            nc.gpsimd.tensor_tensor(out=first, in0=first, in1=second, op=ADD)
 
         def weigh_on_tensor(s, i, planes):
             if s not in part:
@@ -262,7 +266,7 @@ def tile_tideresidualencodertemporaldecoder_t_kernel(
             nc.vector.tensor_tensor(out=plane(s, 1, rows), in0=part[s][:], in1=plane(s, 1, rows), op=ADD)
 
         def store(s, source, rows=slice(0, 2)):
-            nc.sync.dma_start(out=out_view[:, s, rows, :], in_=source.rearrange("p (i j) -> p i j", j=H))
+            nc.sync.dma_start(out=out_view[:, s // 4, s % 4, rows, :], in_=source.rearrange("p (i j) -> p i j", j=H))
 
         groups = {}
 
@@ -304,9 +308,9 @@ def tile_tideresidualencodertemporaldecoder_t_kernel(
         vp_f = keep.tile([P, P_DEC], F32, name="vp_f")
         vp_diag = keep.tile([P, P_DEC, P], F32, name="vp_diag")
         vbank = psum.tile([P, P_DEC], F32, name="vbank", tag="hb", bufs=2)
-        nc.tensor.matmul(out=vbank[:], lhsT=ones_bf[:], rhs=vp_bf[:], start=True, stop=True)
         cast(0)
         transposes(0)
+        nc.tensor.matmul(out=vbank[:], lhsT=ones_bf[:], rhs=vp_bf[:], start=True, stop=True)
         nc.vector.tensor_copy(
             out=group_of("w1")[:].rearrange("p (t m j) -> p m j t", t=4, j=4),
             in_=w1_raw.rearrange("p j (m t) -> p m j t", t=4),
@@ -316,14 +320,14 @@ def tile_tideresidualencodertemporaldecoder_t_kernel(
         cast(2)
         transposes(2, "res")
         cast(3)
-        nc.scalar.copy(out=vp_f[:], in_=vbank[:])
         product(0)
+        nc.vector.tensor_copy(out=vp_f[:], in_=vbank[:])
         transposes(3)
         w1_q, w1_s = quantize("w1", groups["w1"][:], 1)
         quantize_x(0)
         hidden(0)
-        cast(4)
-        weave_on_gpsimd(group_of("wsk0")[:], wsk_raw[0])
+        groups["wsk0"] = groups["w1"]
+        weave_on_gpsimd(groups["wsk0"][:], wsk_raw[0])
         weave_on_scalar(group_of("wsk1")[:], wsk_raw[1])
         product(1)
         product(2)
@@ -347,9 +351,10 @@ def tile_tideresidualencodertemporaldecoder_t_kernel(
         main(0, 1, 0)
         relu_h(1)
         empty_w("w21", 0)
-        quantize_h(1)
+        cast(4)
         w2_q[1], w2_s[1] = quantize("w21", groups["w21"][:], 1)
-        wres_g = hg[1]
+        quantize_h(1)
+        wres_g = groups["w21"][:, 0 : 4 * H]
         weave_on_gpsimd(wres_g, wres_raw)
         hidden(2)
         main(0, 0, 1)
@@ -369,14 +374,9 @@ def tile_tideresidualencodertemporaldecoder_t_kernel(
                     main(s, i, b)
 
         def sums_and_store(s):
-            if s % SLOTS:
-                sums(s, 0, 3)
-            else:
-                sums(s, 0, 2)
-                if s:
-                    join(s - 1, unit(s, 2))
+            sums(s, 0, 3 if s else 2)
             if s:
-                store(s - 1, unit(s, 2))
+                store(s - 1, zring[:, sums_at(s) + 2 * UNIT : sums_at(s) + 3 * UNIT])
 
         both, tile0, tile1 = slice(0, 2), slice(0, 1), slice(1, 2)
         for s in range(STEPS - LEAD):
@@ -451,11 +451,11 @@ def tile_tideresidualencodertemporaldecoder_t_kernel(
         weigh_skip(13)
         weigh_on_tensor(13, 1, [0, 2, 3])
         skip(15)
-        join(12, unit(12, 0))
-        store(12, unit(12, 0))
-        sums(13, 0, 2, tile0)
-        join(13, unit(13, 0, tile0), tile0)
+        sums(13, 0, 3, tile0)
+        store(12, unit(13, 2, tile0), tile0)
+        join_last(13)
         store(13, unit(13, 0, tile0), tile0)
+        store(12, unit(12, 0, tile1), tile1)
         weigh_on_tensor(14, 1, [0, 2, 3])
         adds(15, 0)
         relu_pair(15, 0)

@@ -122,10 +122,7 @@ def tile_tideresidualencodertemporaldecoder_t_kernel(
             else:
                 xg[s] = work.tile([P, 4 * STEP], BF16, name="xg", bufs=LEAD, align_bytes=64)[:]
             nc.vector.tensor_tensor(
-                out=xg[s].rearrange("q (n t) -> q n t", t=4),
-                in0=xt[s][:].bitcast(BF16).rearrange("q (n t) -> q n t", t=4),
-                in1=scale_col[:].rearrange("q (o t) -> q o t", o=1).to_broadcast([P, STEP, 4]),
-                op=MULT,
+                out=xg[s], in0=xt[s][:].bitcast(BF16), in1=scale_all[:], op=MULT
             )
 
         def quantize(name, source, bufs):
@@ -310,11 +307,16 @@ def tile_tideresidualencodertemporaldecoder_t_kernel(
         vbank = psum.tile([P, P_DEC], F32, name="vbank", tag="hb", bufs=2)
         cast(0)
         transposes(0)
-        nc.tensor.matmul(out=vbank[:], lhsT=ones_bf[:], rhs=vp_bf[:], start=True, stop=True)
+        scale_all = keep.tile([P, 4 * STEP], F32, name="scale_all")
         nc.vector.tensor_copy(
-            out=group_of("w1")[:].rearrange("p (t m j) -> p m j t", t=4, j=4),
-            in_=w1_raw.rearrange("p j (m t) -> p m j t", t=4),
+            out=scale_all[:].rearrange("q (n t) -> q n t", t=4),
+            in_=scale_col[:].rearrange("q (o t) -> q o t", o=1).to_broadcast([P, STEP, 4]),
         )
+        nc.tensor.matmul(out=vbank[:], lhsT=ones_bf[:], rhs=vp_bf[:], start=True, stop=True)
+        w1_to = group_of("w1")[:].rearrange("p (t m j) -> p m j t", t=4, j=4)
+        w1_from = w1_raw.rearrange("p j (m t) -> p m j t", t=4)
+        nc.vector.tensor_copy(out=w1_to[:, 0:80], in_=w1_from[:, 0:80])
+        nc.scalar.copy(out=w1_to[:, 80:P], in_=w1_from[:, 80:P])
         cast(1)
         transposes(1, "rb", 4)
         cast(2)
@@ -352,8 +354,8 @@ def tile_tideresidualencodertemporaldecoder_t_kernel(
         relu_h(1)
         empty_w("w21", 0)
         cast(4)
-        w2_q[1], w2_s[1] = quantize("w21", groups["w21"][:], 1)
         quantize_h(1)
+        w2_q[1], w2_s[1] = quantize("w21", groups["w21"][:], 1)
         wres_g = groups["w21"][:, 0 : 4 * H]
         weave_on_gpsimd(wres_g, wres_raw)
         hidden(2)
@@ -460,21 +462,24 @@ def tile_tideresidualencodertemporaldecoder_t_kernel(
         adds(15, 0)
         relu_pair(15, 0)
         adds(15, 1)
-        relu_plane(15, 2)
-        relu_plane(15, 3)
+        relu_plane(15, 2, tile0)
+        relu_plane(15, 3, tile0)
+        relu_plane(15, 2, tile1)
+        relu_plane(15, 3, tile1)
+        weigh_on_tensor(15, 0, [0, 2, 3])
         weigh_skip(14)
         add_part(13, 1)
         store(13, plane(13, 1, tile1), tile1)
         weigh_skip(15)
         weigh(14, 0, tile0, 1)
-        weigh(15, 0, both, 1)
-        weigh(14, 2, tile0, 1)
+        weigh(15, 0, tile1, 1)
         add_part(14, 1)
         store(14, plane(14, 1, tile1), tile1)
-        weigh(15, 2, both, 1)
+        weigh(14, 2, tile0, 1)
+        weigh(15, 2, tile1, 1)
         weigh(14, 3, tile0, 1)
         store(14, plane(14, 1, tile0), tile0)
-        weigh(15, 3, tile0, 1)
-        store(15, plane(15, 1, tile0), tile0)
         weigh(15, 3, tile1, 1)
         store(15, plane(15, 1, tile1), tile1)
+        add_part(15, 0)
+        store(15, plane(15, 1, tile0), tile0)

@@ -26,6 +26,7 @@ LEAD = 4
 FUT_AHEAD = 3
 UNIT = 2 * H
 SLOTS = 8
+WARM_UPS = 6
 PLACE = (0, 2, 1, 3)
 
 
@@ -305,6 +306,12 @@ def tile_tideresidualencodertemporaldecoder_t_kernel(
         vp_f = keep.tile([P, P_DEC], F32, name="vp_f")
         vp_diag = keep.tile([P, P_DEC, P], F32, name="vp_diag")
         vbank = psum.tile([P, P_DEC], F32, name="vbank", tag="hb", bufs=2)
+        warm_out = psum.tile([P, 4, P], F32, name="warm_out", tag="rb", bufs=4)
+        for w in range(WARM_UPS):
+            nc.tensor.matmul(
+                out=warm_out[:], lhsT=ones_bf[:],
+                rhs=ones_bf[:].rearrange("p (o c) -> p o c", o=1).to_broadcast([P, 4, P]), start=True, stop=True,
+            )
         cast(0)
         transposes(0)
         scale_all = keep.tile([P, 4 * STEP], F32, name="scale_all")

@@ -22,12 +22,10 @@ RELU = mybir.ActivationFunctionType.Relu
 P = 128
 STEP = 256
 STEPS = N // STEP
-LEAD = 4
-FUT_AHEAD = 3
 UNIT = 2 * H
-SLOTS = 8
+SLOTS = 6
 WARM_UPS = 6
-PLACE = (0, 2, 1, 3)
+SHARE = 128
 
 
 def tile_tideresidualencodertemporaldecoder_t_kernel(
@@ -43,8 +41,11 @@ def tile_tideresidualencodertemporaldecoder_t_kernel(
         x_view = x_bytes.rearrange("(g p s i) k -> p g s (i k)", p=P, s=4, i=2)
         fut_view = fut.rearrange("(g p s i) q j -> p g s i (q j)", p=P, s=4, i=2)
         out_view = out.rearrange("(g p s i) j -> p g s i j", p=P, s=4, i=2)
+        halves = [slice(0, 512), slice(512, 1024)]
+        both, tile0, tile1 = slice(0, 2), slice(0, 1), slice(1, 2)
 
-        x_in, fut_in = {}, {}
+        x_in, fut_in, raw, woven, wq, ws = ({} for i in range(6))
+        xc, xg, xq, xs, hg, hq, hs, xt, hb, rb, res, part, banks = ({} for i in range(13))
 
         def load_x(first, count):
             t = keep.tile([P, count, 2 * L], U8, name=f"xbytes{first}", align_bytes=64)
@@ -53,57 +54,27 @@ def tile_tideresidualencodertemporaldecoder_t_kernel(
                 x_in[first + j] = t[:, j, :].bitcast(FP8)
 
         def load_fut(s):
-            fut_in[s] = work.tile([P, 2, PH], BF16, name="fut_in", bufs=FUT_AHEAD + 1)
+            fut_in[s] = work.tile([P, 2, PH], BF16, name="fut_in", bufs=4)
             nc.sync.dma_start(out=fut_in[s][:], in_=fut_view[:, s // 4, s % 4, :, :])
 
         def load_w(name, w, cols):
-            t = keep.tile([P, 4, cols.stop - cols.start], BF16, name=name)
+            t = keep.tile([P, 4, cols.stop - cols.start], BF16, name=name + "_raw")
             nc.sync.dma_start(out=t[:], in_=w.rearrange("(p j) c -> p j c", j=4)[:, :, cols])
-            return t[:]
+            raw[name] = t[:]
 
-        scale_col = keep.tile([P, 4], F32, name="scale_col")
-        nc.scalar.dma_start(out=scale_col[:], in_=x_scale.rearrange("o (n c) -> (o n) c", c=4))
-        vp_bf = keep.tile([P, P_DEC], BF16, name="vp_bf")
-        nc.vector.memset(vp_bf[:], 0.0)
-        nc.scalar.dma_start(out=vp_bf[0:1, :], in_=vp.rearrange("(o q) -> o q", o=1))
-        halves = [slice(0, 512), slice(512, 1024)]
-        load_x(0, 1)
-        w1_raw = load_w("w1_raw", w1, slice(0, F))
-        load_x(1, 3)
-        wsk_all = load_w("wsk_raw", wsk, slice(0, PH))
-        wsk_raw = [wsk_all[:, :, b] for b in halves]
-        w2_raw = [load_w(f"w2_raw{b}", w2, halves[b]) for b in range(2)]
-        load_fut(0)
-        load_x(4, 4)
-        wres_raw = load_w("wres_raw", wres, slice(0, H))
-        load_fut(1)
-        load_fut(2)
-        load_x(8, 4)
-        load_x(12, 4)
-
-        ident = keep.tile([P, P], F32, name="ident")
-        make_identity(nc, ident[:])
-        ident_bf = keep.tile([P, P], BF16, name="ident_bf")
-        nc.scalar.activation(out=ident_bf[:], in_=ident[:], func=RELU)
-        ones_bf = keep.tile([P, P], BF16, name="ones_bf")
-        nc.vector.memset(ones_bf[:], 1.0)
-
-        xc, xg, xq, xs, hg, hq, hs, xt, hb, rb, res, part = ({} for i in range(12))
         ring = [keep.tile([P, 8 * STEP], BF16, name=f"ring{r}", align_bytes=64) for r in range(2)]
         zring = keep.tile([P, (SLOTS * 4 + 3) * UNIT], F32, name="zring")
 
         def base(s):
             return (SLOTS - 1 - s % SLOTS) * 4 * UNIT
 
-        def unit(s, place, rows=slice(0, 2)):
-            at = base(s) + place * UNIT
+        def plane(s, p, rows=both):
+            at = base(s) + p * UNIT
             return zring[:, at + rows.start * H : at + rows.stop * H]
 
-        def plane(s, p, rows=slice(0, 2)):
-            return unit(s, PLACE[p], rows)
-
-        def pair(s, b):
-            return zring[:, base(s) : base(s) + 4 * UNIT].rearrange("p (q b c) -> p q b c", q=2, b=2)[:, :, b, :]
+        def pair(s, b, rows=both):
+            at = base(s) + 2 * b * UNIT
+            return zring[:, at : at + 2 * UNIT].rearrange("p (q i j) -> p q i j", q=2, i=2)[:, :, rows, :]
 
         def cast(s):
             xc[s] = work.tile([P, 2 * L], BF16, name="xc", bufs=5)
@@ -117,13 +88,13 @@ def tile_tideresidualencodertemporaldecoder_t_kernel(
                     second = slice(256 * i + u, 256 * (i + 1), 2)
                     nc.tensor.transpose(xt[s][:, second], words[:, second], ident[:])
 
-        def product(s):
-            if s >= LEAD:
-                xg[s] = ring[s % 2][:, 4 * STEP : 8 * STEP]
-            else:
-                xg[s] = work.tile([P, 4 * STEP], BF16, name="xg", bufs=LEAD, align_bytes=64)[:]
+        def product(s, dest):
+            xg[s] = dest
             nc.vector.tensor_tensor(
-                out=xg[s], in0=xt[s][:].bitcast(BF16), in1=scale_all[:], op=MULT
+                out=dest.rearrange("q (n t) -> q n t", t=4),
+                in0=xt[s][:].bitcast(BF16).rearrange("q (n t) -> q n t", t=4),
+                in1=scale_col[:].rearrange("q (o t) -> q o t", o=1).to_broadcast([P, STEP, 4]),
+                op=MULT,
             )
 
         def quantize(name, source, bufs):
@@ -133,100 +104,106 @@ def tile_tideresidualencodertemporaldecoder_t_kernel(
             nc.vector.quantize_mx(out=codes[:].bitcast(FP8X4), scales=scales[:], in_=source)
             return codes, scales
 
-        def quantize_x(s):
-            xq[s], xs[s] = quantize("x", xg[s], 4)
+        def quantize_w(name):
+            wq[name], ws[name] = quantize(name, woven[name], 1)
 
-        def quantize_h(s):
-            hq[s], hs[s] = quantize("h", hg[s], 3)
+        def quantize_acts(source, *what):
+            codes, scales = quantize(f"acts{len(what)}", source, {1: 8, 2: 6}[len(what)])
+            for n, (kind, s) in enumerate(what):
+                cols = slice(n * STEP, (n + 1) * STEP)
+                if kind == "x":
+                    xq[s], xs[s] = codes[:, cols], scales[:, cols]
+                else:
+                    hq[s], hs[s] = codes[:, cols], scales[:, cols]
 
-        def quantize_both(s):
-            codes, scales = quantize("both", ring[s % 2][:], 6)
-            hq[s + 2], hs[s + 2] = codes[:, 0:STEP], scales[:, 0:STEP]
-            if s + LEAD < STEPS:
-                xq[s + LEAD], xs[s + LEAD] = codes[:, STEP : 2 * STEP], scales[:, STEP : 2 * STEP]
-            else:
-                hq[s + 3], hs[s + 3] = codes[:, STEP : 2 * STEP], scales[:, STEP : 2 * STEP]
-
-        def hidden(s):
+        def hidden(s, tag="hb", bufs=2):
             for i in range(2):
-                hb[s, i] = psum.tile([P, 512], F32, name="hb", bufs=2)
+                hb[s, i] = psum.tile([P, 512], F32, name="hb", tag=tag, bufs=bufs)
                 cols = slice(i * P, i * P + P)
                 for t in range(4):
                     chans = slice(t * P, t * P + P)
                     nc.tensor.matmul_mx(
                         out=hb[s, i][:, chans],
-                        lhsT=w1_q[:, chans].bitcast(FP8X4), lhsT_scale=w1_s[:, chans],
+                        lhsT=wq["w1"][:, chans].bitcast(FP8X4), lhsT_scale=ws["w1"][:, chans],
                         rhs=xq[s][:, cols].bitcast(FP8X4), rhs_scale=xs[s][:, cols],
                         start=True, stop=True,
                     )
 
-        def relu_h(s):
-            if s == STEPS - 1:
-                hg[s] = ring[(s - 1) % 2][:, 4 * STEP : 8 * STEP]
-            elif s >= 2:
-                hg[s] = ring[s % 2][:, 0 : 4 * STEP]
-            else:
-                hg[s] = work.tile([P, 4 * STEP], BF16, name="hg", align_bytes=64)[:]
-            for i in range(2):
+        def relu_h(s, dest, tiles=(0, 1)):
+            hg[s] = dest
+            for i in tiles:
                 nc.scalar.activation(
-                    out=hg[s][:, 512 * i : 512 * i + 512].rearrange("m (n t) -> m n t", t=4),
+                    out=dest[:, 512 * i : 512 * i + 512].rearrange("m (n t) -> m n t", t=4),
                     in_=hb[s, i][:].rearrange("m (t n) -> m n t", t=4),
                     func=RELU,
                 )
 
-        def main(s, i, b):
+        def main_pass(s, i, b, kind, opens, tag="rb", bufs=4):
             cols = slice(i * P, i * P + P)
-            rb[s, i, b] = psum.tile([P, 512], F32, name="rb", bufs=4)
+            if opens:
+                rb[s, i, b] = psum.tile([P, 512], F32, name="rb", tag=tag, bufs=bufs)
+            codes, scales, name = (xq[s], xs[s], f"wsk{b}") if kind == "x" else (hq[s], hs[s], f"w2{b}")
             nc.tensor.matmul_mx(
                 out=rb[s, i, b][:],
-                lhsT=xq[s][:, cols].bitcast(FP8X4), lhsT_scale=xs[s][:, cols],
-                rhs=wsk_q[b][:].bitcast(FP8X4), rhs_scale=wsk_s[b][:],
-                start=True, stop=False,
-            )
-            nc.tensor.matmul_mx(
-                out=rb[s, i, b][:],
-                lhsT=hq[s][:, cols].bitcast(FP8X4), lhsT_scale=hs[s][:, cols],
-                rhs=w2_q[b][:].bitcast(FP8X4), rhs_scale=w2_s[b][:],
-                start=False, stop=True,
+                lhsT=codes[:, cols].bitcast(FP8X4), lhsT_scale=scales[:, cols],
+                rhs=wq[name][:].bitcast(FP8X4), rhs_scale=ws[name][:],
+                start=opens, stop=not opens,
             )
 
-        def skip(s, tag="res"):
-            res[s] = psum.tile([P, 512], F32, name="res", tag=tag, bufs=1)
+        def main(s, i, b, tag="rb", bufs=4):
+            main_pass(s, i, b, "x", True, tag, bufs)
+            main_pass(s, i, b, "h", False)
+
+        def skip(s, tag="res", bufs=1):
+            res[s] = psum.tile([P, 512], F32, name="res", tag=tag, bufs=bufs)
             for i in range(2):
                 cols = slice(i * P, i * P + P)
                 nc.tensor.matmul_mx(
                     out=res[s][:, H * i : H * i + H],
                     lhsT=xq[s][:, cols].bitcast(FP8X4), lhsT_scale=xs[s][:, cols],
-                    rhs=wres_q[:].bitcast(FP8X4), rhs_scale=wres_s[:],
+                    rhs=wq["wres"][:].bitcast(FP8X4), rhs_scale=ws["wres"][:],
                     start=True, stop=True,
                 )
 
         def add_fut(s, i, b):
             nc.vector.tensor_tensor(
-                out=pair(s, b)[:, :, i * H : i * H + H],
+                out=pair(s, b)[:, :, i, :],
                 in0=rb[s, i, b][:].rearrange("p (q j) -> p q j", q=2),
                 in1=fut_in[s][:, i, halves[b]].rearrange("p (q j) -> p q j", q=2),
                 op=ADD,
             )
 
-        def relu_pair(s, b):
-            nc.scalar.activation(out=pair(s, b), in_=pair(s, b), func=RELU)
+        def relu_pair(s, b, rows=both):
+            nc.scalar.activation(out=pair(s, b, rows), in_=pair(s, b, rows), func=RELU)
 
-        def relu_plane(s, p, rows=slice(0, 2)):
+        def relu_plane(s, p, rows=both):
             nc.scalar.activation(out=plane(s, p, rows), in_=plane(s, p, rows), func=RELU)
 
-        def scale_plane(s, p, rows=slice(0, 2)):
+        def scale_plane(s, p, rows=both):
             nc.scalar.activation(out=plane(s, p, rows), in_=plane(s, p, rows), func=COPY, scale=vp_f[:, p : p + 1])
 
-        def relu_scale(s, p):
+        def relu_scale(s, p, rows=both):
             nc.vector.tensor_scalar(
-                out=plane(s, p), in0=plane(s, p), scalar1=0.0, scalar2=vp_f[:, p : p + 1], op0=MAX, op1=MULT
+                out=plane(s, p, rows), in0=plane(s, p, rows), scalar1=0.0, scalar2=vp_f[:, p : p + 1], op0=MAX, op1=MULT
             )
 
-        def weigh_skip(s):
-            p = 1
+        def relu_share(s):
+            at = base(s) + 2 * UNIT
+            run = zring[:, at : at + UNIT + SHARE]
+            nc.scalar.activation(out=run, in_=run, func=RELU)
+
+        def scale_share(s):
+            run = plane(s, 3)[:, 0:SHARE]
+            nc.scalar.activation(out=run, in_=run, func=COPY, scale=vp_f[:, 3:4])
+
+        def relu_scale_rest(s):
+            run = plane(s, 3)[:, SHARE:UNIT]
+            nc.vector.tensor_scalar(out=run, in0=run, scalar1=0.0, scalar2=vp_f[:, 3:4], op0=MAX, op1=MULT)
+
+        def weigh_skip(s, p=1, rows=both):
             nc.vector.scalar_tensor_tensor(
-                out=plane(s, p), in0=plane(s, p), scalar=vp_f[:, p : p + 1], in1=res[s][:], op0=MULT, op1=ADD
+                out=plane(s, p, rows), in0=plane(s, p, rows), scalar=vp_f[:, p : p + 1],
+                in1=res[s][:, rows.start * H : rows.stop * H], op0=MULT, op1=ADD,
             )
 
         def weigh(s, p, rows, into):
@@ -238,90 +215,124 @@ def tile_tideresidualencodertemporaldecoder_t_kernel(
         def sums_at(s):
             return base(s + 1) + 4 * UNIT
 
-        def sums(s, first, count, rows=slice(0, 2)):
+        def sums(s, first, count, rows=both):
             at = base(s)
             pairs = zring[:, at + 2 * first * UNIT : at + 2 * (first + count) * UNIT].rearrange("p (c o i j) -> p c o i j", o=2, i=2, j=H)
             dest = zring[:, sums_at(s) + first * UNIT : sums_at(s) + (first + count) * UNIT].rearrange("p (c i j) -> p c i j", i=2, j=H)
             nc.gpsimd.tensor_tensor(out=dest[:, :, rows, :], in0=pairs[:, :, 0, rows, :], in1=pairs[:, :, 1, rows, :], op=ADD)
 
-        def join_last(s):
-            gap = 4 * UNIT + H
-            first = zring[:, base(s) : base(s) + 2 * gap].rearrange("p (c x) -> p c x", c=2)[:, :, 0:H]
-            second = zring[:, base(s) + UNIT : base(s) + UNIT + 2 * gap].rearrange("p (c x) -> p c x", c=2)[:, :, 0:H]
-            nc.gpsimd.tensor_tensor(out=first, in0=first, in1=second, op=ADD)
+        def add_on_gpsimd(dest, first, second):
+            nc.gpsimd.tensor_tensor(out=dest, in0=first, in1=second, op=ADD)
 
-        def weigh_on_tensor(s, i, planes):
-            if s not in part:
-                part[s] = psum.tile([P, H], F32, name="part", tag="hb", bufs=2)
+        def add_on_vector(dest, first, second):
+            nc.vector.tensor_tensor(out=dest, in0=first, in1=second, op=ADD)
+
+        def weigh_on_tensor(s, i, planes, opens, closes, tag="hb", bufs=2):
+            if opens:
+                part[s, i] = psum.tile([P, H], F32, name="part", tag=tag, bufs=bufs)
             for p in planes:
                 nc.tensor.matmul(
-                    out=part[s][:], lhsT=vp_diag[:, p, :], rhs=plane(s, p, slice(i, i + 1)),
-                    start=(p == 0), stop=(p == 3),
+                    out=part[s, i][:], lhsT=vp_diag[:, p, :], rhs=plane(s, p, slice(i, i + 1)),
+                    start=(opens and p == planes[0]), stop=(closes and p == planes[-1]),
                 )
 
-        def add_part(s, i):
-            rows = slice(i, i + 1)
-            nc.vector.tensor_tensor(out=plane(s, 1, rows), in0=part[s][:], in1=plane(s, 1, rows), op=ADD)
+        def weigh_both_on_tensor(s, p, opens, closes):
+            if opens:
+                part[s] = psum.tile([P, UNIT], F32, name="part", tag="hb", bufs=2)
+            nc.tensor.matmul(out=part[s][:], lhsT=vp_diag[:, p, :], rhs=plane(s, p), start=opens, stop=closes)
 
-        def store(s, source, rows=slice(0, 2)):
+        def store(s, source, rows=both):
             nc.sync.dma_start(out=out_view[:, s // 4, s % 4, rows, :], in_=source.rearrange("p (i j) -> p i j", j=H))
 
-        groups = {}
+        def woven_tile(name, width=512):
+            woven[name] = keep.tile([P, 4 * width], BF16, name=name + "_g", align_bytes=64)[:]
+            return woven[name]
 
-        def group_of(name, width=512):
-            if name not in groups:
-                groups[name] = keep.tile([P, 4 * width], BF16, name=name + "_g", align_bytes=64)
-            return groups[name]
-
-        banks = {}
-
-        def fill_w(name, raw, half):
-            views = raw.rearrange("p j (t m) -> p t m j", t=4)
-            banks[name, half] = psum.tile([P, 2, 512], BF16, name="wbank", tag="rb", bufs=4)
+        def fill_w(name, half, tag="rb", bufs=4):
+            views = raw[name].rearrange("p j (t m) -> p t m j", m=P)
+            banks[name, half] = psum.tile([P, 2, 512], BF16, name="wbank", tag=tag, bufs=bufs)
             for n in range(2):
                 nc.tensor.matmul(out=banks[name, half][:, n, :], lhsT=ident_bf[:], rhs=views[:, 2 * half + n], start=True, stop=True)
 
         def empty_w(name, half):
-            dst = group_of(name)[:, 1024 * half : 1024 * half + 1024]
+            dst = woven[name][:, 1024 * half : 1024 * half + 1024]
             nc.scalar.copy(out=dst, in_=banks[name, half][:].rearrange("p n c -> p (n c)"))
 
-        def weave_on_gpsimd(dst, raw):
+        def weave_on_gpsimd(name):
             nc.gpsimd.tensor_scalar(
-                out=dst.rearrange("p (c j) -> p c j", j=4), in0=raw.rearrange("p j c -> p c j"),
+                out=woven[name].rearrange("p (c j) -> p c j", j=4), in0=raw[name].rearrange("p j c -> p c j"),
                 scalar1=1.0, scalar2=0.0, op0=MULT, op1=ADD,
             )
 
-        def weave_on_vector(dst, raw):
-            nc.vector.tensor_copy(
-                out=dst.rearrange("p (c i j) -> p c j i", i=4, j=4), in_=raw.rearrange("p j (c i) -> p c j i", i=4)
-            )
+        def weave_views(name, cols):
+            dst = woven[name][:, 4 * cols.start : 4 * cols.stop].rearrange("p (c i j) -> p c j i", i=4, j=4)
+            return dst, raw[name][:, :, cols].rearrange("p j (c i) -> p c j i", i=4)
 
-        def weave_on_scalar(dst, raw):
-            nc.scalar.copy(
-                out=dst.rearrange("p (c i j) -> p c j i", i=4, j=4), in_=raw.rearrange("p j (c i) -> p c j i", i=4)
-            )
+        def weave_on_vector(name, cols):
+            dst, src = weave_views(name, cols)
+            nc.vector.tensor_copy(out=dst, in_=src)
 
-        wsk_q, wsk_s, w2_q, w2_s = {}, {}, {}, {}
+        def weave_on_scalar(name, cols):
+            dst, src = weave_views(name, cols)
+            nc.scalar.copy(out=dst, in_=src)
 
+        def own_tile(name, bufs):
+            return work.tile([P, 4 * STEP], BF16, name=name, bufs=bufs, align_bytes=64)[:]
+
+        def adds(s, b):
+            for i in range(2):
+                add_fut(s, i, b)
+
+        def mains(s, b, tag="rb", bufs=4):
+            for i in range(2):
+                main(s, i, b, tag, bufs)
+
+        def sums_and_store(s):
+            sums(s, 0, 3 if s else 2)
+            if s:
+                store(s - 1, zring[:, sums_at(s) + 2 * UNIT : sums_at(s) + 3 * UNIT])
+
+
+        vp_bf = keep.tile([P, P_DEC], BF16, name="vp_bf")
+        nc.vector.memset(vp_bf[:], 0.0)
+        ones_bf = keep.tile([P, P], BF16, name="ones_bf")
+        nc.vector.memset(ones_bf[:], 1.0)
+        scale_col = keep.tile([P, 4], F32, name="scale_col")
+        nc.scalar.dma_start(out=scale_col[:], in_=x_scale.rearrange("o (n c) -> (o n) c", c=4))
+        nc.scalar.dma_start(out=vp_bf[0:1, :], in_=vp.rearrange("(o q) -> o q", o=1))
+        load_x(0, 1)
+        load_w("w1", w1, slice(0, F))
+        load_x(1, 3)
+        load_w("wsk", wsk, slice(0, PH))
+        raw["wsk0"], raw["wsk1"] = raw["wsk"][:, :, halves[0]], raw["wsk"][:, :, halves[1]]
+        load_w("w20", w2, halves[0])
+        load_w("w21", w2, halves[1])
+        load_fut(0)
+        load_x(4, 4)
+        load_w("wres", wres, slice(0, H))
+        load_fut(1)
+        load_fut(2)
+        load_x(8, 4)
+        load_x(12, 4)
+        ident = keep.tile([P, P], F32, name="ident")
+        make_identity(nc, ident[:])
+        ident_bf = keep.tile([P, P], BF16, name="ident_bf")
+        nc.scalar.activation(out=ident_bf[:], in_=ident[:], func=RELU)
         vp_f = keep.tile([P, P_DEC], F32, name="vp_f")
         vp_diag = keep.tile([P, P_DEC, P], F32, name="vp_diag")
-        vbank = psum.tile([P, P_DEC], F32, name="vbank", tag="hb", bufs=2)
         warm_out = psum.tile([P, 4, P], F32, name="warm_out", tag="rb", bufs=4)
         for w in range(WARM_UPS):
             nc.tensor.matmul(
                 out=warm_out[:], lhsT=ones_bf[:],
                 rhs=ones_bf[:].rearrange("p (o c) -> p o c", o=1).to_broadcast([P, 4, P]), start=True, stop=True,
             )
+
+        vbank = psum.tile([P, P_DEC], F32, name="vbank", tag="hb", bufs=2)
         cast(0)
         transposes(0)
-        scale_all = keep.tile([P, 4 * STEP], F32, name="scale_all")
-        nc.vector.tensor_copy(
-            out=scale_all[:].rearrange("q (n t) -> q n t", t=4),
-            in_=scale_col[:].rearrange("q (o t) -> q o t", o=1).to_broadcast([P, STEP, 4]),
-        )
         nc.tensor.matmul(out=vbank[:], lhsT=ones_bf[:], rhs=vp_bf[:], start=True, stop=True)
-        w1_to = group_of("w1")[:].rearrange("p (t m j) -> p m j t", t=4, j=4)
-        w1_from = w1_raw.rearrange("p j (m t) -> p m j t", t=4)
+        w1_to = woven_tile("w1").rearrange("p (t m j) -> p m j t", t=4, j=4)
+        w1_from = raw["w1"].rearrange("p j (m t) -> p m j t", t=4)
         nc.vector.tensor_copy(out=w1_to[:, 0:80], in_=w1_from[:, 0:80])
         nc.scalar.copy(out=w1_to[:, 80:P], in_=w1_from[:, 80:P])
         cast(1)
@@ -329,164 +340,187 @@ def tile_tideresidualencodertemporaldecoder_t_kernel(
         cast(2)
         transposes(2, "res")
         cast(3)
-        product(0)
+        product(0, own_tile("xg", 4))
         nc.vector.tensor_copy(out=vp_f[:], in_=vbank[:])
         transposes(3)
-        w1_q, w1_s = quantize("w1", groups["w1"][:], 1)
-        quantize_x(0)
+        quantize_w("w1")
+        quantize_acts(xg[0], ("x", 0))
         hidden(0)
-        groups["wsk0"] = groups["w1"]
-        weave_on_gpsimd(groups["wsk0"][:], wsk_raw[0])
-        weave_on_scalar(group_of("wsk1")[:], wsk_raw[1])
-        product(1)
-        product(2)
-        product(3)
-        relu_h(0)
-        fill_w("w20", w2_raw[0], 0)
-        fill_w("w20", w2_raw[0], 1)
-        quantize_x(1)
-        quantize_x(2)
-        quantize_x(3)
+        woven["wsk0"] = woven["w1"]
+        weave_on_gpsimd("wsk0")
+        woven_tile("wsk1")
+        weave_on_scalar("wsk1", slice(0, 512))
+        for s in (1, 2, 3):
+            product(s, own_tile("xg", 4))
+        relu_h(0, own_tile("hg", 2))
+        woven_tile("w20")
+        woven_tile("w21")
+        fill_w("w20", 0)
+        fill_w("w20", 1)
+        for s in (1, 2, 3):
+            quantize_acts(xg[s], ("x", s))
         hidden(1)
-        fill_w("w21", w2_raw[1], 0)
+        fill_w("w21", 0)
         empty_w("w20", 0)
         empty_w("w20", 1)
-        wsk_q[0], wsk_s[0] = quantize("wsk0", groups["wsk0"][:], 1)
-        wsk_q[1], wsk_s[1] = quantize("wsk1", groups["wsk1"][:], 1)
-        quantize_h(0)
-        w2_q[0], w2_s[0] = quantize("w20", groups["w20"][:], 1)
-        weave_on_vector(group_of("w21")[:, 1024:2048], w2_raw[1][:, :, 256:512])
-        main(0, 0, 0)
-        main(0, 1, 0)
-        relu_h(1)
+        quantize_w("wsk0")
+        quantize_w("wsk1")
+        quantize_acts(hg[0], ("h", 0))
+        quantize_w("w20")
+        weave_on_vector("w21", slice(256, 512))
+        mains(0, 0)
+        relu_h(1, own_tile("hg", 2))
         empty_w("w21", 0)
         cast(4)
-        quantize_h(1)
-        w2_q[1], w2_s[1] = quantize("w21", groups["w21"][:], 1)
-        wres_g = groups["w21"][:, 0 : 4 * H]
-        weave_on_gpsimd(wres_g, wres_raw)
+        quantize_acts(hg[1], ("h", 1))
+        quantize_w("w21")
+        woven["wres"] = woven["w21"][:, 0 : 4 * H]
+        weave_on_gpsimd("wres")
         hidden(2)
-        main(0, 0, 1)
-        main(0, 1, 1)
-        relu_h(2)
+        mains(0, 1)
+        relu_h(2, ring[0][:, 0:1024])
         transposes(4)
+        load_fut(3)
+        cast(5)
+        add_fut(0, 0, 0)
+        main(1, 0, 0)
+        add_fut(0, 1, 0)
+        relu_pair(0, 0)
+        adds(0, 1)
+        quantize_w("wres")
+        skip(0)
+        main(1, 1, 0)
+        hidden(3)
+        mains(1, 1)
+        product(4, ring[0][:, 1024:2048])
+        transposes(5)
+        relu_plane(0, 2)
+        scale_plane(0, 0)
+        scale_plane(0, 2)
+        weigh_skip(0)
+        relu_scale(0, 3)
+        relu_h(3, ring[1][:, 0:1024])
+        quantize_acts(ring[0][:], ("h", 2), ("x", 4))
+        sums_and_store(0)
 
-        def adds(s, b):
-            for i in range(2):
-                add_fut(s, i, b)
-                if s + 1 < STEPS - 2:
-                    main(s + 1, i, b)
-
-        def mains(s):
+        for s in range(1, STEPS - 5):
+            load_fut(s + 3)
+            cast(s + 5)
+            skip(s)
+            hidden(s + 3)
             for b in range(2):
                 for i in range(2):
-                    main(s, i, b)
-
-        def sums_and_store(s):
-            sums(s, 0, 3 if s else 2)
-            if s:
-                store(s - 1, zring[:, sums_at(s) + 2 * UNIT : sums_at(s) + 3 * UNIT])
-
-        both, tile0, tile1 = slice(0, 2), slice(0, 1), slice(1, 2)
-        for s in range(STEPS - LEAD):
-            load_fut(s + FUT_AHEAD)
-            if s + LEAD + 1 < STEPS:
-                cast(s + LEAD + 1)
-            else:
-                for p in (0, 2, 3):
-                    nc.scalar.activation(out=vp_diag[:, p, :], in_=ident[:], func=COPY, scale=vp_f[:, p : p + 1])
-            if s > 0:
-                skip(s)
-                hidden(s + 3)
-                adds(s, 0)
-                relu_pair(s, 0)
-                adds(s, 1)
-            else:
-                add_fut(s, 0, 0)
-                main(s + 1, 0, 0)
-                add_fut(s, 1, 0)
-                relu_pair(s, 0)
-                add_fut(s, 0, 1)
-                add_fut(s, 1, 1)
-                wres_q, wres_s = quantize("wres", wres_g, 1)
-                skip(s)
-                main(s + 1, 1, 0)
-                hidden(s + 3)
-                main(s + 1, 0, 1)
-                main(s + 1, 1, 1)
-            product(s + LEAD)
-            if s + LEAD + 1 < STEPS:
-                transposes(s + LEAD + 1)
+                    add_fut(s, i, b)
+                    main(s + 1, i, b)
+                if b == 0:
+                    relu_pair(s, 0)
+            product(s + 4, ring[s % 2][:, 1024:2048])
+            transposes(s + 5)
             relu_plane(s, 2)
             scale_plane(s, 0)
             scale_plane(s, 2)
             weigh_skip(s)
             relu_scale(s, 3)
-            relu_h(s + 3)
-            quantize_both(s)
+            relu_h(s + 3, ring[(s + 1) % 2][:, 0:1024])
+            quantize_acts(ring[s % 2][:], ("h", s + 2), ("x", s + 4))
             sums_and_store(s)
 
+        def join_last(s):
+            gap = 4 * UNIT + H
+            first = zring[:, base(s) : base(s) + 2 * gap].rearrange("p (c x) -> p c x", c=2)[:, :, 0:H]
+            second = zring[:, base(s) + UNIT : base(s) + UNIT + 2 * gap].rearrange("p (c x) -> p c x", c=2)[:, :, 0:H]
+            add_on_gpsimd(first, first, second)
+
+        def add_part(s, i):
+            rows = slice(i, i + 1)
+            add_on_vector(plane(s, 1, rows), part[s, i][:], plane(s, 1, rows))
+
+        load_fut(14)
+        skip(11)
+        hidden(14)
+        relu_h(14, ring[0][:, 0:1024], (0,))
+        for b in range(2):
+            for i in range(2):
+                add_fut(11, i, b)
+                main(12, i, b)
+            if b == 0:
+                relu_pair(11, 0)
+        relu_h(14, ring[0][:, 0:1024], (1,))
+        product(15, ring[1][:, 1024:2048])
+        relu_plane(11, 2)
+        scale_plane(11, 0)
+        scale_plane(11, 2)
+        weigh_skip(11)
+        relu_scale(11, 3)
+        quantize_acts(ring[1][:], ("h", 13), ("x", 15))
+        quantize_acts(hg[14], ("h", 14))
+        sums_and_store(11)
+        for p in (0, 2, 3):
+            nc.scalar.activation(out=vp_diag[:, p, :], in_=ident[:], func=COPY, scale=vp_f[:, p : p + 1])
         load_fut(15)
         skip(12)
         hidden(15)
-        relu_h(15)
-        adds(12, 0)
-        relu_pair(12, 0)
-        adds(12, 1)
+        relu_h(15, ring[0][:, 1024:2048])
+        for b in range(2):
+            for i in range(2):
+                add_fut(12, i, b)
+                main(13, i, b)
+            if b == 0:
+                relu_pair(12, 0)
         relu_plane(12, 2)
         scale_plane(12, 0)
         scale_plane(12, 2)
+        skip(13, "xt")
         adds(13, 0)
+        mains(14, 0)
         weigh_skip(12)
-        skip(13)
         relu_scale(12, 3)
-        quantize_both(12)
+        quantize_acts(hg[15], ("h", 15))
         sums_and_store(12)
-        main(14, 0, 0)
-        main(14, 1, 0)
+        mains(14, 1, "hb", 2)
+        skip(14)
         relu_pair(13, 0)
         adds(13, 1)
-        main(14, 0, 1)
-        main(14, 1, 1)
+        mains(15, 0)
         relu_pair(13, 1)
-        skip(14, "xt")
         for p in (0, 2, 3):
             scale_plane(13, p, tile0)
-        for b in range(2):
-            for i in range(2):
-                add_fut(14, i, b)
-                main(15, i, b)
-            relu_pair(14, b)
+        adds(14, 0)
+        mains(15, 1)
+        relu_pair(14, 0)
         weigh_skip(13)
-        weigh_on_tensor(13, 1, [0, 2, 3])
-        skip(15)
+        weigh_on_tensor(13, 1, [0, 2, 3], True, True, "xt", 1)
+        adds(14, 1)
+        relu_pair(14, 1)
         sums(13, 0, 3, tile0)
-        store(12, unit(13, 2, tile0), tile0)
+        store(12, plane(13, 2, tile0), tile0)
         join_last(13)
-        store(13, unit(13, 0, tile0), tile0)
-        store(12, unit(12, 0, tile1), tile1)
-        weigh_on_tensor(14, 1, [0, 2, 3])
+        store(13, plane(13, 0, tile0), tile0)
+        store(12, plane(12, 0, tile1), tile1)
+        for i in range(2):
+            weigh_on_tensor(14, i, [0], True, False)
         adds(15, 0)
+        weigh_skip(14)
+        skip(15)
+        for i in range(2):
+            weigh_on_tensor(14, i, [2, 3], False, True)
         relu_pair(15, 0)
         adds(15, 1)
-        relu_plane(15, 2, tile0)
-        relu_plane(15, 3, tile0)
-        relu_plane(15, 2, tile1)
-        relu_plane(15, 3, tile1)
-        weigh_on_tensor(15, 0, [0, 2, 3])
-        weigh_skip(14)
+        relu_pair(15, 1, tile0)
+        relu_pair(15, 1, tile1)
         add_part(13, 1)
         store(13, plane(13, 1, tile1), tile1)
-        weigh_skip(15)
-        weigh(14, 0, tile0, 1)
-        weigh(15, 0, tile1, 1)
+        for rows in (tile0, tile1):
+            weigh_skip(15, 1, rows)
+        for rows in (tile0, tile1):
+            weigh(15, 0, rows, 1)
+        weigh(15, 2, tile0, 1)
+        add_part(14, 0)
+        store(14, plane(14, 1, tile0), tile0)
+        weigh(15, 3, tile0, 1)
+        store(15, plane(15, 1, tile0), tile0)
+        weigh(15, 2, tile1, 1)
         add_part(14, 1)
         store(14, plane(14, 1, tile1), tile1)
-        weigh(14, 2, tile0, 1)
-        weigh(15, 2, tile1, 1)
-        weigh(14, 3, tile0, 1)
-        store(14, plane(14, 1, tile0), tile0)
         weigh(15, 3, tile1, 1)
         store(15, plane(15, 1, tile1), tile1)
-        add_part(15, 0)
-        store(15, plane(15, 1, tile0), tile0)

@@ -26,6 +26,7 @@ UNIT = 2 * H
 SLOTS = 6
 WARM_UPS = 6
 SHARE = 128
+FLAT_FROM = 5
 
 
 def tile_tideresidualencodertemporaldecoder_t_kernel(
@@ -86,14 +87,16 @@ def tile_tideresidualencodertemporaldecoder_t_kernel(
             for u in range(2):
                 for i in range(2):
                     second = slice(256 * i + u, 256 * (i + 1), 2)
-                    nc.tensor.transpose(xt[s][:, second], words[:, second], ident[:])
+                    run = slice(256 * u + P * i, 256 * u + P * i + P)
+                    nc.tensor.transpose(xt[s][:, second if s < FLAT_FROM else run], words[:, second], ident[:])
 
         def product(s, dest):
             xg[s] = dest
+            order = "q (n u e) -> q n u e" if s < FLAT_FROM else "q (u n e) -> q n u e"
             nc.vector.tensor_tensor(
-                out=dest.rearrange("q (n t) -> q n t", t=4),
-                in0=xt[s][:].bitcast(BF16).rearrange("q (n t) -> q n t", t=4),
-                in1=scale_col[:].rearrange("q (o t) -> q o t", o=1).to_broadcast([P, STEP, 4]),
+                out=dest.rearrange("q (n u e) -> q n u e", u=2, e=2),
+                in0=xt[s][:].bitcast(BF16).rearrange(order, u=2, e=2),
+                in1=scale_col[:].rearrange("q (o u e) -> q o u e", o=1, u=2).to_broadcast([P, STEP, 2, 2]),
                 op=MULT,
             )
 

@@ -25,7 +25,7 @@ STEPS = N // STEP
 UNIT = 2 * H
 SLOTS = 6
 WARM_UPS = 6
-SHARE = 128
+SHARE = 96
 FLAT_FROM = 5
 
 
@@ -419,11 +419,12 @@ def tile_tideresidualencodertemporaldecoder_t_kernel(
                     relu_pair(s, 0)
             product(s + 4, ring[s % 2][:, 1024:2048])
             transposes(s + 5)
-            relu_plane(s, 2)
+            relu_share(s)
             scale_plane(s, 0)
             scale_plane(s, 2)
+            scale_share(s)
             weigh_skip(s)
-            relu_scale(s, 3)
+            relu_scale_rest(s)
             relu_h(s + 3, ring[(s + 1) % 2][:, 0:1024])
             quantize_acts(ring[s % 2][:], ("h", s + 2), ("x", s + 4))
             sums_and_store(s)

@@ -26,7 +26,8 @@ UNIT = 2 * H
 SLOTS = 6
 WARM_UPS = 6
 SHARE = 96
-FLAT_FROM = 5
+FLAT_FROM = 4
+BY_TILE = 13
 
 
 def tile_tideresidualencodertemporaldecoder_t_kernel(
@@ -69,13 +70,15 @@ def tile_tideresidualencodertemporaldecoder_t_kernel(
         def base(s):
             return (SLOTS - 1 - s % SLOTS) * 4 * UNIT
 
+        def slot(s):
+            order = "p (i q j) -> p q i j" if s == BY_TILE else "p (q i j) -> p q i j"
+            return zring[:, base(s) : base(s) + 4 * UNIT].rearrange(order, q=P_DEC, i=2)
+
         def plane(s, p, rows=both):
-            at = base(s) + p * UNIT
-            return zring[:, at + rows.start * H : at + rows.stop * H]
+            return slot(s)[:, p, rows, :]
 
         def pair(s, b, rows=both):
-            at = base(s) + 2 * b * UNIT
-            return zring[:, at : at + 2 * UNIT].rearrange("p (q i j) -> p q i j", q=2, i=2)[:, :, rows, :]
+            return slot(s)[:, 2 * b : 2 * b + 2, rows, :]
 
         def cast(s):
             xc[s] = work.tile([P, 2 * L], BF16, name="xc", bufs=5)
@@ -196,17 +199,19 @@ def tile_tideresidualencodertemporaldecoder_t_kernel(
             nc.scalar.activation(out=run, in_=run, func=RELU)
 
         def scale_share(s):
-            run = plane(s, 3)[:, 0:SHARE]
+            at = base(s) + 3 * UNIT
+            run = zring[:, at : at + SHARE]
             nc.scalar.activation(out=run, in_=run, func=COPY, scale=vp_f[:, 3:4])
 
         def relu_scale_rest(s):
-            run = plane(s, 3)[:, SHARE:UNIT]
+            at = base(s) + 3 * UNIT
+            run = zring[:, at + SHARE : at + UNIT]
             nc.vector.tensor_scalar(out=run, in0=run, scalar1=0.0, scalar2=vp_f[:, 3:4], op0=MAX, op1=MULT)
 
         def weigh_skip(s, p=1, rows=both):
             nc.vector.scalar_tensor_tensor(
                 out=plane(s, p, rows), in0=plane(s, p, rows), scalar=vp_f[:, p : p + 1],
-                in1=res[s][:, rows.start * H : rows.stop * H], op0=MULT, op1=ADD,
+                in1=res[s][:].rearrange("p (i j) -> p i j", i=2)[:, rows, :], op0=MULT, op1=ADD,
             )
 
         def weigh(s, p, rows, into):
@@ -235,17 +240,12 @@ def tile_tideresidualencodertemporaldecoder_t_kernel(
                 part[s, i] = psum.tile([P, H], F32, name="part", tag=tag, bufs=bufs)
             for p in planes:
                 nc.tensor.matmul(
-                    out=part[s, i][:], lhsT=vp_diag[:, p, :], rhs=plane(s, p, slice(i, i + 1)),
+                    out=part[s, i][:], lhsT=vp_diag[:, p, :], rhs=plane(s, p)[:, i, :],
                     start=(opens and p == planes[0]), stop=(closes and p == planes[-1]),
                 )
 
-        def weigh_both_on_tensor(s, p, opens, closes):
-            if opens:
-                part[s] = psum.tile([P, UNIT], F32, name="part", tag="hb", bufs=2)
-            nc.tensor.matmul(out=part[s][:], lhsT=vp_diag[:, p, :], rhs=plane(s, p), start=opens, stop=closes)
-
         def store(s, source, rows=both):
-            nc.sync.dma_start(out=out_view[:, s // 4, s % 4, rows, :], in_=source.rearrange("p (i j) -> p i j", j=H))
+            nc.sync.dma_start(out=out_view[:, s // 4, s % 4, rows, :], in_=source)
 
         def woven_tile(name, width=512):
             woven[name] = keep.tile([P, 4 * width], BF16, name=name + "_g", align_bytes=64)[:]
@@ -260,6 +260,14 @@ def tile_tideresidualencodertemporaldecoder_t_kernel(
         def empty_w(name, half):
             dst = woven[name][:, 1024 * half : 1024 * half + 1024]
             nc.scalar.copy(out=dst, in_=banks[name, half][:].rearrange("p n c -> p (n c)"))
+
+        def fill_quarter(name, quarter):
+            view = raw[name].rearrange("p j (t m) -> p t m j", m=P)[:, quarter]
+            banks[name, "q"] = psum.tile([P, 512], BF16, name="wbank", tag="res", bufs=1)
+            nc.tensor.matmul(out=banks[name, "q"][:], lhsT=ident_bf[:], rhs=view, start=True, stop=True)
+
+        def empty_quarter(name, quarter):
+            nc.scalar.copy(out=woven[name][:, 512 * quarter : 512 * quarter + 512], in_=banks[name, "q"][:])
 
         def weave_on_gpsimd(name):
             nc.gpsimd.tensor_scalar(
@@ -293,7 +301,7 @@ def tile_tideresidualencodertemporaldecoder_t_kernel(
         def sums_and_store(s):
             sums(s, 0, 3 if s else 2)
             if s:
-                store(s - 1, zring[:, sums_at(s) + 2 * UNIT : sums_at(s) + 3 * UNIT])
+                store(s - 1, zring[:, sums_at(s) + 2 * UNIT : sums_at(s) + 3 * UNIT].rearrange("p (i j) -> p i j", i=2))
 
 
         vp_bf = keep.tile([P, P_DEC], BF16, name="vp_bf")
@@ -429,15 +437,8 @@ def tile_tideresidualencodertemporaldecoder_t_kernel(
             quantize_acts(ring[s % 2][:], ("h", s + 2), ("x", s + 4))
             sums_and_store(s)
 
-        def join_last(s):
-            gap = 4 * UNIT + H
-            first = zring[:, base(s) : base(s) + 2 * gap].rearrange("p (c x) -> p c x", c=2)[:, :, 0:H]
-            second = zring[:, base(s) + UNIT : base(s) + UNIT + 2 * gap].rearrange("p (c x) -> p c x", c=2)[:, :, 0:H]
-            add_on_gpsimd(first, first, second)
-
         def add_part(s, i):
-            rows = slice(i, i + 1)
-            add_on_vector(plane(s, 1, rows), part[s, i][:], plane(s, 1, rows))
+            add_on_vector(plane(s, 1)[:, i, :], part[s, i][:], plane(s, 1)[:, i, :])
 
         load_fut(14)
         skip(11)
@@ -463,6 +464,7 @@ def tile_tideresidualencodertemporaldecoder_t_kernel(
             nc.scalar.activation(out=vp_diag[:, p, :], in_=ident[:], func=COPY, scale=vp_f[:, p : p + 1])
         load_fut(15)
         skip(12)
+        skip(13, "xt")
         hidden(15)
         relu_h(15, ring[0][:, 1024:2048])
         for b in range(2):
@@ -474,7 +476,6 @@ def tile_tideresidualencodertemporaldecoder_t_kernel(
         relu_plane(12, 2)
         scale_plane(12, 0)
         scale_plane(12, 2)
-        skip(13, "xt")
         adds(13, 0)
         mains(14, 0)
         weigh_skip(12)
@@ -493,37 +494,36 @@ def tile_tideresidualencodertemporaldecoder_t_kernel(
         mains(15, 1)
         relu_pair(14, 0)
         weigh_skip(13)
-        weigh_on_tensor(13, 1, [0, 2, 3], True, True, "xt", 1)
+        skip(15, "xt")
         adds(14, 1)
+        weigh_on_tensor(13, 1, [0, 2, 3], True, True)
         relu_pair(14, 1)
-        sums(13, 0, 3, tile0)
-        store(12, plane(13, 2, tile0), tile0)
-        join_last(13)
-        store(13, plane(13, 0, tile0), tile0)
-        store(12, plane(12, 0, tile1), tile1)
-        for i in range(2):
-            weigh_on_tensor(14, i, [0], True, False)
+        blocks = zring[:, base(13) : base(13) + 8 * UNIT].rearrange("p (c o x) -> p c o x", c=2, o=4)
+        add_on_gpsimd(blocks[:, :, 0, :], blocks[:, :, 0, :], blocks[:, :, 1, :])
+        store(12, plane(12, 0))
+        add_on_gpsimd(plane(13, 0, tile0), plane(13, 0, tile0), plane(13, 1, tile0))
+        weigh_on_tensor(14, 0, [0, 2, 3], True, True)
         adds(15, 0)
         weigh_skip(14)
-        skip(15)
-        for i in range(2):
-            weigh_on_tensor(14, i, [2, 3], False, True)
+        weigh_on_tensor(14, 1, [0, 2, 3], True, True, "rb", 4)
         relu_pair(15, 0)
-        adds(15, 1)
-        relu_pair(15, 1, tile0)
-        relu_pair(15, 1, tile1)
+        add_fut(15, 0, 1)
         add_part(13, 1)
         store(13, plane(13, 1, tile1), tile1)
+        store(13, plane(13, 0, tile0), tile0)
+        add_fut(15, 1, 1)
+        relu_pair(15, 1, tile0)
+        relu_pair(15, 1, tile1)
         for rows in (tile0, tile1):
             weigh_skip(15, 1, rows)
         for rows in (tile0, tile1):
             weigh(15, 0, rows, 1)
-        weigh(15, 2, tile0, 1)
         add_part(14, 0)
         store(14, plane(14, 1, tile0), tile0)
+        for rows in (tile0, tile1):
+            weigh(15, 2, rows, 1)
         weigh(15, 3, tile0, 1)
         store(15, plane(15, 1, tile0), tile0)
-        weigh(15, 2, tile1, 1)
         add_part(14, 1)
         store(14, plane(14, 1, tile1), tile1)
         weigh(15, 3, tile1, 1)

@@ -482,6 +482,8 @@ def tile_tideresidualencodertemporaldecoder_t_kernel(
         relu_scale(12, 3)
         quantize_acts(hg[15], ("h", 15))
         sums_and_store(12)
+        add_on_gpsimd(plane(12, 0), plane(12, 0), plane(12, 1))
+        store(12, plane(12, 0))
         mains(14, 1, "hb", 2)
         skip(14)
         relu_pair(13, 0)
@@ -498,9 +500,7 @@ def tile_tideresidualencodertemporaldecoder_t_kernel(
         adds(14, 1)
         weigh_on_tensor(13, 1, [0, 2, 3], True, True)
         relu_pair(14, 1)
-        blocks = zring[:, base(13) : base(13) + 8 * UNIT].rearrange("p (c o x) -> p c o x", c=2, o=4)
-        add_on_gpsimd(blocks[:, :, 0, :], blocks[:, :, 0, :], blocks[:, :, 1, :])
-        store(12, plane(12, 0))
+        add_on_gpsimd(pair(13, 0, tile0), pair(13, 0, tile0), pair(13, 1, tile0))
         add_on_gpsimd(plane(13, 0, tile0), plane(13, 0, tile0), plane(13, 1, tile0))
         weigh_on_tensor(14, 0, [0, 2, 3], True, True)
         adds(15, 0)

from contextlib import ExitStack

import concourse.mybir as mybir
from concourse.masks import make_identity

N, L, F, H, P_DEC = 4096, 512, 512, 256, 4
PH = P_DEC * H
FLOPS = 2 * N * (L * F + F * PH + L * PH + L * H)

F32 = mybir.dt.float32
BF16 = mybir.dt.bfloat16
U32 = mybir.dt.uint32
U8 = mybir.dt.uint8
FP8 = mybir.dt.float8_e4m3fn
FP8X4 = mybir.dt.float8_e4m3fn_x4
ADD = mybir.AluOpType.add
MULT = mybir.AluOpType.mult
MAX = mybir.AluOpType.max
COPY = mybir.ActivationFunctionType.Copy
RELU = mybir.ActivationFunctionType.Relu

P = 128
STEP = 256
STEPS = N // STEP
UNIT = 2 * H
SLOTS = 6
WARM_UPS = 6
SHARE = 96
FLAT_FROM = 4
BY_TILE = 13


def tile_tideresidualencodertemporaldecoder_t_kernel(
    tc, x_bytes, x_scale, fut, w1, w2, wsk, vp, wres, out
):
    nc = tc.nc
    with ExitStack() as ctx:
        keep = ctx.enter_context(tc.tile_pool(name="keep", bufs=1))
        work = ctx.enter_context(tc.tile_pool(name="work", bufs=2))
        psum = ctx.enter_context(tc.psum_pool(name="psum", bufs=1))
        ctx.enter_context(tc.manual_schedule())

        x_view = x_bytes.rearrange("(g p s i) k -> p g s (i k)", p=P, s=4, i=2)
        fut_view = fut.rearrange("(g p s i) q j -> p g s i (q j)", p=P, s=4, i=2)
        out_view = out.rearrange("(g p s i) j -> p g s i j", p=P, s=4, i=2)
        halves = [slice(0, 512), slice(512, 1024)]
        both, tile0, tile1 = slice(0, 2), slice(0, 1), slice(1, 2)

        x_in, fut_in, raw, woven, wq, ws = ({} for i in range(6))
        xc, xg, xq, xs, hg, hq, hs, xt, hb, rb, res, part, banks = ({} for i in range(13))

        def load_x(first, count):
            t = keep.tile([P, count, 2 * L], U8, name=f"xbytes{first}", align_bytes=64)
            nc.sync.dma_start(out=t[:], in_=x_view[:, first // 4, first % 4 : first % 4 + count, :])
            for j in range(count):
                x_in[first + j] = t[:, j, :].bitcast(FP8)

        def load_fut(s):
            fut_in[s] = work.tile([P, 2, PH], BF16, name="fut_in", bufs=4)
            nc.sync.dma_start(out=fut_in[s][:], in_=fut_view[:, s // 4, s % 4, :, :])

        def load_w(name, w, cols):
            t = keep.tile([P, 4, cols.stop - cols.start], BF16, name=name + "_raw")
            nc.sync.dma_start(out=t[:], in_=w.rearrange("(p j) c -> p j c", j=4)[:, :, cols])
            raw[name] = t[:]

        ring = [keep.tile([P, 8 * STEP], BF16, name=f"ring{r}", align_bytes=64) for r in range(2)]
        zring = keep.tile([P, (SLOTS * 4 + 3) * UNIT], F32, name="zring")

        def base(s):
            return (SLOTS - 1 - s % SLOTS) * 4 * UNIT

        def slot(s):
            order = "p (i q j) -> p q i j" if s == BY_TILE else "p (q i j) -> p q i j"
            return zring[:, base(s) : base(s) + 4 * UNIT].rearrange(order, q=P_DEC, i=2)

        def plane(s, p, rows=both):
            return slot(s)[:, p, rows, :]

        def pair(s, b, rows=both):
            return slot(s)[:, 2 * b : 2 * b + 2, rows, :]

        def cast(s):
            xc[s] = work.tile([P, 2 * L], BF16, name="xc", bufs=5)
            nc.scalar.copy(out=xc[s][:], in_=x_in[s])

        def transposes(s, tag="xt", bufs=1):
            xt[s] = psum.tile([P, 512], F32, name="xt", tag=tag, bufs=bufs)
            words = xc[s][:].bitcast(F32)
            for u in range(2):
                for i in range(2):
                    second = slice(256 * i + u, 256 * (i + 1), 2)
                    run = slice(256 * u + P * i, 256 * u + P * i + P)
                    nc.tensor.transpose(xt[s][:, second if s < FLAT_FROM else run], words[:, second], ident[:])

        def product(s, dest):
            xg[s] = dest
            order = "q (n u e) -> q n u e" if s < FLAT_FROM else "q (u n e) -> q n u e"
            nc.vector.tensor_tensor(
                out=dest.rearrange("q (n u e) -> q n u e", u=2, e=2),
                in0=xt[s][:].bitcast(BF16).rearrange(order, u=2, e=2),
                in1=scale_col[:].rearrange("q (o u e) -> q o u e", o=1, u=2).to_broadcast([P, STEP, 2, 2]),
                op=MULT,
            )

        def quantize(name, source, bufs):
            width = source.shape[1] // 4
            codes = work.tile([P, width], U32, name=name + "_q", bufs=bufs, align_bytes=64)
            scales = work.tile([P, width], U8, name=name + "_s", bufs=bufs, align_bytes=64)
            nc.vector.quantize_mx(out=codes[:].bitcast(FP8X4), scales=scales[:], in_=source)
            return codes, scales

        def quantize_w(name):
            wq[name], ws[name] = quantize(name, woven[name], 1)

        def quantize_acts(source, *what):
            codes, scales = quantize(f"acts{len(what)}", source, {1: 8, 2: 6}[len(what)])
            for n, (kind, s) in enumerate(what):
                cols = slice(n * STEP, (n + 1) * STEP)
                if kind == "x":
                    xq[s], xs[s] = codes[:, cols], scales[:, cols]
                else:
                    hq[s], hs[s] = codes[:, cols], scales[:, cols]

        def hidden(s, tag="hb", bufs=2):
            for i in range(2):
                hb[s, i] = psum.tile([P, 512], F32, name="hb", tag=tag, bufs=bufs)
                cols = slice(i * P, i * P + P)
                for t in range(4):
                    chans = slice(t * P, t * P + P)
                    nc.tensor.matmul_mx(
                        out=hb[s, i][:, chans],
                        lhsT=wq["w1"][:, chans].bitcast(FP8X4), lhsT_scale=ws["w1"][:, chans],
                        rhs=xq[s][:, cols].bitcast(FP8X4), rhs_scale=xs[s][:, cols],
                        start=True, stop=True,
                    )

        def relu_h(s, dest, tiles=(0, 1)):
            hg[s] = dest
            for i in tiles:
                nc.scalar.activation(
                    out=dest[:, 512 * i : 512 * i + 512].rearrange("m (n t) -> m n t", t=4),
                    in_=hb[s, i][:].rearrange("m (t n) -> m n t", t=4),
                    func=RELU,
                )

        def main_pass(s, i, b, kind, opens, tag="rb", bufs=4):
            cols = slice(i * P, i * P + P)
            if opens:
                rb[s, i, b] = psum.tile([P, 512], F32, name="rb", tag=tag, bufs=bufs)
            codes, scales, name = (xq[s], xs[s], f"wsk{b}") if kind == "x" else (hq[s], hs[s], f"w2{b}")
            nc.tensor.matmul_mx(
                out=rb[s, i, b][:],
                lhsT=codes[:, cols].bitcast(FP8X4), lhsT_scale=scales[:, cols],
                rhs=wq[name][:].bitcast(FP8X4), rhs_scale=ws[name][:],
                start=opens, stop=not opens,
            )

        def main(s, i, b, tag="rb", bufs=4):
            main_pass(s, i, b, "x", True, tag, bufs)
            main_pass(s, i, b, "h", False)

        def skip(s, tag="res", bufs=1):
            res[s] = psum.tile([P, 512], F32, name="res", tag=tag, bufs=bufs)
            for i in range(2):
                cols = slice(i * P, i * P + P)
                nc.tensor.matmul_mx(
                    out=res[s][:, H * i : H * i + H],
                    lhsT=xq[s][:, cols].bitcast(FP8X4), lhsT_scale=xs[s][:, cols],
                    rhs=wq["wres"][:].bitcast(FP8X4), rhs_scale=ws["wres"][:],
                    start=True, stop=True,
                )

        def add_fut(s, i, b):
            nc.vector.tensor_tensor(
                out=pair(s, b)[:, :, i, :],
                in0=rb[s, i, b][:].rearrange("p (q j) -> p q j", q=2),
                in1=fut_in[s][:, i, halves[b]].rearrange("p (q j) -> p q j", q=2),
                op=ADD,
            )

        def relu_pair(s, b, rows=both):
            nc.scalar.activation(out=pair(s, b, rows), in_=pair(s, b, rows), func=RELU)

        def relu_plane(s, p, rows=both):
            nc.scalar.activation(out=plane(s, p, rows), in_=plane(s, p, rows), func=RELU)

        def scale_plane(s, p, rows=both):
            nc.scalar.activation(out=plane(s, p, rows), in_=plane(s, p, rows), func=COPY, scale=vp_f[:, p : p + 1])

        def relu_scale(s, p, rows=both):
            nc.vector.tensor_scalar(
                out=plane(s, p, rows), in0=plane(s, p, rows), scalar1=0.0, scalar2=vp_f[:, p : p + 1], op0=MAX, op1=MULT
            )

        def relu_share(s):
            at = base(s) + 2 * UNIT
            run = zring[:, at : at + UNIT + SHARE]
            nc.scalar.activation(out=run, in_=run, func=RELU)

        def scale_share(s):
            at = base(s) + 3 * UNIT
            run = zring[:, at : at + SHARE]
            nc.scalar.activation(out=run, in_=run, func=COPY, scale=vp_f[:, 3:4])

        def relu_scale_rest(s):
            at = base(s) + 3 * UNIT
            run = zring[:, at + SHARE : at + UNIT]
            nc.vector.tensor_scalar(out=run, in0=run, scalar1=0.0, scalar2=vp_f[:, 3:4], op0=MAX, op1=MULT)

        def weigh_skip(s, p=1, rows=both):
            nc.vector.scalar_tensor_tensor(
                out=plane(s, p, rows), in0=plane(s, p, rows), scalar=vp_f[:, p : p + 1],
                in1=res[s][:].rearrange("p (i j) -> p i j", i=2)[:, rows, :], op0=MULT, op1=ADD,
            )

        def weigh(s, p, rows, into):
            nc.vector.scalar_tensor_tensor(
                out=plane(s, into, rows), in0=plane(s, p, rows), scalar=vp_f[:, p : p + 1],
                in1=plane(s, into, rows), op0=MULT, op1=ADD,
            )

        def sums_at(s):
            return base(s + 1) + 4 * UNIT

        def sums(s, first, count, rows=both):
            at = base(s)
            pairs = zring[:, at + 2 * first * UNIT : at + 2 * (first + count) * UNIT].rearrange("p (c o i j) -> p c o i j", o=2, i=2, j=H)
            dest = zring[:, sums_at(s) + first * UNIT : sums_at(s) + (first + count) * UNIT].rearrange("p (c i j) -> p c i j", i=2, j=H)
            nc.gpsimd.tensor_tensor(out=dest[:, :, rows, :], in0=pairs[:, :, 0, rows, :], in1=pairs[:, :, 1, rows, :], op=ADD)

        def add_on_gpsimd(dest, first, second):
            nc.gpsimd.tensor_tensor(out=dest, in0=first, in1=second, op=ADD)

        def add_on_vector(dest, first, second):
            nc.vector.tensor_tensor(out=dest, in0=first, in1=second, op=ADD)

        def weigh_on_tensor(s, i, planes, opens, closes, tag="hb", bufs=2):
            if opens:
                part[s, i] = psum.tile([P, H], F32, name="part", tag=tag, bufs=bufs)
            for p in planes:
                nc.tensor.matmul(
                    out=part[s, i][:], lhsT=vp_diag[:, p, :], rhs=plane(s, p)[:, i, :],
                    start=(opens and p == planes[0]), stop=(closes and p == planes[-1]),
                )

        def store(s, source, rows=both):
            nc.sync.dma_start(out=out_view[:, s // 4, s % 4, rows, :], in_=source)

        def woven_tile(name, width=512):
            woven[name] = keep.tile([P, 4 * width], BF16, name=name + "_g", align_bytes=64)[:]
            return woven[name]

        def fill_w(name, half, tag="rb", bufs=4):
            views = raw[name].rearrange("p j (t m) -> p t m j", m=P)
            banks[name, half] = psum.tile([P, 2, 512], BF16, name="wbank", tag=tag, bufs=bufs)
            for n in range(2):
                nc.tensor.matmul(out=banks[name, half][:, n, :], lhsT=ident_bf[:], rhs=views[:, 2 * half + n], start=True, stop=True)

        def empty_w(name, half):
            dst = woven[name][:, 1024 * half : 1024 * half + 1024]
            nc.scalar.copy(out=dst, in_=banks[name, half][:].rearrange("p n c -> p (n c)"))

        def fill_quarter(name, quarter):
            view = raw[name].rearrange("p j (t m) -> p t m j", m=P)[:, quarter]
            banks[name, "q"] = psum.tile([P, 512], BF16, name="wbank", tag="res", bufs=1)
            nc.tensor.matmul(out=banks[name, "q"][:], lhsT=ident_bf[:], rhs=view, start=True, stop=True)

        def empty_quarter(name, quarter):
            nc.scalar.copy(out=woven[name][:, 512 * quarter : 512 * quarter + 512], in_=banks[name, "q"][:])

        def weave_on_gpsimd(name):
            nc.gpsimd.tensor_scalar(
                out=woven[name].rearrange("p (c j) -> p c j", j=4), in0=raw[name].rearrange("p j c -> p c j"),
                scalar1=1.0, scalar2=0.0, op0=MULT, op1=ADD,
            )

        def weave_views(name, cols):
            dst = woven[name][:, 4 * cols.start : 4 * cols.stop].rearrange("p (c i j) -> p c j i", i=4, j=4)
            return dst, raw[name][:, :, cols].rearrange("p j (c i) -> p c j i", i=4)

        def weave_on_vector(name, cols):
            dst, src = weave_views(name, cols)
            nc.vector.tensor_copy(out=dst, in_=src)

        def weave_on_scalar(name, cols):
            dst, src = weave_views(name, cols)
            nc.scalar.copy(out=dst, in_=src)

        def own_tile(name, bufs):
            return work.tile([P, 4 * STEP], BF16, name=name, bufs=bufs, align_bytes=64)[:]

        def adds(s, b):
            for i in range(2):
                add_fut(s, i, b)

        def mains(s, b, tag="rb", bufs=4):
            for i in range(2):
                main(s, i, b, tag, bufs)

        def sums_and_store(s):
            sums(s, 0, 3 if s else 2)
            if s:
                store(s - 1, zring[:, sums_at(s) + 2 * UNIT : sums_at(s) + 3 * UNIT].rearrange("p (i j) -> p i j", i=2))


        vp_bf = keep.tile([P, P_DEC], BF16, name="vp_bf")
        nc.vector.memset(vp_bf[:], 0.0)
        ones_bf = keep.tile([P, P], BF16, name="ones_bf")
        nc.vector.memset(ones_bf[:], 1.0)
        scale_col = keep.tile([P, 4], F32, name="scale_col")
        nc.scalar.dma_start(out=scale_col[:], in_=x_scale.rearrange("o (n c) -> (o n) c", c=4))
        nc.scalar.dma_start(out=vp_bf[0:1, :], in_=vp.rearrange("(o q) -> o q", o=1))
        load_x(0, 1)
        load_w("w1", w1, slice(0, F))
        load_x(1, 3)
        load_w("wsk", wsk, slice(0, PH))
        raw["wsk0"], raw["wsk1"] = raw["wsk"][:, :, halves[0]], raw["wsk"][:, :, halves[1]]
        load_w("w20", w2, halves[0])
        load_w("w21", w2, halves[1])
        load_fut(0)
        load_x(4, 4)
        load_w("wres", wres, slice(0, H))
        load_fut(1)
        load_fut(2)
        load_x(8, 4)
        load_x(12, 4)
        ident = keep.tile([P, P], F32, name="ident")
        make_identity(nc, ident[:])
        ident_bf = keep.tile([P, P], BF16, name="ident_bf")
        nc.scalar.activation(out=ident_bf[:], in_=ident[:], func=RELU)
        vp_f = keep.tile([P, P_DEC], F32, name="vp_f")
        vp_diag = keep.tile([P, P_DEC, P], F32, name="vp_diag")
        warm_out = psum.tile([P, 4, P], F32, name="warm_out", tag="rb", bufs=4)
        for w in range(WARM_UPS):
            nc.tensor.matmul(
                out=warm_out[:], lhsT=ones_bf[:],
                rhs=ones_bf[:].rearrange("p (o c) -> p o c", o=1).to_broadcast([P, 4, P]), start=True, stop=True,
            )

        vbank = psum.tile([P, P_DEC], F32, name="vbank", tag="hb", bufs=2)
        cast(0)
        transposes(0)
        nc.tensor.matmul(out=vbank[:], lhsT=ones_bf[:], rhs=vp_bf[:], start=True, stop=True)
        w1_to = woven_tile("w1").rearrange("p (t m j) -> p m j t", t=4, j=4)
        w1_from = raw["w1"].rearrange("p j (m t) -> p m j t", t=4)
        nc.vector.tensor_copy(out=w1_to[:, 0:80], in_=w1_from[:, 0:80])
        nc.scalar.copy(out=w1_to[:, 80:P], in_=w1_from[:, 80:P])
        cast(1)
        transposes(1, "rb", 4)
        cast(2)
        transposes(2, "res")
        cast(3)
        product(0, own_tile("xg", 4))
        nc.vector.tensor_copy(out=vp_f[:], in_=vbank[:])
        transposes(3)
        quantize_w("w1")
        quantize_acts(xg[0], ("x", 0))
        hidden(0)
        woven["wsk0"] = woven["w1"]
        weave_on_gpsimd("wsk0")
        woven_tile("wsk1")
        weave_on_scalar("wsk1", slice(0, 512))
        for s in (1, 2, 3):
            product(s, own_tile("xg", 4))
        relu_h(0, own_tile("hg", 2))
        woven_tile("w20")
        woven_tile("w21")
        fill_w("w20", 0)
        fill_w("w20", 1)
        for s in (1, 2, 3):
            quantize_acts(xg[s], ("x", s))
        hidden(1)
        fill_w("w21", 0)
        empty_w("w20", 0)
        empty_w("w20", 1)
        quantize_w("wsk0")
        quantize_w("wsk1")
        quantize_acts(hg[0], ("h", 0))
        quantize_w("w20")
        weave_on_vector("w21", slice(256, 512))
        mains(0, 0)
        relu_h(1, own_tile("hg", 2))
        empty_w("w21", 0)
        cast(4)
        quantize_acts(hg[1], ("h", 1))
        quantize_w("w21")
        woven["wres"] = woven["w21"][:, 0 : 4 * H]
        weave_on_gpsimd("wres")
        hidden(2)
        mains(0, 1)
        relu_h(2, ring[0][:, 0:1024])
        transposes(4)
        load_fut(3)
        cast(5)
        add_fut(0, 0, 0)
        main(1, 0, 0)
        add_fut(0, 1, 0)
        relu_pair(0, 0)
        adds(0, 1)
        quantize_w("wres")
        skip(0)
        main(1, 1, 0)
        hidden(3)
        mains(1, 1)
        product(4, ring[0][:, 1024:2048])
        transposes(5)
        relu_plane(0, 2)
        scale_plane(0, 0)
        scale_plane(0, 2)
        weigh_skip(0)
        relu_scale(0, 3)
        relu_h(3, ring[1][:, 0:1024])
        quantize_acts(ring[0][:], ("h", 2), ("x", 4))
        sums_and_store(0)

        for s in range(1, STEPS - 5):
            load_fut(s + 3)
            cast(s + 5)
            skip(s)
            hidden(s + 3)
            for b in range(2):
                for i in range(2):
                    add_fut(s, i, b)
                    main(s + 1, i, b)
                if b == 0:
                    relu_pair(s, 0)
            product(s + 4, ring[s % 2][:, 1024:2048])
            transposes(s + 5)
            relu_share(s)
            scale_plane(s, 0)
            scale_plane(s, 2)
            scale_share(s)
            weigh_skip(s)
            relu_scale_rest(s)
            relu_h(s + 3, ring[(s + 1) % 2][:, 0:1024])
            quantize_acts(ring[s % 2][:], ("h", s + 2), ("x", s + 4))
            sums_and_store(s)

        def add_part(s, i):
            add_on_vector(plane(s, 1)[:, i, :], part[s, i][:], plane(s, 1)[:, i, :])

        load_fut(14)
        skip(11)
        hidden(14)
        relu_h(14, ring[0][:, 0:1024], (0,))
        for b in range(2):
            for i in range(2):
                add_fut(11, i, b)
                main(12, i, b)
            if b == 0:
                relu_pair(11, 0)
        relu_h(14, ring[0][:, 0:1024], (1,))
        product(15, ring[1][:, 1024:2048])
        relu_plane(11, 2)
        scale_plane(11, 0)
        scale_plane(11, 2)
        weigh_skip(11)
        relu_scale(11, 3)
        quantize_acts(ring[1][:], ("h", 13), ("x", 15))
        quantize_acts(hg[14], ("h", 14))
        sums_and_store(11)
        for p in (0, 2, 3):
            nc.scalar.activation(out=vp_diag[:, p, :], in_=ident[:], func=COPY, scale=vp_f[:, p : p + 1])
        load_fut(15)
        skip(12)
        skip(13, "xt")
        hidden(15)
        relu_h(15, ring[0][:, 1024:2048])
        for b in range(2):
            for i in range(2):
                add_fut(12, i, b)
                main(13, i, b)
            if b == 0:
                relu_pair(12, 0)
        relu_plane(12, 2)
        scale_plane(12, 0)
        scale_plane(12, 2)
        adds(13, 0)
        mains(14, 0)
        weigh_skip(12)
        relu_scale(12, 3)
        quantize_acts(hg[15], ("h", 15))
        sums_and_store(12)
        add_on_gpsimd(plane(12, 0), plane(12, 0), plane(12, 1))
        store(12, plane(12, 0))
        mains(14, 1, "hb", 2)
        skip(14)
        relu_pair(13, 0)
        adds(13, 1)
        mains(15, 0)
        relu_pair(13, 1)
        for p in (0, 2, 3):
            scale_plane(13, p, tile0)
        adds(14, 0)
        mains(15, 1)
        relu_pair(14, 0)
        weigh_skip(13)
        skip(15, "xt")
        adds(14, 1)
        weigh_on_tensor(13, 1, [0, 2, 3], True, True)
        relu_pair(14, 1)
        add_on_gpsimd(pair(13, 0, tile0), pair(13, 0, tile0), pair(13, 1, tile0))
        add_on_gpsimd(plane(13, 0, tile0), plane(13, 0, tile0), plane(13, 1, tile0))
        weigh_on_tensor(14, 0, [0, 2, 3], True, True)
        adds(15, 0)
        weigh_skip(14)
        weigh_on_tensor(14, 1, [0, 2, 3], True, True, "rb", 4)
        relu_pair(15, 0)
        add_fut(15, 0, 1)
        add_part(13, 1)
        store(13, plane(13, 1, tile1), tile1)
        store(13, plane(13, 0, tile0), tile0)
        add_fut(15, 1, 1)
        relu_pair(15, 1, tile0)
        relu_pair(15, 1, tile1)
        for rows in (tile0, tile1):
            weigh_skip(15, 1, rows)
        for rows in (tile0, tile1):
            weigh(15, 0, rows, 1)
        add_part(14, 0)
        store(14, plane(14, 1, tile0), tile0)
        for rows in (tile0, tile1):
            weigh(15, 2, rows, 1)
        weigh(15, 3, tile0, 1)
        store(15, plane(15, 1, tile0), tile0)
        add_part(14, 1)
        store(14, plane(14, 1, tile1), tile1)
        weigh(15, 3, tile1, 1)
        store(15, plane(15, 1, tile1), tile1)
